import numpy as np
import ml_dtypes


def mxq(x, axis, fmt="e4m3"):
    dtype, down = {"e4m3": (ml_dtypes.float8_e4m3fn, 7), "e5m2": (ml_dtypes.float8_e5m2, 14)}[fmt]
    v = np.moveaxis(np.asarray(x, np.float32).astype(ml_dtypes.bfloat16).astype(np.float64), axis, -1)
    blocks = v.reshape(v.shape[:-1] + (-1, 32))
    amax = np.abs(blocks).max(-1, keepdims=True)
    byte = np.maximum(np.where(amax > 0, np.frexp(amax)[1] - 1 + 127, 0) - down, 1)
    scale = np.exp2(byte - 127.0)
    codes = (blocks / scale).astype(np.float32).astype(dtype).astype(np.float64)
    return np.moveaxis((codes * scale).reshape(v.shape), -1, axis)


WIDE = False


def mx_kscale(k):
    if not WIDE:
        return np.ones(k)
    levels = np.array([10, -10, 5, -5, 0])
    if k % 512:
        return np.exp2(np.random.permutation(np.resize(levels, k // 32))).repeat(32)
    a = np.empty((k // 512, 16))
    for p in range(k // 512):
        a[p, :8] = np.random.permutation(np.resize(levels, 8))
        for g in range(8):
            far = levels[np.abs(levels - a[p, g]) >= 10]
            a[p, g + 8] = far[np.random.randint(len(far))]
    return np.exp2(a.ravel()).repeat(32)


def f64(x):
    return np.asarray(x).astype(np.float64)


def striped(idx):
    return np.tile(idx.reshape(-1, 16).T, (8, 1)).astype(np.uint16)


def unstriped(offs):
    return offs[:16].T.reshape(-1).astype(np.int64)


E2M1 = np.array([0.0, 0.5, 1.0, 1.5, 2.0, 3.0, 4.0, 6.0, -0.0, -0.5, -1.0, -1.5, -2.0, -3.0, -4.0, -6.0])


def pack_weight(w, fmt):
    k, n = w.shape
    w = f64(np.asarray(w, np.float32).astype(ml_dtypes.bfloat16)).reshape(k // 32, 32, n)
    amax = np.abs(w).max(1)
    if fmt == "e4m3":
        byte = np.frexp(amax)[1] - 1 + 127 - 7
    else:
        mant, ex = np.frexp(amax / 6.0)
        byte = np.where(mant > 0.5, ex, ex - 1) + 127
    byte = np.clip(np.where(amax > 0, byte, 1), 1, 254)
    scaled = (w * np.exp2(127.0 - byte)[:, None, :]).reshape(k, n).astype(np.float32)
    by_word = np.ascontiguousarray(scaled.reshape(k // 512, 128, 4, n).transpose(0, 1, 3, 2))
    if fmt == "e4m3":
        words = by_word.astype(ml_dtypes.float8_e4m3fn).view(np.uint8)
    else:
        c = by_word.astype(ml_dtypes.float4_e2m1fn).view(np.uint8) & 0xF
        words = (c[..., 0::2] | (c[..., 1::2] << 4)).reshape(k // 512, 128, 2 * n)
    return np.ascontiguousarray(words), np.ascontiguousarray(byte.astype(np.uint8).reshape(k // 512, 16, n))


def unpack_weight(words, scales, fmt):
    g, _, n = scales.shape
    words = np.ascontiguousarray(words).reshape(g, 128, n, -1)
    if fmt == "e4m3":
        vals = words.view(ml_dtypes.float8_e4m3fn).astype(np.float64)
    else:
        nib = np.empty((g, 128, n, 4), np.uint8)
        nib[..., 0::2] = words & 0xF
        nib[..., 1::2] = words >> 4
        vals = E2M1[nib]
    vals = vals * np.repeat(np.exp2(scales.astype(np.float64) - 127.0), 8, axis=1)[..., None]
    return vals.transpose(0, 1, 3, 2).reshape(g * 512, n)


def gelu(v):
    return 0.5 * v * (1.0 + np.tanh(np.sqrt(2.0 / np.pi) * (v + 0.044715 * v**3)))


K, H, T, S, T2, T3, S2, P = 1536, 512, 2048, 1024, 2048, 2048, 1024, 1024

def setup_inputs():
    n = np.random.standard_normal
    s = mx_kscale(K)[:, None]
    u = mx_kscale(H)[:, None]
    tab_words, tab_scales = pack_weight(n((K, T)) * s, "e4m3")
    tab2_words, tab2_scales = pack_weight(n((H, T3)) / np.sqrt(H) / u, "e4m3")
    w4_words, w4_scales = pack_weight(0.7 * n((K, H)) / np.sqrt(K) / s * u.T, "e2m1")
    return {
        "tab_words": tab_words, "tab_scales": tab_scales,
        "offs": striped(np.random.permutation(T)[:S]),
        "tab2_words": tab2_words, "tab2_scales": tab2_scales,
        "offs2": striped(np.random.permutation(T3)[:S2]),
        "w1": (0.7 * n((K, H)) / np.sqrt(K) / s * u.T).astype(np.float32),
        "w4_words": w4_words, "w4_scales": w4_scales,
        "page0": (n((H, T2)) * u).astype(np.float32),
        "wgs": np.exp(0.3 * n((128, S))).astype(np.float32),
        "offs3": striped(np.random.permutation(T2)[:S]),
        "offs4": striped(np.random.permutation(T2)[:P]),
        "gate": (0.8 * n((S2, P))).astype(np.float32),
    }

def reference(tab_words, tab_scales, offs, tab2_words, tab2_scales, offs2, w1, w4_words, w4_scales, page0, wgs, offs3, offs4, gate):
    v = unpack_weight(tab_words, tab_scales, "e4m3")[:, unstriped(offs)]
    v2 = unpack_weight(tab2_words, tab2_scales, "e4m3")[:, unstriped(offs2)]
    w4 = unpack_weight(w4_words, w4_scales, "e2m1")
    a = mxq(f64(w1), 0, "e4m3").T @ v
    b = w4.T @ v
    h = np.abs(a - b)
    page = f64(page0).copy()
    page[:, unstriped(offs3)] = np.tile(f64(wgs), (H // 128, 1)) * h
    e = v2.T @ mxq(page, 0, "e4m3")
    d = e[:, unstriped(offs4)] - f64(gate)
    return np.exp(-0.25 * np.square(d))

@@ -1,0 +1,211 @@
+from contextlib import ExitStack
+
+import concourse.mybir as mybir
+
+K, H, T, S = 1536, 512, 2048, 1024
+FLOPS = 2 * 2 * K * H * S + 2 * H * S * T
+
+F32 = mybir.dt.float32
+BF16 = mybir.dt.bfloat16
+I32 = mybir.dt.int32
+U32 = mybir.dt.uint32
+U16 = mybir.dt.uint16
+U8 = mybir.dt.uint8
+FP8X4 = mybir.dt.float8_e4m3fn_x4
+FP4X4 = mybir.dt.float4_e2m1fn_x4
+ACT = mybir.ActivationFunctionType
+ALU = mybir.AluOpType
+
+P = 128
+PACK = 4
+PASSES = K // (P * PACK)
+BANK = 512
+QUADS = (0, 2, 1, 3)
+
+
+def tile_list_plot_track_scores_kernel(
+    tc, tab_words, tab_scales, offs, tab2_words, tab2_scales, offs2, w1, w4_words, w4_scales,
+    page0, wgs, offs3, offs4, gate, out,
+):
+    nc = tc.nc
+    with ExitStack() as ctx:
+        lists = ctx.enter_context(tc.tile_pool(name="lists", bufs=1))
+        sb = ctx.enter_context(tc.tile_pool(name="sb", bufs=1))
+        psum = ctx.enter_context(tc.psum_pool(name="psum", bufs=1))
+
+        def load_list(src, name):
+            t = lists.tile([P, S // 16], U16, name=name)
+            nc.sync.dma_start(t[:], src)
+            return t
+
+        def load_scales(plane, src):
+            passes = src.shape[0]
+            rows = plane[:].bitcast(I32).rearrange("p (a c) -> p a c", a=passes)
+            for q in QUADS:
+                nc.sync.dma_start(
+                    rows[32 * q : 32 * q + 4, :, :],
+                    src.bitcast(I32)[:, 4 * q : 4 * q + 4, :].rearrange("a r c -> r a c"),
+                )
+
+        def half(lst, c):
+            return lst[:, c * 32 : (c + 1) * 32]
+
+        tab_sc = sb.tile([P, PASSES * T], U8, name="tab_sc", align_bytes=64)
+        w4_sc_raw = sb.tile([P, PASSES * H], U8, name="w4_sc_raw", align_bytes=64)
+        tab2_sc = sb.tile([P, T], U8, name="tab2_sc", align_bytes=64)
+        nc.vector.memset(tab_sc[:].bitcast(I32), 0)
+        nc.gpsimd.memset(w4_sc_raw[:].bitcast(I32), 0)
+        nc.gpsimd.memset(tab2_sc[:].bitcast(I32), 0)
+
+        def load_words(a):
+            win = sb.tile([P, T], I32, name=f"tab_win{a}", tag=f"win{a}", align_bytes=64)
+            nc.sync.dma_start(win[:], tab_words[a].rearrange("p t i -> p (t i)").bitcast(I32))
+            return win
+
+        def load_w1(a):
+            raw = sb.tile([P, PACK, H], F32, name=f"w1_raw{a}", tag=f"raw{a}", align_bytes=64)
+            nc.sync.dma_start(raw[:], w1[512 * a : 512 * (a + 1), :].rearrange("(p j) c -> p j c", j=PACK))
+            return raw
+
+        idx = load_list(offs, "idx")
+        tab_win = [load_words(0)]
+        load_scales(tab_sc, tab_scales)
+        load_scales(w4_sc_raw, w4_scales)
+        w4_raw = sb.tile([P, PASSES, 2 * H], U8, name="w4_raw", align_bytes=64)
+        nc.sync.dma_start(w4_raw[:].bitcast(I32), w4_words.bitcast(I32).rearrange("a p c -> p a c"))
+        w1_raw = [load_w1(0)]
+        tab_win.append(load_words(1))
+        w1_raw.append(load_w1(1))
+        w1_raw.append(load_w1(2))
+        tab_win.append(load_words(2))
+
+        idx3 = load_list(offs3, "idx3")
+        wgs_rows = wgs.rearrange("(q i) j -> q i j", i=PACK)
+        wgs_first = sb.tile([P, S], F32, name="wgs_first", align_bytes=64)
+        wgs_rest = sb.tile([P, PACK - 1, S], F32, name="wgs_rest", tag="wgs_rest", align_bytes=64)
+        page_rows = page0.rearrange("(p i) t -> p i t", i=PACK)
+        page = [sb.tile([P, T], F32, name=f"page{i}", align_bytes=64) for i in range(PACK)]
+        for q in QUADS:
+            nc.sync.dma_start(wgs_first[32 * q : 32 * q + 32, :], wgs_rows[:, 0, :])
+        nc.sync.dma_start(page[0][:], page_rows[:, 0, :])
+        for q in QUADS:
+            nc.sync.dma_start(wgs_rest[32 * q : 32 * q + 32, :, :], wgs_rows[:, 1:PACK, :])
+        nc.sync.dma_start(page[1][:], page_rows[:, 1, :])
+        idx2 = load_list(offs2, "idx2")
+        idx4 = load_list(offs4, "idx4")
+        load_scales(tab2_sc, tab2_scales)
+        tab2_win = sb.tile([P, T], I32, name="tab2_win", align_bytes=64)
+        nc.sync.dma_start(tab2_win[:], tab2_words[0].rearrange("p t i -> p (t i)").bitcast(I32))
+        for i in range(2, PACK):
+            nc.sync.dma_start(page[i][:], page_rows[:, i, :])
+
+        w4_codes = sb.tile([P, PASSES, 2 * H], U8, name="w4_codes", tag="woven", align_bytes=64)
+        w4_sc = sb.tile([P, PASSES, H], U8, name="w4_sc", align_bytes=64)
+        v_words, v_sc, w1_codes, w1_sc = [], [], [], []
+        for a in range(PASSES):
+            sc = sb.tile([P, S], U8, name=f"v_sc{a}", tag="v_sc0" if a == 0 else f"w1_bf{a - 1}", align_bytes=64)
+            words = [sb.tile([P, BANK], U32, name=f"v_words{a}{c}", align_bytes=64) for c in range(2)]
+            grouped = sb.tile([P, H * PACK], BF16, name=f"w1_bf{a}", tag=f"w1_bf{a}", align_bytes=64)
+            codes = sb.tile([P, H], U32, name=f"w1_codes{a}", align_bytes=64)
+            wsc = sb.tile([P, H], U8, name=f"w1_sc{a}", align_bytes=64)
+            nc.scalar.activation(
+                grouped[:].rearrange("p (i m j) -> p m j i", i=PACK, j=PACK),
+                w1_raw[a][:].rearrange("p j (m i) -> p m j i", i=PACK),
+                ACT.Copy, scale=-1.0,
+            )
+            nc.vector.tensor_copy(sc[:], tab_sc[:, a * T : (a + 1) * T].indirect(idx[:]))
+            if a == 0:
+                nc.vector.tensor_copy(
+                    w4_codes[:].bitcast(U16).rearrange("p a (i m) -> p a i m", i=PACK),
+                    w4_raw[:].bitcast(U16).rearrange("p a (m i) -> p a i m", i=PACK),
+                )
+                nc.vector.tensor_copy(
+                    w4_sc[:].rearrange("p a (i m) -> p a i m", i=PACK),
+                    w4_sc_raw[:].rearrange("p (a m i) -> p a i m", a=PASSES, i=PACK),
+                )
+            nc.vector.quantize_mx(out=codes[:].bitcast(FP8X4), scales=wsc[:], in_=grouped[:])
+            for c in range(2):
+                nc.vector.tensor_copy(words[c][:], tab_win[a][:].bitcast(U32).indirect(half(idx, c)))
+            v_words.append(words)
+            v_sc.append(sc)
+            w1_codes.append(codes)
+            w1_sc.append(wsc)
+
+        h = [sb.tile([P, S], F32, name=f"h{i}", tag=f"h{i}", align_bytes=64) for i in range(PACK)]
+        for i in range(PACK):
+            cols = slice(P * i, P * (i + 1))
+            for c in range(2):
+                acc = psum.tile([P, BANK], F32, name=f"acc{i}{c}", tag=f"bank{(2 * i + c) % 6}")
+                for a in range(PASSES):
+                    rhs = v_words[a][c][:].bitcast(FP8X4)
+                    rhs_sc = v_sc[a][:, c * BANK : (c + 1) * BANK]
+                    nc.tensor.matmul_mx(
+                        out=acc[:], lhsT=w4_codes[:, a, 2 * P * i : 2 * P * (i + 1)].bitcast(FP4X4),
+                        lhsT_scale=w4_sc[:, a, cols],
+                        rhs=rhs, rhs_scale=rhs_sc, start=(a == 0), stop=False,
+                    )
+                    nc.tensor.matmul_mx(
+                        out=acc[:], lhsT=w1_codes[a][:, cols].bitcast(FP8X4), lhsT_scale=w1_sc[a][:, cols],
+                        rhs=rhs, rhs_scale=rhs_sc, start=False, stop=(a == PASSES - 1),
+                    )
+                nc.scalar.activation(h[i][:, c * BANK : (c + 1) * BANK], acc[:], ACT.Abs)
+
+        chunks = T // BANK
+        woven = sb.tile([P, T * PACK], BF16, name="woven", tag="woven", align_bytes=64)
+        woven_cols = woven[:].rearrange("p (t i) -> p t i", i=PACK)
+        for i in range(PACK):
+            if i == 0:
+                for c in range(2):
+                    cols = slice(c * BANK, (c + 1) * BANK)
+                    nc.vector.tensor_tensor(page[0][:].indirect(half(idx3, c)), h[0][:, cols], wgs_first[:, cols], ALU.mult)
+            else:
+                nc.vector.tensor_tensor(page[i][:].indirect(idx3[:]), h[i][:], wgs_rest[:, i - 1, :], ALU.mult)
+            if i < PACK - 1:
+                nc.scalar.copy(woven_cols[:, :, i], page[i][:])
+            else:
+                for c in range(chunks):
+                    cols = slice(c * BANK, (c + 1) * BANK)
+                    nc.scalar.copy(woven_cols[:, cols, i], page[i][:, cols])
+
+        v2_words = sb.tile([P, S], U32, name="v2_words", tag=f"h{PACK - 1}", align_bytes=64)
+        v2_sc = sb.tile([P, S], U8, name="v2_sc", tag="wgs_rest", align_bytes=64)
+        nc.vector.tensor_copy(v2_words[:], tab2_win[:].bitcast(U32).indirect(idx2[:]))
+        nc.vector.tensor_copy(v2_sc[:], tab2_sc[:].indirect(idx2[:]))
+
+        page_codes, page_sc = [], []
+        for c in range(chunks):
+            codes = sb.tile([P, BANK], U32, name=f"page_codes{c}", align_bytes=64)
+            sc = sb.tile([P, BANK], U8, name=f"page_sc{c}", align_bytes=64)
+            nc.vector.quantize_mx(out=codes[:].bitcast(FP8X4), scales=sc[:],
+                                  in_=woven[:, c * BANK * PACK : (c + 1) * BANK * PACK])
+            page_codes.append(codes)
+            page_sc.append(sc)
+
+        gates = []
+        for g in range(S // (2 * P)):
+            pair = sb.tile([P, 2, S], F32, name=f"gate{g}", tag=f"raw{g}", align_bytes=64)
+            nc.sync.dma_start(pair[:], gate[2 * P * g : 2 * P * (g + 1), :].rearrange("(u p) m -> p u m", u=2))
+            gates.append(pair)
+
+        tiles = S // P
+        for n in range(tiles):
+            rows = slice(P * n, P * (n + 1))
+            e = sb.tile([P, T], F32, name=f"e{n}", tag=f"win{n % PASSES}", align_bytes=64)
+            for c in range(chunks):
+                bank = psum.tile([P, BANK], F32, name=f"e{n}{c}", tag=f"bank{chunks * (n % 2) + c}")
+                nc.tensor.matmul_mx(
+                    out=bank[:], lhsT=v2_words[:, rows].bitcast(FP8X4), lhsT_scale=v2_sc[:, rows],
+                    rhs=page_codes[c][:].bitcast(FP8X4), rhs_scale=page_sc[c][:], start=True, stop=True,
+                )
+                nc.scalar.copy(e[:, c * BANK : (c + 1) * BANK], bank[:])
+            d = sb.tile([P, S], F32, name=f"d{n}", tag=f"w1_bf{n % PASSES}", align_bytes=64)
+            score = sb.tile([P, S], F32, name=f"score{n}", tag=f"h{n % 3}", align_bytes=64)
+            parts = 2 if n == tiles - 1 else 1
+            width = S // parts
+            for c in range(parts):
+                cols = slice(c * width, (c + 1) * width)
+                picks = idx4[:, c * width // 16 : (c + 1) * width // 16]
+                nc.vector.tensor_tensor(d[:, cols], e[:].indirect(picks), gates[n // 2][:, n % 2, cols], ALU.subtract)
+                nc.vector.tensor_tensor(d[:, cols], d[:, cols], d[:, cols], ALU.mult)
+                nc.scalar.activation(score[:, cols], d[:, cols], ACT.Exp, scale=-0.25)
+                nc.sync.dma_start(out[rows, cols], score[:, cols])

@@ -21,6 +21,7 @@ PACK = 4
 PASSES = K // (P * PACK)
 BANK = 512
 QUADS = (0, 2, 1, 3)
+ORDER = (2, 0, 1, 3)
 
 
 def tile_list_plot_track_scores_kernel(
@@ -50,12 +51,18 @@ def tile_list_plot_track_scores_kernel(
         def half(lst, c):
             return lst[:, c * 32 : (c + 1) * 32]
 
-        tab_sc = sb.tile([P, PASSES * T], U8, name="tab_sc", align_bytes=64)
+        tab_sc = sb.tile([P, T], U8, name="tab_sc", align_bytes=64)
+        v_sc = [sb.tile([P, S], U8, name=f"v_sc{a}", align_bytes=64) for a in range(PASSES)]
         w4_sc_raw = sb.tile([P, PASSES * H], U8, name="w4_sc_raw", align_bytes=64)
         tab2_sc = sb.tile([P, T], U8, name="tab2_sc", align_bytes=64)
         nc.vector.memset(tab_sc[:].bitcast(I32), 0)
-        nc.gpsimd.memset(w4_sc_raw[:].bitcast(I32), 0)
-        nc.gpsimd.memset(tab2_sc[:].bitcast(I32), 0)
+        nc.vector.memset(w4_sc_raw[:].bitcast(I32), 0)
+        nc.vector.memset(tab2_sc[:].bitcast(I32), 0)
+        for a in range(1, PASSES):
+            nc.gpsimd.memset(v_sc[a][:].bitcast(I32), 0)
+        warm = sb.tile([P, 1], F32, name="warm")
+        nc.vector.memset(warm[:], 0.0)
+        nc.scalar.activation(warm[:], warm[:], ACT.Exp)
 
         def load_words(a):
             win = sb.tile([P, T], I32, name=f"tab_win{a}", tag=f"win{a}", align_bytes=64)
@@ -69,41 +76,43 @@ def tile_list_plot_track_scores_kernel(
 
         idx = load_list(offs, "idx")
         tab_win = [load_words(0)]
-        load_scales(tab_sc, tab_scales)
-        load_scales(w4_sc_raw, w4_scales)
+        idx2 = load_list(offs2, "idx2")
+        idx3 = load_list(offs3, "idx3")
+        idx4 = load_list(offs4, "idx4")
+        for q in QUADS:
+            nc.sync.dma_start(
+                tab_sc[:].bitcast(I32)[32 * q : 32 * q + 4 * PASSES, :],
+                tab_scales.bitcast(I32)[:, 4 * q : 4 * q + 4, :],
+            )
         w4_raw = sb.tile([P, PASSES, 2 * H], U8, name="w4_raw", align_bytes=64)
         nc.sync.dma_start(w4_raw[:].bitcast(I32), w4_words.bitcast(I32).rearrange("a p c -> p a c"))
+        load_scales(w4_sc_raw, w4_scales)
         w1_raw = [load_w1(0)]
-        tab_win.append(load_words(1))
+        load_scales(tab2_sc, tab2_scales)
         w1_raw.append(load_w1(1))
+        tab_win.append(load_words(1))
         w1_raw.append(load_w1(2))
         tab_win.append(load_words(2))
 
-        idx3 = load_list(offs3, "idx3")
         wgs_rows = wgs.rearrange("(q i) j -> q i j", i=PACK)
-        wgs_first = sb.tile([P, S], F32, name="wgs_first", align_bytes=64)
-        wgs_rest = sb.tile([P, PACK - 1, S], F32, name="wgs_rest", tag="wgs_rest", align_bytes=64)
         page_rows = page0.rearrange("(p i) t -> p i t", i=PACK)
-        page = [sb.tile([P, T], F32, name=f"page{i}", align_bytes=64) for i in range(PACK)]
-        for q in QUADS:
-            nc.sync.dma_start(wgs_first[32 * q : 32 * q + 32, :], wgs_rows[:, 0, :])
-        nc.sync.dma_start(page[0][:], page_rows[:, 0, :])
-        for q in QUADS:
-            nc.sync.dma_start(wgs_rest[32 * q : 32 * q + 32, :, :], wgs_rows[:, 1:PACK, :])
-        nc.sync.dma_start(page[1][:], page_rows[:, 1, :])
-        idx2 = load_list(offs2, "idx2")
-        idx4 = load_list(offs4, "idx4")
-        load_scales(tab2_sc, tab2_scales)
+        factor = [sb.tile([P, S], F32, name=f"factor{i}", align_bytes=64) for i in range(PACK)]
+        page = [sb.tile([P, T], F32, name=f"page{i}", tag=f"page{i}", align_bytes=64) for i in range(PACK)]
         tab2_win = sb.tile([P, T], I32, name="tab2_win", align_bytes=64)
-        nc.sync.dma_start(tab2_win[:], tab2_words[0].rearrange("p t i -> p (t i)").bitcast(I32))
-        for i in range(2, PACK):
+        for i in ORDER:
+            if i == ORDER[-1]:
+                nc.sync.dma_start(tab2_win[:], tab2_words[0].rearrange("p t i -> p (t i)").bitcast(I32))
+            for q in QUADS:
+                nc.sync.dma_start(factor[i][32 * q : 32 * q + 32, :], wgs_rows[:, i, :])
             nc.sync.dma_start(page[i][:], page_rows[:, i, :])
 
         w4_codes = sb.tile([P, PASSES, 2 * H], U8, name="w4_codes", tag="woven", align_bytes=64)
         w4_sc = sb.tile([P, PASSES, H], U8, name="w4_sc", align_bytes=64)
-        v_words, v_sc, w1_codes, w1_sc = [], [], [], []
+        v_words, w1_codes, w1_sc = [], [], []
+        nc.vector.tensor_copy(v_sc[0][:], tab_sc[:].indirect(idx[:]))
+        for a in range(1, PASSES):
+            nc.gpsimd.dma_start(v_sc[a][:].bitcast(I32)[0:112, :], v_sc[0][:].bitcast(I32)[4 * a : 4 * a + 112, :])
         for a in range(PASSES):
-            sc = sb.tile([P, S], U8, name=f"v_sc{a}", tag="v_sc0" if a == 0 else f"w1_bf{a - 1}", align_bytes=64)
             words = [sb.tile([P, BANK], U32, name=f"v_words{a}{c}", align_bytes=64) for c in range(2)]
             grouped = sb.tile([P, H * PACK], BF16, name=f"w1_bf{a}", tag=f"w1_bf{a}", align_bytes=64)
             codes = sb.tile([P, H], U32, name=f"w1_codes{a}", align_bytes=64)
@@ -113,64 +122,92 @@ def tile_list_plot_track_scores_kernel(
                 w1_raw[a][:].rearrange("p j (m i) -> p m j i", i=PACK),
                 ACT.Copy, scale=-1.0,
             )
-            nc.vector.tensor_copy(sc[:], tab_sc[:, a * T : (a + 1) * T].indirect(idx[:]))
-            if a == 0:
-                nc.vector.tensor_copy(
-                    w4_codes[:].bitcast(U16).rearrange("p a (i m) -> p a i m", i=PACK),
-                    w4_raw[:].bitcast(U16).rearrange("p a (m i) -> p a i m", i=PACK),
-                )
-                nc.vector.tensor_copy(
-                    w4_sc[:].rearrange("p a (i m) -> p a i m", i=PACK),
-                    w4_sc_raw[:].rearrange("p (a m i) -> p a i m", a=PASSES, i=PACK),
-                )
+            nc.vector.tensor_copy(
+                w4_codes[:, a, :].bitcast(U16).rearrange("p (i m) -> p i m", i=PACK),
+                w4_raw[:, a, :].bitcast(U16).rearrange("p (m i) -> p i m", i=PACK),
+            )
+            nc.vector.tensor_copy(
+                w4_sc[:, a, :].rearrange("p (i m) -> p i m", i=PACK),
+                w4_sc_raw[:, a * H : (a + 1) * H].rearrange("p (m i) -> p i m", i=PACK),
+            )
             nc.vector.quantize_mx(out=codes[:].bitcast(FP8X4), scales=wsc[:], in_=grouped[:])
             for c in range(2):
                 nc.vector.tensor_copy(words[c][:], tab_win[a][:].bitcast(U32).indirect(half(idx, c)))
+            if a == 0:
+                v2_sc = sb.tile([P, S], U8, name="v2_sc", tag="w1_bf0", align_bytes=64)
+                nc.vector.tensor_copy(v2_sc[:], tab2_sc[:].indirect(idx2[:]))
             v_words.append(words)
-            v_sc.append(sc)
             w1_codes.append(codes)
             w1_sc.append(wsc)
 
-        h = [sb.tile([P, S], F32, name=f"h{i}", tag=f"h{i}", align_bytes=64) for i in range(PACK)]
-        for i in range(PACK):
+        chunks = T // BANK
+        acc, h = {}, {}
+
+        def views(pos):
+            i = ORDER[pos]
             cols = slice(P * i, P * (i + 1))
             for c in range(2):
-                acc = psum.tile([P, BANK], F32, name=f"acc{i}{c}", tag=f"bank{(2 * i + c) % 6}")
-                for a in range(PASSES):
-                    rhs = v_words[a][c][:].bitcast(FP8X4)
-                    rhs_sc = v_sc[a][:, c * BANK : (c + 1) * BANK]
+                acc[i, c] = psum.tile([P, BANK], F32, name=f"acc{i}{c}", tag=f"bank{(2 * pos + c) % 6}")
+                picked = slice(c * BANK, (c + 1) * BANK)
+                passes = [("w4", 0), ("w1", 0), ("w1", 1), ("w4", 1), ("w4", 2), ("w1", 2)]
+                for k, (which, a) in enumerate(passes):
+                    if which == "w4":
+                        lhsT = w4_codes[:, a, 2 * P * i : 2 * P * (i + 1)].bitcast(FP4X4)
+                        lhsT_sc = w4_sc[:, a, cols]
+                        rhs_sc = v_sc[a][:, picked]
+                    else:
+                        lhsT = w1_codes[a][:, cols].bitcast(FP8X4)
+                        lhsT_sc = w1_sc[a][:, cols]
+                        rhs_sc = v_sc[0][4 * a :, picked]
                     nc.tensor.matmul_mx(
-                        out=acc[:], lhsT=w4_codes[:, a, 2 * P * i : 2 * P * (i + 1)].bitcast(FP4X4),
-                        lhsT_scale=w4_sc[:, a, cols],
-                        rhs=rhs, rhs_scale=rhs_sc, start=(a == 0), stop=False,
+                        out=acc[i, c][:], lhsT=lhsT, lhsT_scale=lhsT_sc,
+                        rhs=v_words[a][c][:].bitcast(FP8X4), rhs_scale=rhs_sc,
+                        start=(k == 0), stop=(k == len(passes) - 1),
                     )
-                    nc.tensor.matmul_mx(
-                        out=acc[:], lhsT=w1_codes[a][:, cols].bitcast(FP8X4), lhsT_scale=w1_sc[a][:, cols],
-                        rhs=rhs, rhs_scale=rhs_sc, start=False, stop=(a == PASSES - 1),
-                    )
-                nc.scalar.activation(h[i][:, c * BANK : (c + 1) * BANK], acc[:], ACT.Abs)
 
-        chunks = T // BANK
-        woven = sb.tile([P, T * PACK], BF16, name="woven", tag="woven", align_bytes=64)
-        woven_cols = woven[:].rearrange("p (t i) -> p t i", i=PACK)
-        for i in range(PACK):
-            if i == 0:
+        def magnitude(pos):
+            i = ORDER[pos]
+            tag = f"page{ORDER[0]}" if pos == PACK - 1 else f"h{pos}"
+            h[i] = sb.tile([P, S], F32, name=f"h{i}", tag=tag, align_bytes=64)
+            for c in range(2):
+                nc.scalar.activation(h[i][:, c * BANK : (c + 1) * BANK], acc[i, c][:], ACT.Abs)
+
+        def replace(pos):
+            i = ORDER[pos]
+            if pos == 0:
                 for c in range(2):
                     cols = slice(c * BANK, (c + 1) * BANK)
-                    nc.vector.tensor_tensor(page[0][:].indirect(half(idx3, c)), h[0][:, cols], wgs_first[:, cols], ALU.mult)
+                    nc.vector.tensor_tensor(page[i][:].indirect(half(idx3, c)), h[i][:, cols], factor[i][:, cols], ALU.mult)
             else:
-                nc.vector.tensor_tensor(page[i][:].indirect(idx3[:]), h[i][:], wgs_rest[:, i - 1, :], ALU.mult)
-            if i < PACK - 1:
+                nc.vector.tensor_tensor(page[i][:].indirect(idx3[:]), h[i][:], factor[i][:], ALU.mult)
+
+        def weave(pos):
+            i = ORDER[pos]
+            if pos < PACK - 1:
                 nc.scalar.copy(woven_cols[:, :, i], page[i][:])
             else:
                 for c in range(chunks):
                     cols = slice(c * BANK, (c + 1) * BANK)
-                    nc.scalar.copy(woven_cols[:, cols, i], page[i][:, cols])
+                    if c < 2:
+                        nc.vector.tensor_copy(woven_cols[:, cols, i], page[i][:, cols])
+                    else:
+                        nc.scalar.copy(woven_cols[:, cols, i], page[i][:, cols])
 
-        v2_words = sb.tile([P, S], U32, name="v2_words", tag=f"h{PACK - 1}", align_bytes=64)
-        v2_sc = sb.tile([P, S], U8, name="v2_sc", tag="wgs_rest", align_bytes=64)
+        for pos in range(PACK - 1):
+            views(pos)
+            magnitude(pos)
+        views(PACK - 1)
+        woven = sb.tile([P, T * PACK], BF16, name="woven", tag="woven", align_bytes=64)
+        woven_cols = woven[:].rearrange("p (t i) -> p t i", i=PACK)
+        replace(0)
+        weave(0)
+        magnitude(PACK - 1)
+        for pos in range(1, PACK):
+            replace(pos)
+            weave(pos)
+
+        v2_words = sb.tile([P, S], U32, name="v2_words", tag=f"page{ORDER[0]}", align_bytes=64)
         nc.vector.tensor_copy(v2_words[:], tab2_win[:].bitcast(U32).indirect(idx2[:]))
-        nc.vector.tensor_copy(v2_sc[:], tab2_sc[:].indirect(idx2[:]))
 
         page_codes, page_sc = [], []
         for c in range(chunks):
@@ -188,24 +225,46 @@ def tile_list_plot_track_scores_kernel(
             gates.append(pair)
 
         tiles = S // P
-        for n in range(tiles):
+        e, d = {}, {}
+
+        def product(n):
             rows = slice(P * n, P * (n + 1))
-            e = sb.tile([P, T], F32, name=f"e{n}", tag=f"win{n % PASSES}", align_bytes=64)
+            e[n] = sb.tile([P, T], F32, name=f"e{n}", tag=f"win{n % PASSES}", align_bytes=64)
             for c in range(chunks):
                 bank = psum.tile([P, BANK], F32, name=f"e{n}{c}", tag=f"bank{chunks * (n % 2) + c}")
                 nc.tensor.matmul_mx(
                     out=bank[:], lhsT=v2_words[:, rows].bitcast(FP8X4), lhsT_scale=v2_sc[:, rows],
                     rhs=page_codes[c][:].bitcast(FP8X4), rhs_scale=page_sc[c][:], start=True, stop=True,
                 )
-                nc.scalar.copy(e[:, c * BANK : (c + 1) * BANK], bank[:])
-            d = sb.tile([P, S], F32, name=f"d{n}", tag=f"w1_bf{n % PASSES}", align_bytes=64)
+                nc.scalar.copy(e[n][:, c * BANK : (c + 1) * BANK], bank[:])
+
+        def pick(n):
+            d[n] = sb.tile([P, S], F32, name=f"d{n}", tag=f"d{n % 3}", align_bytes=64)
+            if n < tiles - 1:
+                nc.vector.tensor_tensor(d[n][:], e[n][:].indirect(idx4[:]), gates[n // 2][:, n % 2, :], ALU.subtract)
+            else:
+                for c in range(2):
+                    cols = slice(c * BANK, (c + 1) * BANK)
+                    nc.vector.tensor_tensor(d[n][:, cols], e[n][:].indirect(half(idx4, c)),
+                                            gates[n // 2][:, n % 2, cols], ALU.subtract)
+
+        def finish(n):
+            rows = slice(P * n, P * (n + 1))
             score = sb.tile([P, S], F32, name=f"score{n}", tag=f"h{n % 3}", align_bytes=64)
             parts = 2 if n == tiles - 1 else 1
-            width = S // parts
             for c in range(parts):
-                cols = slice(c * width, (c + 1) * width)
-                picks = idx4[:, c * width // 16 : (c + 1) * width // 16]
-                nc.vector.tensor_tensor(d[:, cols], e[:].indirect(picks), gates[n // 2][:, n % 2, cols], ALU.subtract)
-                nc.vector.tensor_tensor(d[:, cols], d[:, cols], d[:, cols], ALU.mult)
-                nc.scalar.activation(score[:, cols], d[:, cols], ACT.Exp, scale=-0.25)
+                cols = slice(c * S // parts, (c + 1) * S // parts)
+                if n < tiles - 2:
+                    nc.vector.tensor_tensor(d[n][:, cols], d[n][:, cols], d[n][:, cols], ALU.mult)
+                else:
+                    nc.scalar.activation(d[n][:, cols], d[n][:, cols], ACT.Square)
+                nc.scalar.activation(score[:, cols], d[n][:, cols], ACT.Exp, scale=-0.25)
                 nc.sync.dma_start(out[rows, cols], score[:, cols])
+
+        for step in range(tiles + 2):
+            if step < tiles:
+                product(step)
+            if 1 <= step <= tiles:
+                pick(step - 1)
+            if step >= 2:
+                finish(step - 2)

@@ -22,6 +22,7 @@ PASSES = K // (P * PACK)
 BANK = 512
 QUADS = (0, 2, 1, 3)
 ORDER = (2, 0, 1, 3)
+LAST = ((0, 512), (512, 768), (768, 1024))
 
 
 def tile_list_plot_track_scores_kernel(
@@ -51,18 +52,13 @@ def tile_list_plot_track_scores_kernel(
         def half(lst, c):
             return lst[:, c * 32 : (c + 1) * 32]
 
-        tab_sc = sb.tile([P, T], U8, name="tab_sc", align_bytes=64)
-        v_sc = [sb.tile([P, S], U8, name=f"v_sc{a}", align_bytes=64) for a in range(PASSES)]
-        w4_sc_raw = sb.tile([P, PASSES * H], U8, name="w4_sc_raw", align_bytes=64)
+        tab_sc = sb.tile([P, PASSES * T], U8, name="tab_sc", align_bytes=64)
+        w4_sc_raw = sb.tile([P, PASSES * H], U8, name="w4_sc_raw", tag="w4_sc_raw", align_bytes=64)
         tab2_sc = sb.tile([P, T], U8, name="tab2_sc", align_bytes=64)
-        nc.vector.memset(tab_sc[:].bitcast(I32), 0)
+        nc.vector.memset(tab_sc[:, 0 : 2 * T].bitcast(I32), 0)
+        nc.gpsimd.memset(tab_sc[:, 2 * T : 3 * T].bitcast(I32), 0)
         nc.vector.memset(w4_sc_raw[:].bitcast(I32), 0)
-        nc.vector.memset(tab2_sc[:].bitcast(I32), 0)
-        for a in range(1, PASSES):
-            nc.gpsimd.memset(v_sc[a][:].bitcast(I32), 0)
-        warm = sb.tile([P, 1], F32, name="warm")
-        nc.vector.memset(warm[:], 0.0)
-        nc.scalar.activation(warm[:], warm[:], ACT.Exp)
+        nc.gpsimd.memset(tab2_sc[:].bitcast(I32), 0)
 
         def load_words(a):
             win = sb.tile([P, T], I32, name=f"tab_win{a}", tag=f"win{a}", align_bytes=64)
@@ -79,49 +75,32 @@ def tile_list_plot_track_scores_kernel(
         idx2 = load_list(offs2, "idx2")
         idx3 = load_list(offs3, "idx3")
         idx4 = load_list(offs4, "idx4")
-        for q in QUADS:
-            nc.sync.dma_start(
-                tab_sc[:].bitcast(I32)[32 * q : 32 * q + 4 * PASSES, :],
-                tab_scales.bitcast(I32)[:, 4 * q : 4 * q + 4, :],
-            )
+        load_scales(tab_sc, tab_scales)
         w4_raw = sb.tile([P, PASSES, 2 * H], U8, name="w4_raw", align_bytes=64)
         nc.sync.dma_start(w4_raw[:].bitcast(I32), w4_words.bitcast(I32).rearrange("a p c -> p a c"))
         load_scales(w4_sc_raw, w4_scales)
         w1_raw = [load_w1(0)]
-        load_scales(tab2_sc, tab2_scales)
-        w1_raw.append(load_w1(1))
         tab_win.append(load_words(1))
+        w1_raw.append(load_w1(1))
         w1_raw.append(load_w1(2))
         tab_win.append(load_words(2))
 
         wgs_rows = wgs.rearrange("(q i) j -> q i j", i=PACK)
         page_rows = page0.rearrange("(p i) t -> p i t", i=PACK)
-        factor = [sb.tile([P, S], F32, name=f"factor{i}", align_bytes=64) for i in range(PACK)]
         page = [sb.tile([P, T], F32, name=f"page{i}", tag=f"page{i}", align_bytes=64) for i in range(PACK)]
         tab2_win = sb.tile([P, T], I32, name="tab2_win", align_bytes=64)
+        factor = [sb.tile([P, S], F32, name=f"factor{i}", tag=f"factor{i}", align_bytes=64) for i in range(PACK)]
         for i in ORDER:
             if i == ORDER[-1]:
+                load_scales(tab2_sc, tab2_scales)
                 nc.sync.dma_start(tab2_win[:], tab2_words[0].rearrange("p t i -> p (t i)").bitcast(I32))
             for q in QUADS:
                 nc.sync.dma_start(factor[i][32 * q : 32 * q + 32, :], wgs_rows[:, i, :])
             nc.sync.dma_start(page[i][:], page_rows[:, i, :])
 
-        w4_codes = sb.tile([P, PASSES, 2 * H], U8, name="w4_codes", tag="woven", align_bytes=64)
+        w4_codes = sb.tile([P, PASSES, 2 * H], U8, name="w4_codes", tag="woven3", align_bytes=64)
         w4_sc = sb.tile([P, PASSES, H], U8, name="w4_sc", align_bytes=64)
-        v_words, w1_codes, w1_sc = [], [], []
-        nc.vector.tensor_copy(v_sc[0][:], tab_sc[:].indirect(idx[:]))
-        for a in range(1, PASSES):
-            nc.gpsimd.dma_start(v_sc[a][:].bitcast(I32)[0:112, :], v_sc[0][:].bitcast(I32)[4 * a : 4 * a + 112, :])
         for a in range(PASSES):
-            words = [sb.tile([P, BANK], U32, name=f"v_words{a}{c}", align_bytes=64) for c in range(2)]
-            grouped = sb.tile([P, H * PACK], BF16, name=f"w1_bf{a}", tag=f"w1_bf{a}", align_bytes=64)
-            codes = sb.tile([P, H], U32, name=f"w1_codes{a}", align_bytes=64)
-            wsc = sb.tile([P, H], U8, name=f"w1_sc{a}", align_bytes=64)
-            nc.scalar.activation(
-                grouped[:].rearrange("p (i m j) -> p m j i", i=PACK, j=PACK),
-                w1_raw[a][:].rearrange("p j (m i) -> p m j i", i=PACK),
-                ACT.Copy, scale=-1.0,
-            )
             nc.vector.tensor_copy(
                 w4_codes[:, a, :].bitcast(U16).rearrange("p (i m) -> p i m", i=PACK),
                 w4_raw[:, a, :].bitcast(U16).rearrange("p (m i) -> p i m", i=PACK),
@@ -130,13 +109,25 @@ def tile_list_plot_track_scores_kernel(
                 w4_sc[:, a, :].rearrange("p (i m) -> p i m", i=PACK),
                 w4_sc_raw[:, a * H : (a + 1) * H].rearrange("p (m i) -> p i m", i=PACK),
             )
+        v_words, v_sc, w1_codes, w1_sc = [], [], [], []
+        for a in range(PASSES):
+            last = a == PASSES - 1
+            sc = sb.tile([P, S], U8, name=f"v_sc{a}", tag=("v_sc0", "w4_sc_raw", "win1")[a], align_bytes=64)
+            nc.vector.tensor_copy(sc[:], tab_sc[:, a * T : (a + 1) * T].indirect(idx[:]))
+            grouped = sb.tile([P, H * PACK], BF16, name=f"w1_bf{a}", tag="woven1" if last else f"w1_bf{a}", align_bytes=64)
+            codes = sb.tile([P, H], U32, name=f"w1_codes{a}", tag="woven0" if last else f"w1_codes{a}", align_bytes=64)
+            wsc = sb.tile([P, H], U8, name=f"w1_sc{a}", tag="woven2" if last else f"w1_sc{a}", align_bytes=64)
+            nc.scalar.activation(
+                grouped[:].rearrange("p (i m j) -> p m j i", i=PACK, j=PACK),
+                w1_raw[a][:].rearrange("p j (m i) -> p m j i", i=PACK),
+                ACT.Copy, scale=-1.0,
+            )
             nc.vector.quantize_mx(out=codes[:].bitcast(FP8X4), scales=wsc[:], in_=grouped[:])
+            words = sb.tile([P, S], U32, name=f"v_words{a}", tag="woven1" if last else f"v_words{a}", align_bytes=64)
             for c in range(2):
-                nc.vector.tensor_copy(words[c][:], tab_win[a][:].bitcast(U32).indirect(half(idx, c)))
-            if a == 0:
-                v2_sc = sb.tile([P, S], U8, name="v2_sc", tag="w1_bf0", align_bytes=64)
-                nc.vector.tensor_copy(v2_sc[:], tab2_sc[:].indirect(idx2[:]))
+                nc.vector.tensor_copy(words[:, c * BANK : (c + 1) * BANK], tab_win[a][:].bitcast(U32).indirect(half(idx, c)))
             v_words.append(words)
+            v_sc.append(sc)
             w1_codes.append(codes)
             w1_sc.append(wsc)
 
@@ -149,91 +140,108 @@ def tile_list_plot_track_scores_kernel(
             for c in range(2):
                 acc[i, c] = psum.tile([P, BANK], F32, name=f"acc{i}{c}", tag=f"bank{(2 * pos + c) % 6}")
                 picked = slice(c * BANK, (c + 1) * BANK)
-                passes = [("w4", 0), ("w1", 0), ("w1", 1), ("w4", 1), ("w4", 2), ("w1", 2)]
+                passes = [(which, a) for a in range(PASSES) for which in ("w4", "w1")]
                 for k, (which, a) in enumerate(passes):
                     if which == "w4":
                         lhsT = w4_codes[:, a, 2 * P * i : 2 * P * (i + 1)].bitcast(FP4X4)
                         lhsT_sc = w4_sc[:, a, cols]
-                        rhs_sc = v_sc[a][:, picked]
                     else:
                         lhsT = w1_codes[a][:, cols].bitcast(FP8X4)
                         lhsT_sc = w1_sc[a][:, cols]
-                        rhs_sc = v_sc[0][4 * a :, picked]
                     nc.tensor.matmul_mx(
                         out=acc[i, c][:], lhsT=lhsT, lhsT_scale=lhsT_sc,
-                        rhs=v_words[a][c][:].bitcast(FP8X4), rhs_scale=rhs_sc,
+                        rhs=v_words[a][:, picked].bitcast(FP8X4), rhs_scale=v_sc[a][:, picked],
                         start=(k == 0), stop=(k == len(passes) - 1),
                     )
 
-        def magnitude(pos):
+        def magnitude(pos, c, tag):
             i = ORDER[pos]
-            tag = f"page{ORDER[0]}" if pos == PACK - 1 else f"h{pos}"
-            h[i] = sb.tile([P, S], F32, name=f"h{i}", tag=tag, align_bytes=64)
+            h[i, c] = sb.tile([P, BANK], F32, name=f"h{i}{c}", tag=tag, align_bytes=64)[:]
+            nc.scalar.activation(h[i, c], acc[i, c][:], ACT.Abs)
+
+        def magnitude_whole(pos):
+            i = ORDER[pos]
+            h[i] = sb.tile([P, S], F32, name=f"h{i}", tag=f"h{pos}", align_bytes=64)
             for c in range(2):
-                nc.scalar.activation(h[i][:, c * BANK : (c + 1) * BANK], acc[i, c][:], ACT.Abs)
+                h[i, c] = h[i][:, c * BANK : (c + 1) * BANK]
+                nc.scalar.activation(h[i, c], acc[i, c][:], ACT.Abs)
 
         def replace(pos):
             i = ORDER[pos]
-            if pos == 0:
+            if pos in (0, PACK - 1):
                 for c in range(2):
-                    cols = slice(c * BANK, (c + 1) * BANK)
-                    nc.vector.tensor_tensor(page[i][:].indirect(half(idx3, c)), h[i][:, cols], factor[i][:, cols], ALU.mult)
+                    nc.vector.tensor_tensor(page[i][:].indirect(half(idx3, c)), h[i, c],
+                                            factor[i][:, c * BANK : (c + 1) * BANK], ALU.mult)
             else:
                 nc.vector.tensor_tensor(page[i][:].indirect(idx3[:]), h[i][:], factor[i][:], ALU.mult)
 
         def weave(pos):
             i = ORDER[pos]
-            if pos < PACK - 1:
-                nc.scalar.copy(woven_cols[:, :, i], page[i][:])
-            else:
-                for c in range(chunks):
-                    cols = slice(c * BANK, (c + 1) * BANK)
-                    if c < 2:
-                        nc.vector.tensor_copy(woven_cols[:, cols, i], page[i][:, cols])
-                    else:
-                        nc.scalar.copy(woven_cols[:, cols, i], page[i][:, cols])
+            for c in range(chunks):
+                src = page[i][:, c * BANK : (c + 1) * BANK]
+                if pos == PACK - 1 and c < 2:
+                    nc.vector.tensor_copy(woven[c][:, :, i], src)
+                else:
+                    nc.scalar.copy(woven[c][:, :, i], src)
 
         for pos in range(PACK - 1):
             views(pos)
-            magnitude(pos)
+            magnitude_whole(pos)
         views(PACK - 1)
-        woven = sb.tile([P, T * PACK], BF16, name="woven", tag="woven", align_bytes=64)
-        woven_cols = woven[:].rearrange("p (t i) -> p t i", i=PACK)
+        magnitude(PACK - 1, 0, "h3")
+        woven = [sb.tile([P, BANK, PACK], BF16, name=f"woven{c}", tag=f"woven{c}", align_bytes=64) for c in range(chunks)]
         replace(0)
         weave(0)
-        magnitude(PACK - 1)
+        magnitude(PACK - 1, 1, f"page{ORDER[0]}")
         for pos in range(1, PACK):
             replace(pos)
             weave(pos)
 
-        v2_words = sb.tile([P, S], U32, name="v2_words", tag=f"page{ORDER[0]}", align_bytes=64)
-        nc.vector.tensor_copy(v2_words[:], tab2_win[:].bitcast(U32).indirect(idx2[:]))
+        plots = {}
+
+        def pick_plots(lo, hi, words_tag, sc_tag):
+            words = sb.tile([P, hi - lo], U32, name=f"v2_words{lo}", tag=words_tag, align_bytes=64)
+            sc = sb.tile([P, hi - lo], U8, name=f"v2_sc{lo}", tag=sc_tag, align_bytes=64)
+            part = idx2[:, lo // 16 : hi // 16]
+            for n in range(lo // P, hi // P):
+                cols = slice(P * n - lo, P * (n + 1) - lo)
+                plots[n] = (words[:, cols], sc[:, cols])
+            return (lambda: nc.vector.tensor_copy(words[:], tab2_win[:].bitcast(U32).indirect(part)),
+                    lambda: nc.vector.tensor_copy(sc[:], tab2_sc[:].indirect(part)))
+
+        for step in pick_plots(0, 256, f"page{ORDER[0]}", f"factor{ORDER[-1]}"):
+            step()
 
         page_codes, page_sc = [], []
         for c in range(chunks):
             codes = sb.tile([P, BANK], U32, name=f"page_codes{c}", align_bytes=64)
             sc = sb.tile([P, BANK], U8, name=f"page_sc{c}", align_bytes=64)
             nc.vector.quantize_mx(out=codes[:].bitcast(FP8X4), scales=sc[:],
-                                  in_=woven[:, c * BANK * PACK : (c + 1) * BANK * PACK])
+                                  in_=woven[c][:].rearrange("p t i -> p (t i)"))
             page_codes.append(codes)
             page_sc.append(sc)
+        for step in pick_plots(256, 512, "woven3", f"page{ORDER[-1]}"):
+            step()
 
         gates = []
-        for g in range(S // (2 * P)):
-            pair = sb.tile([P, 2, S], F32, name=f"gate{g}", tag=f"raw{g}", align_bytes=64)
-            nc.sync.dma_start(pair[:], gate[2 * P * g : 2 * P * (g + 1), :].rearrange("(u p) m -> p u m", u=2))
-            gates.append(pair)
+        for n in range(2):
+            single = sb.tile([P, S], F32, name=f"gate{n}", tag=f"gate{n}", align_bytes=64)
+            nc.sync.dma_start(single[:], gate[P * n : P * (n + 1), :])
+            gates.append(single[:])
+        for g in range(PASSES):
+            pair = sb.tile([P, 2, S], F32, name=f"gates{g}", tag=f"raw{g}", align_bytes=64)
+            nc.sync.dma_start(pair[:], gate[2 * P * (g + 1) : 2 * P * (g + 2), :].rearrange("(u p) m -> p u m", u=2))
+            gates.extend([pair[:, 0, :], pair[:, 1, :]])
 
         tiles = S // P
         e, d = {}, {}
 
         def product(n):
-            rows = slice(P * n, P * (n + 1))
             e[n] = sb.tile([P, T], F32, name=f"e{n}", tag=f"win{n % PASSES}", align_bytes=64)
             for c in range(chunks):
                 bank = psum.tile([P, BANK], F32, name=f"e{n}{c}", tag=f"bank{chunks * (n % 2) + c}")
                 nc.tensor.matmul_mx(
-                    out=bank[:], lhsT=v2_words[:, rows].bitcast(FP8X4), lhsT_scale=v2_sc[:, rows],
+                    out=bank[:], lhsT=plots[n][0].bitcast(FP8X4), lhsT_scale=plots[n][1],
                     rhs=page_codes[c][:].bitcast(FP8X4), rhs_scale=page_sc[c][:], start=True, stop=True,
                 )
                 nc.scalar.copy(e[n][:, c * BANK : (c + 1) * BANK], bank[:])
@@ -241,20 +249,18 @@ def tile_list_plot_track_scores_kernel(
         def pick(n):
             d[n] = sb.tile([P, S], F32, name=f"d{n}", tag=f"d{n % 3}", align_bytes=64)
             if n < tiles - 1:
-                nc.vector.tensor_tensor(d[n][:], e[n][:].indirect(idx4[:]), gates[n // 2][:, n % 2, :], ALU.subtract)
+                nc.vector.tensor_tensor(d[n][:], e[n][:].indirect(idx4[:]), gates[n], ALU.subtract)
             else:
-                for c in range(2):
-                    cols = slice(c * BANK, (c + 1) * BANK)
-                    nc.vector.tensor_tensor(d[n][:, cols], e[n][:].indirect(half(idx4, c)),
-                                            gates[n // 2][:, n % 2, cols], ALU.subtract)
+                for lo, hi in LAST:
+                    nc.vector.tensor_tensor(d[n][:, lo:hi], e[n][:].indirect(idx4[:, lo // 16 : hi // 16]),
+                                            gates[n][:, lo:hi], ALU.subtract)
 
         def finish(n):
             rows = slice(P * n, P * (n + 1))
             score = sb.tile([P, S], F32, name=f"score{n}", tag=f"h{n % 3}", align_bytes=64)
-            parts = 2 if n == tiles - 1 else 1
-            for c in range(parts):
-                cols = slice(c * S // parts, (c + 1) * S // parts)
-                if n < tiles - 2:
+            for lo, hi in LAST if n == tiles - 1 else ((0, S),):
+                cols = slice(lo, hi)
+                if n < tiles - 3:
                     nc.vector.tensor_tensor(d[n][:, cols], d[n][:, cols], d[n][:, cols], ALU.mult)
                 else:
                     nc.scalar.activation(d[n][:, cols], d[n][:, cols], ACT.Square)
@@ -266,5 +272,8 @@ def tile_list_plot_track_scores_kernel(
                 product(step)
             if 1 <= step <= tiles:
                 pick(step - 1)
+            if step == 2:
+                for gather in pick_plots(512, S, "gate0", "gate1"):
+                    gather()
             if step >= 2:
                 finish(step - 2)

@@ -112,7 +112,7 @@ def tile_list_plot_track_scores_kernel(
         v_words, v_sc, w1_codes, w1_sc = [], [], [], []
         for a in range(PASSES):
             last = a == PASSES - 1
-            sc = sb.tile([P, S], U8, name=f"v_sc{a}", tag=("v_sc0", "w4_sc_raw", "win1")[a], align_bytes=64)
+            sc = sb.tile([P, S], U8, name=f"v_sc{a}", tag=("v_sc0", "w4_sc_raw", "w1_bf1")[a], align_bytes=64)
             nc.vector.tensor_copy(sc[:], tab_sc[:, a * T : (a + 1) * T].indirect(idx[:]))
             grouped = sb.tile([P, H * PACK], BF16, name=f"w1_bf{a}", tag="woven1" if last else f"w1_bf{a}", align_bytes=64)
             codes = sb.tile([P, H], U32, name=f"w1_codes{a}", tag="woven0" if last else f"w1_codes{a}", align_bytes=64)
@@ -140,7 +140,7 @@ def tile_list_plot_track_scores_kernel(
             for c in range(2):
                 acc[i, c] = psum.tile([P, BANK], F32, name=f"acc{i}{c}", tag=f"bank{(2 * pos + c) % 6}")
                 picked = slice(c * BANK, (c + 1) * BANK)
-                passes = [(which, a) for a in range(PASSES) for which in ("w4", "w1")]
+                passes = [("w4", 0), ("w1", 0)] + [(which, a) for a in range(1, PASSES) for which in ("w1", "w4")]
                 for k, (which, a) in enumerate(passes):
                     if which == "w4":
                         lhsT = w4_codes[:, a, 2 * P * i : 2 * P * (i + 1)].bitcast(FP4X4)

@@ -40,25 +40,30 @@ def tile_list_plot_track_scores_kernel(
             nc.sync.dma_start(t[:], src)
             return t
 
-        def load_scales(plane, src):
+        def load_scale_rows(plane, src):
             passes = src.shape[0]
             rows = plane[:].bitcast(I32).rearrange("p (a c) -> p a c", a=passes)
-            for q in QUADS:
+            for r in range(4):
                 nc.sync.dma_start(
-                    rows[32 * q : 32 * q + 4, :, :],
-                    src.bitcast(I32)[:, 4 * q : 4 * q + 4, :].rearrange("a r c -> r a c"),
+                    rows[r : P : 32, :, :],
+                    src.bitcast(I32)[:, r : 16 : 4, :].rearrange("a q c -> q a c"),
                 )
 
         def half(lst, c):
             return lst[:, c * 32 : (c + 1) * 32]
 
-        tab_sc = sb.tile([P, PASSES * T], U8, name="tab_sc", align_bytes=64)
+        tab_sc = sb.tile([P, T], U8, name="tab_sc", tag="tab_sc", align_bytes=64)
         w4_sc_raw = sb.tile([P, PASSES * H], U8, name="w4_sc_raw", tag="w4_sc_raw", align_bytes=64)
-        tab2_sc = sb.tile([P, T], U8, name="tab2_sc", align_bytes=64)
-        nc.vector.memset(tab_sc[:, 0 : 2 * T].bitcast(I32), 0)
-        nc.gpsimd.memset(tab_sc[:, 2 * T : 3 * T].bitcast(I32), 0)
+        tab2_sc = sb.tile([P, T], U8, name="tab2_sc", tag="tab2_sc", align_bytes=64)
+        moved = [sb.tile([P, S], U8, name=f"moved{a}", align_bytes=64) for a in range(1, PASSES)]
+        nc.gpsimd.memset(tab_sc[:].bitcast(I32), 0)
+        for q in QUADS:
+            nc.gpsimd.dma_start(tab_sc[:].bitcast(I32)[32 * q : 32 * q + 4 * PASSES, :],
+                                tab_scales.bitcast(I32)[:, 4 * q : 4 * q + 4, :])
         nc.vector.memset(w4_sc_raw[:].bitcast(I32), 0)
-        nc.gpsimd.memset(tab2_sc[:].bitcast(I32), 0)
+        nc.vector.memset(tab2_sc[:].bitcast(I32), 0)
+        for plane in moved:
+            nc.vector.memset(plane[:].bitcast(I32), 0)
 
         def load_words(a):
             win = sb.tile([P, T], I32, name=f"tab_win{a}", tag=f"win{a}", align_bytes=64)
@@ -70,66 +75,91 @@ def tile_list_plot_track_scores_kernel(
             nc.sync.dma_start(raw[:], w1[512 * a : 512 * (a + 1), :].rearrange("(p j) c -> p j c", j=PACK))
             return raw
 
-        idx = load_list(offs, "idx")
         tab_win = [load_words(0)]
-        idx2 = load_list(offs2, "idx2")
-        idx3 = load_list(offs3, "idx3")
-        idx4 = load_list(offs4, "idx4")
-        load_scales(tab_sc, tab_scales)
-        w4_raw = sb.tile([P, PASSES, 2 * H], U8, name="w4_raw", align_bytes=64)
-        nc.sync.dma_start(w4_raw[:].bitcast(I32), w4_words.bitcast(I32).rearrange("a p c -> p a c"))
-        load_scales(w4_sc_raw, w4_scales)
+        idx = load_list(offs, "idx")
         w1_raw = [load_w1(0)]
+        w4_raw = sb.tile([P, PASSES, 2 * H], U8, name="w4_raw", tag="w4_raw", align_bytes=64)
+        nc.sync.dma_start(w4_raw[:].bitcast(I32), w4_words.bitcast(I32).rearrange("a p c -> p a c"))
         tab_win.append(load_words(1))
+        idx2 = load_list(offs2, "idx2")
         w1_raw.append(load_w1(1))
+        idx3 = load_list(offs3, "idx3")
+        load_scale_rows(w4_sc_raw, w4_scales)
         w1_raw.append(load_w1(2))
+        load_scale_rows(tab2_sc, tab2_scales)
         tab_win.append(load_words(2))
 
         wgs_rows = wgs.rearrange("(q i) j -> q i j", i=PACK)
         page_rows = page0.rearrange("(p i) t -> p i t", i=PACK)
         page = [sb.tile([P, T], F32, name=f"page{i}", tag=f"page{i}", align_bytes=64) for i in range(PACK)]
         tab2_win = sb.tile([P, T], I32, name="tab2_win", align_bytes=64)
-        factor = [sb.tile([P, S], F32, name=f"factor{i}", tag=f"factor{i}", align_bytes=64) for i in range(PACK)]
-        for i in ORDER:
-            if i == ORDER[-1]:
-                load_scales(tab2_sc, tab2_scales)
-                nc.sync.dma_start(tab2_win[:], tab2_words[0].rearrange("p t i -> p (t i)").bitcast(I32))
-            for q in QUADS:
-                nc.sync.dma_start(factor[i][32 * q : 32 * q + 32, :], wgs_rows[:, i, :])
-            nc.sync.dma_start(page[i][:], page_rows[:, i, :])
+        factor = {}
 
-        w4_codes = sb.tile([P, PASSES, 2 * H], U8, name="w4_codes", tag="woven3", align_bytes=64)
-        w4_sc = sb.tile([P, PASSES, H], U8, name="w4_sc", align_bytes=64)
-        for a in range(PASSES):
-            nc.vector.tensor_copy(
-                w4_codes[:, a, :].bitcast(U16).rearrange("p (i m) -> p i m", i=PACK),
-                w4_raw[:, a, :].bitcast(U16).rearrange("p (m i) -> p i m", i=PACK),
-            )
-            nc.vector.tensor_copy(
-                w4_sc[:, a, :].rearrange("p (i m) -> p i m", i=PACK),
-                w4_sc_raw[:, a * H : (a + 1) * H].rearrange("p (m i) -> p i m", i=PACK),
-            )
-        v_words, v_sc, w1_codes, w1_sc = [], [], [], []
-        for a in range(PASSES):
-            last = a == PASSES - 1
-            sc = sb.tile([P, S], U8, name=f"v_sc{a}", tag=("v_sc0", "w4_sc_raw", "w1_bf1")[a], align_bytes=64)
-            nc.vector.tensor_copy(sc[:], tab_sc[:, a * T : (a + 1) * T].indirect(idx[:]))
-            grouped = sb.tile([P, H * PACK], BF16, name=f"w1_bf{a}", tag="woven1" if last else f"w1_bf{a}", align_bytes=64)
-            codes = sb.tile([P, H], U32, name=f"w1_codes{a}", tag="woven0" if last else f"w1_codes{a}", align_bytes=64)
-            wsc = sb.tile([P, H], U8, name=f"w1_sc{a}", tag="woven2" if last else f"w1_sc{a}", align_bytes=64)
+        def load_factor(i, lo, hi):
+            factor[i, lo] = sb.tile([P, hi - lo], F32, name=f"factor{i}_{lo}", align_bytes=64)
+            for q in QUADS:
+                nc.sync.dma_start(factor[i, lo][32 * q : 32 * q + 32, :], wgs_rows[:, i, lo:hi])
+
+        load_factor(ORDER[0], 0, BANK)
+        nc.sync.dma_start(page[ORDER[0]][:], page_rows[:, ORDER[0], :])
+        load_factor(ORDER[0], BANK, S)
+        for i in ORDER[1:]:
+            if i == ORDER[-1]:
+                nc.sync.dma_start(tab2_win[:], tab2_words[0].rearrange("p t i -> p (t i)").bitcast(I32))
+            load_factor(i, 0, S)
+            nc.sync.dma_start(page[i][:], page_rows[:, i, :])
+        idx4 = load_list(offs4, "idx4")
+
+        v_words = {}
+
+        def pick_words(a, lo, hi, tag):
+            words = sb.tile([P, hi - lo], U32, name=f"v_words{a}_{lo}", tag=tag, align_bytes=64)
+            nc.vector.tensor_copy(words[:], tab_win[a][:].bitcast(U32).indirect(idx[:, lo // 16 : hi // 16]))
+            for c in range(lo // BANK, hi // BANK):
+                v_words[a, c] = words[:, c * BANK - lo : (c + 1) * BANK - lo]
+
+        w1_codes, w1_sc = [], []
+
+        def quantise_w1(a):
+            grouped = sb.tile([P, H * PACK], BF16, name=f"w1_bf{a}", tag=f"w1_bf{a}", align_bytes=64)
+            codes = sb.tile([P, H], U32, name=f"w1_codes{a}", align_bytes=64)
+            wsc = sb.tile([P, H], U8, name=f"w1_sc{a}", tag=("w4_raw", "tab2_sc", "w1_sc2")[a], align_bytes=64)
             nc.scalar.activation(
                 grouped[:].rearrange("p (i m j) -> p m j i", i=PACK, j=PACK),
                 w1_raw[a][:].rearrange("p j (m i) -> p m j i", i=PACK),
                 ACT.Copy, scale=-1.0,
             )
             nc.vector.quantize_mx(out=codes[:].bitcast(FP8X4), scales=wsc[:], in_=grouped[:])
-            words = sb.tile([P, S], U32, name=f"v_words{a}", tag="woven1" if last else f"v_words{a}", align_bytes=64)
-            for c in range(2):
-                nc.vector.tensor_copy(words[:, c * BANK : (c + 1) * BANK], tab_win[a][:].bitcast(U32).indirect(half(idx, c)))
-            v_words.append(words)
-            v_sc.append(sc)
             w1_codes.append(codes)
             w1_sc.append(wsc)
+
+        pick_words(0, 0, S, "v_words0")
+        v_sc = sb.tile([P, S], U8, name="v_sc", align_bytes=64)
+        nc.vector.tensor_copy(v_sc[:], tab_sc[:].indirect(idx[:]))
+        for a in range(1, PASSES):
+            nc.gpsimd.dma_start(moved[a - 1][:].bitcast(I32)[0:112, :], v_sc[:].bitcast(I32)[4 * a : 4 * a + 112, :])
+        v_sc_base = [v_sc] + moved
+
+        w4_codes = sb.tile([P, PASSES, 2 * H], U8, name="w4_codes", tag="tab_sc", align_bytes=64)
+        for a in range(PASSES):
+            nc.vector.tensor_copy(
+                w4_codes[:, a, :].bitcast(U16).rearrange("p (i m) -> p i m", i=PACK),
+                w4_raw[:, a, :].bitcast(U16).rearrange("p (m i) -> p i m", i=PACK),
+            )
+        quantise_w1(0)
+        pick_words(1, 0, S, "w1_bf0")
+        w4_sc = sb.tile([P, PASSES, H], U8, name="w4_sc", tag="win1", align_bytes=64)
+        for a in range(PASSES):
+            nc.vector.tensor_copy(
+                w4_sc[:, a, :].rearrange("p (i m) -> p i m", i=PACK),
+                w4_sc_raw[:, a * H : (a + 1) * H].rearrange("p (m i) -> p i m", i=PACK),
+            )
+        v2_sc = sb.tile([P, S], U8, name="v2_sc", tag="w4_sc_raw", align_bytes=64)
+        nc.vector.tensor_copy(v2_sc[:], tab2_sc[:].indirect(idx2[:]))
+        quantise_w1(1)
+        pick_words(2, 0, BANK, "w1_bf1")
+        quantise_w1(2)
+        pick_words(2, BANK, S, "w1_bf2")
 
         chunks = T // BANK
         acc, h = {}, {}
@@ -138,90 +168,85 @@ def tile_list_plot_track_scores_kernel(
             i = ORDER[pos]
             cols = slice(P * i, P * (i + 1))
             for c in range(2):
-                acc[i, c] = psum.tile([P, BANK], F32, name=f"acc{i}{c}", tag=f"bank{(2 * pos + c) % 6}")
+                acc[i, c] = psum.tile([P, BANK], F32, name=f"acc{i}{c}", tag=f"bank{(2 * pos + c) % 4}")
                 picked = slice(c * BANK, (c + 1) * BANK)
-                passes = [("w4", 0), ("w1", 0)] + [(which, a) for a in range(1, PASSES) for which in ("w1", "w4")]
+                passes = [("w1", 0), ("w4", 0)] + [(which, a) for a in range(1, PASSES) for which in ("w4", "w1")]
                 for k, (which, a) in enumerate(passes):
                     if which == "w4":
                         lhsT = w4_codes[:, a, 2 * P * i : 2 * P * (i + 1)].bitcast(FP4X4)
                         lhsT_sc = w4_sc[:, a, cols]
+                        rhs_sc = v_sc_base[a][:, picked]
                     else:
                         lhsT = w1_codes[a][:, cols].bitcast(FP8X4)
                         lhsT_sc = w1_sc[a][:, cols]
+                        rhs_sc = v_sc[4 * a : P, picked]
                     nc.tensor.matmul_mx(
                         out=acc[i, c][:], lhsT=lhsT, lhsT_scale=lhsT_sc,
-                        rhs=v_words[a][:, picked].bitcast(FP8X4), rhs_scale=v_sc[a][:, picked],
+                        rhs=v_words[a, c].bitcast(FP8X4), rhs_scale=rhs_sc,
                         start=(k == 0), stop=(k == len(passes) - 1),
                     )
 
-        def magnitude(pos, c, tag):
+        def magnitude(pos, tag):
             i = ORDER[pos]
-            h[i, c] = sb.tile([P, BANK], F32, name=f"h{i}{c}", tag=tag, align_bytes=64)[:]
-            nc.scalar.activation(h[i, c], acc[i, c][:], ACT.Abs)
-
-        def magnitude_whole(pos):
-            i = ORDER[pos]
-            h[i] = sb.tile([P, S], F32, name=f"h{i}", tag=f"h{pos}", align_bytes=64)
+            h[i] = sb.tile([P, S], F32, name=f"h{i}", tag=tag, align_bytes=64)
             for c in range(2):
-                h[i, c] = h[i][:, c * BANK : (c + 1) * BANK]
-                nc.scalar.activation(h[i, c], acc[i, c][:], ACT.Abs)
+                nc.scalar.activation(h[i][:, c * BANK : (c + 1) * BANK], acc[i, c][:], ACT.Abs)
 
         def replace(pos):
             i = ORDER[pos]
-            if pos in (0, PACK - 1):
+            if pos == 0:
                 for c in range(2):
-                    nc.vector.tensor_tensor(page[i][:].indirect(half(idx3, c)), h[i, c],
-                                            factor[i][:, c * BANK : (c + 1) * BANK], ALU.mult)
+                    nc.vector.tensor_tensor(page[i][:].indirect(half(idx3, c)), h[i][:, c * BANK : (c + 1) * BANK],
+                                            factor[i, c * BANK][:], ALU.mult)
             else:
-                nc.vector.tensor_tensor(page[i][:].indirect(idx3[:]), h[i][:], factor[i][:], ALU.mult)
+                nc.vector.tensor_tensor(page[i][:].indirect(idx3[:]), h[i][:], factor[i, 0][:], ALU.mult)
+
+        def weave_chunk(pos, c):
+            i = ORDER[pos]
+            src = page[i][:, c * BANK : (c + 1) * BANK]
+            if pos == PACK - 1 and c != 1:
+                nc.vector.tensor_copy(woven[c][:, :, i], src)
+            else:
+                nc.scalar.copy(woven[c][:, :, i], src)
 
         def weave(pos):
-            i = ORDER[pos]
             for c in range(chunks):
-                src = page[i][:, c * BANK : (c + 1) * BANK]
-                if pos == PACK - 1 and c < 2:
-                    nc.vector.tensor_copy(woven[c][:, :, i], src)
-                else:
-                    nc.scalar.copy(woven[c][:, :, i], src)
-
-        for pos in range(PACK - 1):
-            views(pos)
-            magnitude_whole(pos)
-        views(PACK - 1)
-        magnitude(PACK - 1, 0, "h3")
-        woven = [sb.tile([P, BANK, PACK], BF16, name=f"woven{c}", tag=f"woven{c}", align_bytes=64) for c in range(chunks)]
-        replace(0)
-        weave(0)
-        magnitude(PACK - 1, 1, f"page{ORDER[0]}")
-        for pos in range(1, PACK):
-            replace(pos)
-            weave(pos)
+                weave_chunk(pos, c)
 
         plots = {}
 
-        def pick_plots(lo, hi, words_tag, sc_tag):
-            words = sb.tile([P, hi - lo], U32, name=f"v2_words{lo}", tag=words_tag, align_bytes=64)
-            sc = sb.tile([P, hi - lo], U8, name=f"v2_sc{lo}", tag=sc_tag, align_bytes=64)
-            part = idx2[:, lo // 16 : hi // 16]
+        def pick_plots(lo, hi, tag):
+            words = sb.tile([P, hi - lo], U32, name=f"v2_words{lo}", tag=tag, align_bytes=64)
+            nc.vector.tensor_copy(words[:], tab2_win[:].bitcast(U32).indirect(idx2[:, lo // 16 : hi // 16]))
             for n in range(lo // P, hi // P):
-                cols = slice(P * n - lo, P * (n + 1) - lo)
-                plots[n] = (words[:, cols], sc[:, cols])
-            return (lambda: nc.vector.tensor_copy(words[:], tab2_win[:].bitcast(U32).indirect(part)),
-                    lambda: nc.vector.tensor_copy(sc[:], tab2_sc[:].indirect(part)))
+                plots[n] = (words[:, P * n - lo : P * (n + 1) - lo], v2_sc[:, P * n : P * (n + 1)])
 
-        for step in pick_plots(0, 256, f"page{ORDER[0]}", f"factor{ORDER[-1]}"):
-            step()
+        for pos in range(PACK - 1):
+            views(pos)
+            magnitude(pos, f"h{pos}")
+        views(PACK - 1)
+        woven = [sb.tile([P, BANK, PACK], BF16, name=f"woven{c}", tag=f"woven{c}", align_bytes=64) for c in range(chunks)]
+        replace(0)
+        weave(0)
+        magnitude(PACK - 1, f"page{ORDER[0]}")
+        for pos in range(1, PACK):
+            if pos == PACK - 1:
+                pick_plots(0, BANK, "v2_words")
+            replace(pos)
+            if pos < PACK - 1:
+                weave(pos)
 
         page_codes, page_sc = [], []
         for c in range(chunks):
+            for ahead in ((0, 1, 2), (3,), (), ())[c]:
+                weave_chunk(PACK - 1, ahead)
             codes = sb.tile([P, BANK], U32, name=f"page_codes{c}", align_bytes=64)
             sc = sb.tile([P, BANK], U8, name=f"page_sc{c}", align_bytes=64)
             nc.vector.quantize_mx(out=codes[:].bitcast(FP8X4), scales=sc[:],
                                   in_=woven[c][:].rearrange("p t i -> p (t i)"))
             page_codes.append(codes)
             page_sc.append(sc)
-        for step in pick_plots(256, 512, "woven3", f"page{ORDER[-1]}"):
-            step()
+        pick_plots(BANK, S, "woven3")
 
         gates = []
         for n in range(2):
@@ -255,12 +280,13 @@ def tile_list_plot_track_scores_kernel(
                     nc.vector.tensor_tensor(d[n][:, lo:hi], e[n][:].indirect(idx4[:, lo // 16 : hi // 16]),
                                             gates[n][:, lo:hi], ALU.subtract)
 
+
         def finish(n):
             rows = slice(P * n, P * (n + 1))
             score = sb.tile([P, S], F32, name=f"score{n}", tag=f"h{n % 3}", align_bytes=64)
             for lo, hi in LAST if n == tiles - 1 else ((0, S),):
                 cols = slice(lo, hi)
-                if n < tiles - 3:
+                if n not in (tiles - 3, tiles - 2):
                     nc.vector.tensor_tensor(d[n][:, cols], d[n][:, cols], d[n][:, cols], ALU.mult)
                 else:
                     nc.scalar.activation(d[n][:, cols], d[n][:, cols], ACT.Square)
@@ -272,8 +298,5 @@ def tile_list_plot_track_scores_kernel(
                 product(step)
             if 1 <= step <= tiles:
                 pick(step - 1)
-            if step == 2:
-                for gather in pick_plots(512, S, "gate0", "gate1"):
-                    gather()
             if step >= 2:
                 finish(step - 2)

@@ -22,6 +22,7 @@ PASSES = K // (P * PACK)
 BANK = 512
 QUADS = (0, 2, 1, 3)
 ORDER = (2, 0, 1, 3)
+SCALAR_SQUARES = (5, 6)
 LAST = ((0, 512), (512, 768), (768, 1024))
 
 
@@ -96,7 +97,7 @@ def tile_list_plot_track_scores_kernel(
         factor = {}
 
         def load_factor(i, lo, hi):
-            factor[i, lo] = sb.tile([P, hi - lo], F32, name=f"factor{i}_{lo}", align_bytes=64)
+            factor[i, lo] = sb.tile([P, hi - lo], F32, name=f"factor{i}_{lo}", tag=f"factor{i}_{lo}", align_bytes=64)
             for q in QUADS:
                 nc.sync.dma_start(factor[i, lo][32 * q : 32 * q + 32, :], wgs_rows[:, i, lo:hi])
 
@@ -204,10 +205,10 @@ def tile_list_plot_track_scores_kernel(
         def weave_chunk(pos, c):
             i = ORDER[pos]
             src = page[i][:, c * BANK : (c + 1) * BANK]
-            if pos == PACK - 1 and c != 1:
-                nc.vector.tensor_copy(woven[c][:, :, i], src)
+            if pos == PACK - 1 and c == 0:
+                nc.vector.tensor_copy(pairs[c][:, i // 2, :, i % 2], src)
             else:
-                nc.scalar.copy(woven[c][:, :, i], src)
+                nc.scalar.copy(pairs[c][:, i // 2, :, i % 2], src)
 
         def weave(pos):
             for c in range(chunks):
@@ -225,7 +226,7 @@ def tile_list_plot_track_scores_kernel(
             views(pos)
             magnitude(pos, f"h{pos}")
         views(PACK - 1)
-        woven = [sb.tile([P, BANK, PACK], BF16, name=f"woven{c}", tag=f"woven{c}", align_bytes=64) for c in range(chunks)]
+        pairs = [sb.tile([P, 2, BANK, 2], BF16, name=f"pairs{c}", align_bytes=64) for c in range(chunks)]
         replace(0)
         weave(0)
         magnitude(PACK - 1, f"page{ORDER[0]}")
@@ -233,20 +234,23 @@ def tile_list_plot_track_scores_kernel(
             if pos == PACK - 1:
                 pick_plots(0, BANK, "v2_words")
             replace(pos)
-            if pos < PACK - 1:
-                weave(pos)
+            weave(pos)
 
         page_codes, page_sc = [], []
+        woven_tags = ("h0", "h1", f"factor{ORDER[1]}_0", f"factor{ORDER[2]}_0")
         for c in range(chunks):
-            for ahead in ((0, 1, 2), (3,), (), ())[c]:
-                weave_chunk(PACK - 1, ahead)
+            woven = sb.tile([P, BANK * PACK], BF16, name=f"woven{c}", tag=woven_tags[c], align_bytes=64)
+            nc.vector.tensor_copy(
+                woven[:].bitcast(I32).rearrange("p (t u) -> p t u", u=2),
+                pairs[c][:].rearrange("p u t e -> p (u t e)").bitcast(I32).rearrange("p (u t) -> p t u", u=2),
+            )
             codes = sb.tile([P, BANK], U32, name=f"page_codes{c}", align_bytes=64)
             sc = sb.tile([P, BANK], U8, name=f"page_sc{c}", align_bytes=64)
             nc.vector.quantize_mx(out=codes[:].bitcast(FP8X4), scales=sc[:],
-                                  in_=woven[c][:].rearrange("p t i -> p (t i)"))
+                                  in_=woven[:])
             page_codes.append(codes)
             page_sc.append(sc)
-        pick_plots(BANK, S, "woven3")
+        pick_plots(BANK, S, woven_tags[-1])
 
         gates = []
         for n in range(2):
@@ -272,7 +276,7 @@ def tile_list_plot_track_scores_kernel(
                 nc.scalar.copy(e[n][:, c * BANK : (c + 1) * BANK], bank[:])
 
         def pick(n):
-            d[n] = sb.tile([P, S], F32, name=f"d{n}", tag=f"d{n % 3}", align_bytes=64)
+            d[n] = sb.tile([P, S], F32, name=f"d{n}", tag=f"page{n % PACK}", align_bytes=64)
             if n < tiles - 1:
                 nc.vector.tensor_tensor(d[n][:], e[n][:].indirect(idx4[:]), gates[n], ALU.subtract)
             else:
@@ -281,22 +285,29 @@ def tile_list_plot_track_scores_kernel(
                                             gates[n][:, lo:hi], ALU.subtract)
 
 
+        def parts(n):
+            return [slice(lo, hi) for lo, hi in (LAST if n == tiles - 1 else ((0, S),))]
+
+        def square(n):
+            if n not in SCALAR_SQUARES:
+                for cols in parts(n):
+                    nc.vector.tensor_tensor(d[n][:, cols], d[n][:, cols], d[n][:, cols], ALU.mult)
+
         def finish(n):
             rows = slice(P * n, P * (n + 1))
             score = sb.tile([P, S], F32, name=f"score{n}", tag=f"h{n % 3}", align_bytes=64)
-            for lo, hi in LAST if n == tiles - 1 else ((0, S),):
-                cols = slice(lo, hi)
-                if n not in (tiles - 3, tiles - 2):
-                    nc.vector.tensor_tensor(d[n][:, cols], d[n][:, cols], d[n][:, cols], ALU.mult)
-                else:
+            for cols in parts(n):
+                if n in SCALAR_SQUARES:
                     nc.scalar.activation(d[n][:, cols], d[n][:, cols], ACT.Square)
                 nc.scalar.activation(score[:, cols], d[n][:, cols], ACT.Exp, scale=-0.25)
                 nc.sync.dma_start(out[rows, cols], score[:, cols])
 
-        for step in range(tiles + 2):
+        for step in range(tiles + 3):
             if step < tiles:
                 product(step)
             if 1 <= step <= tiles:
                 pick(step - 1)
-            if step >= 2:
-                finish(step - 2)
+            if 2 <= step <= tiles + 1:
+                square(step - 2)
+            if step >= 3:
+                finish(step - 3)

@@ -1,6 +1,7 @@
 from contextlib import ExitStack
 
 import concourse.mybir as mybir
+from concourse.masks import make_identity
 
 K, H, T, S = 1536, 512, 2048, 1024
 FLOPS = 2 * 2 * K * H * S + 2 * H * S * T
@@ -45,7 +46,7 @@ def tile_list_plot_track_scores_kernel(
             passes = src.shape[0]
             rows = plane[:].bitcast(I32).rearrange("p (a c) -> p a c", a=passes)
             for r in range(4):
-                nc.sync.dma_start(
+                nc.gpsimd.dma_start(
                     rows[r : P : 32, :, :],
                     src.bitcast(I32)[:, r : 16 : 4, :].rearrange("a q c -> q a c"),
                 )
@@ -58,6 +59,8 @@ def tile_list_plot_track_scores_kernel(
         tab2_sc = sb.tile([P, T], U8, name="tab2_sc", tag="tab2_sc", align_bytes=64)
         moved = [sb.tile([P, S], U8, name=f"moved{a}", align_bytes=64) for a in range(1, PASSES)]
         nc.gpsimd.memset(tab_sc[:].bitcast(I32), 0)
+        ident = sb.tile([P, P], F32, name="ident", align_bytes=64)
+        make_identity(nc, ident[:])
         for q in QUADS:
             nc.gpsimd.dma_start(tab_sc[:].bitcast(I32)[32 * q : 32 * q + 4 * PASSES, :],
                                 tab_scales.bitcast(I32)[:, 4 * q : 4 * q + 4, :])
@@ -65,6 +68,8 @@ def tile_list_plot_track_scores_kernel(
         nc.vector.memset(tab2_sc[:].bitcast(I32), 0)
         for plane in moved:
             nc.vector.memset(plane[:].bitcast(I32), 0)
+        load_scale_rows(w4_sc_raw, w4_scales)
+        load_scale_rows(tab2_sc, tab2_scales)
 
         def load_words(a):
             win = sb.tile([P, T], I32, name=f"tab_win{a}", tag=f"win{a}", align_bytes=64)
@@ -81,33 +86,21 @@ def tile_list_plot_track_scores_kernel(
         w1_raw = [load_w1(0)]
         w4_raw = sb.tile([P, PASSES, 2 * H], U8, name="w4_raw", tag="w4_raw", align_bytes=64)
         nc.sync.dma_start(w4_raw[:].bitcast(I32), w4_words.bitcast(I32).rearrange("a p c -> p a c"))
+        wgs_sb = sb.tile([P, S], F32, name="wgs_sb", align_bytes=64)
+        nc.sync.dma_start(wgs_sb[:], wgs)
         tab_win.append(load_words(1))
-        idx2 = load_list(offs2, "idx2")
         w1_raw.append(load_w1(1))
-        idx3 = load_list(offs3, "idx3")
-        load_scale_rows(w4_sc_raw, w4_scales)
+        idx2 = load_list(offs2, "idx2")
         w1_raw.append(load_w1(2))
-        load_scale_rows(tab2_sc, tab2_scales)
         tab_win.append(load_words(2))
+        idx3 = load_list(offs3, "idx3")
 
-        wgs_rows = wgs.rearrange("(q i) j -> q i j", i=PACK)
         page_rows = page0.rearrange("(p i) t -> p i t", i=PACK)
         page = [sb.tile([P, T], F32, name=f"page{i}", tag=f"page{i}", align_bytes=64) for i in range(PACK)]
         tab2_win = sb.tile([P, T], I32, name="tab2_win", align_bytes=64)
-        factor = {}
-
-        def load_factor(i, lo, hi):
-            factor[i, lo] = sb.tile([P, hi - lo], F32, name=f"factor{i}_{lo}", tag=f"factor{i}_{lo}", align_bytes=64)
-            for q in QUADS:
-                nc.sync.dma_start(factor[i, lo][32 * q : 32 * q + 32, :], wgs_rows[:, i, lo:hi])
-
-        load_factor(ORDER[0], 0, BANK)
-        nc.sync.dma_start(page[ORDER[0]][:], page_rows[:, ORDER[0], :])
-        load_factor(ORDER[0], BANK, S)
-        for i in ORDER[1:]:
+        for i in ORDER:
             if i == ORDER[-1]:
                 nc.sync.dma_start(tab2_win[:], tab2_words[0].rearrange("p t i -> p (t i)").bitcast(I32))
-            load_factor(i, 0, S)
             nc.sync.dma_start(page[i][:], page_rows[:, i, :])
         idx4 = load_list(offs4, "idx4")
 
@@ -124,7 +117,7 @@ def tile_list_plot_track_scores_kernel(
         def quantise_w1(a):
             grouped = sb.tile([P, H * PACK], BF16, name=f"w1_bf{a}", tag=f"w1_bf{a}", align_bytes=64)
             codes = sb.tile([P, H], U32, name=f"w1_codes{a}", align_bytes=64)
-            wsc = sb.tile([P, H], U8, name=f"w1_sc{a}", tag=("w4_raw", "tab2_sc", "w1_sc2")[a], align_bytes=64)
+            wsc = sb.tile([P, H], U8, name=f"w1_sc{a}", tag=("w4_raw", "w4_sc_raw", "w1_sc2")[a], align_bytes=64)
             nc.scalar.activation(
                 grouped[:].rearrange("p (i m j) -> p m j i", i=PACK, j=PACK),
                 w1_raw[a][:].rearrange("p j (m i) -> p m j i", i=PACK),
@@ -155,12 +148,37 @@ def tile_list_plot_track_scores_kernel(
                 w4_sc[:, a, :].rearrange("p (i m) -> p i m", i=PACK),
                 w4_sc_raw[:, a * H : (a + 1) * H].rearrange("p (m i) -> p i m", i=PACK),
             )
-        v2_sc = sb.tile([P, S], U8, name="v2_sc", tag="w4_sc_raw", align_bytes=64)
-        nc.vector.tensor_copy(v2_sc[:], tab2_sc[:].indirect(idx2[:]))
         quantise_w1(1)
-        pick_words(2, 0, BANK, "w1_bf1")
+        v2_sc = sb.tile([P, S], U8, name="v2_sc", tag="w1_bf1", align_bytes=64)
+        nc.vector.tensor_copy(v2_sc[:], tab2_sc[:].indirect(idx2[:]))
+        pick_words(2, 0, BANK, "tab2_sc")
         quantise_w1(2)
         pick_words(2, BANK, S, "w1_bf2")
+
+        turned = []
+        for b in range(2):
+            bank = psum.tile([P, PACK, P], F32, name=f"turned{b}", tag=f"bank{4 + b}")
+            for u in range(PACK):
+                col = P * (PACK * b + u)
+                nc.tensor.transpose(bank[:, u, :], wgs_sb[:, col : col + P], ident[:])
+            turned.append(bank)
+        factor = {}
+
+        def deal_factor(pos, tag, first_bank):
+            i = ORDER[pos]
+            spread = sb.tile([P, 2, PACK, 4, 32], F32, name=f"spread{i}", tag=tag, align_bytes=64)
+            factor[i] = sb.tile([P, S], F32, name=f"factor{i}", tag=f"factor{i}_0", align_bytes=64)
+            for b in range(2):
+                rows = turned[b][:].rearrange("p u (q i) -> p u q i", i=PACK)[:, :, :, i]
+                nc.scalar.copy(spread[:, b], rows.unsqueeze(2).to_broadcast([P, PACK, 4, 32]))
+            for b in range(2):
+                bank = psum.tile([P, PACK, P], F32, name=f"back{i}{b}", tag=f"bank{first_bank + b}")
+                for u in range(PACK):
+                    nc.tensor.transpose(bank[:, u, :], spread[:, b, u].rearrange("p g q -> p (g q)"), ident[:])
+                nc.scalar.copy(factor[i][:, b * BANK : (b + 1) * BANK], bank[:].rearrange("p u j -> p (u j)"))
+
+        deal_factor(0, "spread0", 6)
+        deal_factor(1, "spread1", 6)
 
         chunks = T // BANK
         acc, h = {}, {}
@@ -169,7 +187,7 @@ def tile_list_plot_track_scores_kernel(
             i = ORDER[pos]
             cols = slice(P * i, P * (i + 1))
             for c in range(2):
-                acc[i, c] = psum.tile([P, BANK], F32, name=f"acc{i}{c}", tag=f"bank{(2 * pos + c) % 4}")
+                acc[i, c] = psum.tile([P, BANK], F32, name=f"acc{i}{c}", tag=f"bank{(0, 2, 6, 2)[pos] + c}")
                 picked = slice(c * BANK, (c + 1) * BANK)
                 passes = [("w1", 0), ("w4", 0)] + [(which, a) for a in range(1, PASSES) for which in ("w4", "w1")]
                 for k, (which, a) in enumerate(passes):
@@ -198,9 +216,9 @@ def tile_list_plot_track_scores_kernel(
             if pos == 0:
                 for c in range(2):
                     nc.vector.tensor_tensor(page[i][:].indirect(half(idx3, c)), h[i][:, c * BANK : (c + 1) * BANK],
-                                            factor[i, c * BANK][:], ALU.mult)
+                                            factor[i][:, c * BANK : (c + 1) * BANK], ALU.mult)
             else:
-                nc.vector.tensor_tensor(page[i][:].indirect(idx3[:]), h[i][:], factor[i, 0][:], ALU.mult)
+                nc.vector.tensor_tensor(page[i][:].indirect(idx3[:]), h[i][:], factor[i][:], ALU.mult)
 
         def weave_chunk(pos, c):
             i = ORDER[pos]
@@ -225,19 +243,22 @@ def tile_list_plot_track_scores_kernel(
         for pos in range(PACK - 1):
             views(pos)
             magnitude(pos, f"h{pos}")
+            if pos == 1:
+                deal_factor(2, "spread0", 0)
         views(PACK - 1)
         pairs = [sb.tile([P, 2, BANK, 2], BF16, name=f"pairs{c}", align_bytes=64) for c in range(chunks)]
         replace(0)
         weave(0)
+        deal_factor(PACK - 1, "h0", 0)
         magnitude(PACK - 1, f"page{ORDER[0]}")
         for pos in range(1, PACK):
             if pos == PACK - 1:
-                pick_plots(0, BANK, "v2_words")
+                pick_plots(0, BANK, f"factor{ORDER[2]}_0")
             replace(pos)
             weave(pos)
 
         page_codes, page_sc = [], []
-        woven_tags = ("h0", "h1", f"factor{ORDER[1]}_0", f"factor{ORDER[2]}_0")
+        woven_tags = ("h0", "h1", f"factor{ORDER[0]}_0", f"factor{ORDER[1]}_0")
         for c in range(chunks):
             woven = sb.tile([P, BANK * PACK], BF16, name=f"woven{c}", tag=woven_tags[c], align_bytes=64)
             nc.vector.tensor_copy(

@@ -46,7 +46,7 @@ def tile_list_plot_track_scores_kernel(
             passes = src.shape[0]
             rows = plane[:].bitcast(I32).rearrange("p (a c) -> p a c", a=passes)
             for r in range(4):
-                nc.gpsimd.dma_start(
+                nc.sync.dma_start(
                     rows[r : P : 32, :, :],
                     src.bitcast(I32)[:, r : 16 : 4, :].rearrange("a q c -> q a c"),
                 )
@@ -68,8 +68,6 @@ def tile_list_plot_track_scores_kernel(
         nc.vector.memset(tab2_sc[:].bitcast(I32), 0)
         for plane in moved:
             nc.vector.memset(plane[:].bitcast(I32), 0)
-        load_scale_rows(w4_sc_raw, w4_scales)
-        load_scale_rows(tab2_sc, tab2_scales)
 
         def load_words(a):
             win = sb.tile([P, T], I32, name=f"tab_win{a}", tag=f"win{a}", align_bytes=64)
@@ -91,7 +89,9 @@ def tile_list_plot_track_scores_kernel(
         tab_win.append(load_words(1))
         w1_raw.append(load_w1(1))
         idx2 = load_list(offs2, "idx2")
+        load_scale_rows(w4_sc_raw, w4_scales)
         w1_raw.append(load_w1(2))
+        load_scale_rows(tab2_sc, tab2_scales)
         tab_win.append(load_words(2))
         idx3 = load_list(offs3, "idx3")
 
@@ -117,7 +117,7 @@ def tile_list_plot_track_scores_kernel(
         def quantise_w1(a):
             grouped = sb.tile([P, H * PACK], BF16, name=f"w1_bf{a}", tag=f"w1_bf{a}", align_bytes=64)
             codes = sb.tile([P, H], U32, name=f"w1_codes{a}", align_bytes=64)
-            wsc = sb.tile([P, H], U8, name=f"w1_sc{a}", tag=("w4_raw", "w4_sc_raw", "w1_sc2")[a], align_bytes=64)
+            wsc = sb.tile([P, H], U8, name=f"w1_sc{a}", tag=("tab_sc", "tab2_sc", "w1_sc2")[a], align_bytes=64)
             nc.scalar.activation(
                 grouped[:].rearrange("p (i m j) -> p m j i", i=PACK, j=PACK),
                 w1_raw[a][:].rearrange("p j (m i) -> p m j i", i=PACK),
@@ -134,7 +134,7 @@ def tile_list_plot_track_scores_kernel(
             nc.gpsimd.dma_start(moved[a - 1][:].bitcast(I32)[0:112, :], v_sc[:].bitcast(I32)[4 * a : 4 * a + 112, :])
         v_sc_base = [v_sc] + moved
 
-        w4_codes = sb.tile([P, PASSES, 2 * H], U8, name="w4_codes", tag="tab_sc", align_bytes=64)
+        w4_codes = sb.tile([P, PASSES, 2 * H], U8, name="w4_codes", align_bytes=64)
         for a in range(PASSES):
             nc.vector.tensor_copy(
                 w4_codes[:, a, :].bitcast(U16).rearrange("p (i m) -> p i m", i=PACK),
@@ -148,10 +148,10 @@ def tile_list_plot_track_scores_kernel(
                 w4_sc[:, a, :].rearrange("p (i m) -> p i m", i=PACK),
                 w4_sc_raw[:, a * H : (a + 1) * H].rearrange("p (m i) -> p i m", i=PACK),
             )
-        quantise_w1(1)
-        v2_sc = sb.tile([P, S], U8, name="v2_sc", tag="w1_bf1", align_bytes=64)
+        v2_sc = sb.tile([P, S], U8, name="v2_sc", tag="w4_sc_raw", align_bytes=64)
         nc.vector.tensor_copy(v2_sc[:], tab2_sc[:].indirect(idx2[:]))
-        pick_words(2, 0, BANK, "tab2_sc")
+        quantise_w1(1)
+        pick_words(2, 0, BANK, "w1_bf1")
         quantise_w1(2)
         pick_words(2, BANK, S, "w1_bf2")
 

@@ -24,6 +24,7 @@ BANK = 512
 QUADS = (0, 2, 1, 3)
 ORDER = (2, 0, 1, 3)
 SCALAR_SQUARES = (5, 6)
+HEAD = 32 - 4 * PASSES
 LAST = ((0, 512), (512, 768), (768, 1024))
 
 
@@ -42,11 +43,11 @@ def tile_list_plot_track_scores_kernel(
             nc.sync.dma_start(t[:], src)
             return t
 
-        def load_scale_rows(plane, src):
+        def load_scale_rows(queue, plane, src):
             passes = src.shape[0]
             rows = plane[:].bitcast(I32).rearrange("p (a c) -> p a c", a=passes)
             for r in range(4):
-                nc.sync.dma_start(
+                queue.dma_start(
                     rows[r : P : 32, :, :],
                     src.bitcast(I32)[:, r : 16 : 4, :].rearrange("a q c -> q a c"),
                 )
@@ -57,15 +58,14 @@ def tile_list_plot_track_scores_kernel(
         tab_sc = sb.tile([P, T], U8, name="tab_sc", tag="tab_sc", align_bytes=64)
         w4_sc_raw = sb.tile([P, PASSES * H], U8, name="w4_sc_raw", tag="w4_sc_raw", align_bytes=64)
         tab2_sc = sb.tile([P, T], U8, name="tab2_sc", tag="tab2_sc", align_bytes=64)
-        moved = [sb.tile([P, S], U8, name=f"moved{a}", align_bytes=64) for a in range(1, PASSES)]
-        nc.gpsimd.memset(tab_sc[:].bitcast(I32), 0)
+        moved = [sb.tile([P, S], U8, name=f"moved{a}", align_bytes=64) for a in range(PASSES)]
         ident = sb.tile([P, P], F32, name="ident", align_bytes=64)
         make_identity(nc, ident[:])
-        for q in QUADS:
-            nc.gpsimd.dma_start(tab_sc[:].bitcast(I32)[32 * q : 32 * q + 4 * PASSES, :],
-                                tab_scales.bitcast(I32)[:, 4 * q : 4 * q + 4, :])
+        nc.gpsimd.memset(tab2_sc[:].bitcast(I32), 0)
+        load_scale_rows(nc.gpsimd, tab2_sc, tab2_scales)
         nc.vector.memset(w4_sc_raw[:].bitcast(I32), 0)
-        nc.vector.memset(tab2_sc[:].bitcast(I32), 0)
+        for q in range(4):
+            nc.vector.memset(tab_sc[:].bitcast(I32)[32 * q : 32 * q + HEAD, :], 0)
         for plane in moved:
             nc.vector.memset(plane[:].bitcast(I32), 0)
 
@@ -81,17 +81,34 @@ def tile_list_plot_track_scores_kernel(
 
         tab_win = [load_words(0)]
         idx = load_list(offs, "idx")
+        wgs_sb = sb.tile([P, S], F32, name="wgs_sb", align_bytes=64)
+        nc.sync.dma_start(wgs_sb[:], wgs)
+        for q in QUADS:
+            nc.sync.dma_start(tab_sc[:].bitcast(I32)[32 * q + HEAD : 32 * q + 32, :],
+                              tab_scales.bitcast(I32)[:, 4 * q : 4 * q + 4, :])
         w1_raw = [load_w1(0)]
         w4_raw = sb.tile([P, PASSES, 2 * H], U8, name="w4_raw", tag="w4_raw", align_bytes=64)
         nc.sync.dma_start(w4_raw[:].bitcast(I32), w4_words.bitcast(I32).rearrange("a p c -> p a c"))
-        wgs_sb = sb.tile([P, S], F32, name="wgs_sb", align_bytes=64)
-        nc.sync.dma_start(wgs_sb[:], wgs)
         tab_win.append(load_words(1))
-        w1_raw.append(load_w1(1))
         idx2 = load_list(offs2, "idx2")
-        load_scale_rows(w4_sc_raw, w4_scales)
+        load_scale_rows(nc.sync, w4_sc_raw, w4_scales)
+        w1_raw.append(load_w1(1))
         w1_raw.append(load_w1(2))
-        load_scale_rows(tab2_sc, tab2_scales)
+
+        v_words = {}
+
+        def pick_words(a, lo, hi, tag):
+            words = sb.tile([P, hi - lo], U32, name=f"v_words{a}_{lo}", tag=tag, align_bytes=64)
+            nc.vector.tensor_copy(words[:], tab_win[a][:].bitcast(U32).indirect(idx[:, lo // 16 : hi // 16]))
+            for c in range(lo // BANK, hi // BANK):
+                v_words[a, c] = words[:, c * BANK - lo : (c + 1) * BANK - lo]
+
+        pick_words(0, 0, S, "v_words0")
+        v_sc = sb.tile([P, S], U8, name="v_sc", align_bytes=64)
+        nc.vector.tensor_copy(v_sc[:], tab_sc[:].indirect(idx[:]))
+        for a in range(PASSES):
+            nc.sync.dma_start(moved[a][:].bitcast(I32)[0:100, :],
+                              v_sc[:].bitcast(I32)[HEAD + 4 * a : HEAD + 4 * a + 100, :])
         tab_win.append(load_words(2))
         idx3 = load_list(offs3, "idx3")
 
@@ -104,20 +121,12 @@ def tile_list_plot_track_scores_kernel(
             nc.sync.dma_start(page[i][:], page_rows[:, i, :])
         idx4 = load_list(offs4, "idx4")
 
-        v_words = {}
-
-        def pick_words(a, lo, hi, tag):
-            words = sb.tile([P, hi - lo], U32, name=f"v_words{a}_{lo}", tag=tag, align_bytes=64)
-            nc.vector.tensor_copy(words[:], tab_win[a][:].bitcast(U32).indirect(idx[:, lo // 16 : hi // 16]))
-            for c in range(lo // BANK, hi // BANK):
-                v_words[a, c] = words[:, c * BANK - lo : (c + 1) * BANK - lo]
-
         w1_codes, w1_sc = [], []
 
         def quantise_w1(a):
             grouped = sb.tile([P, H * PACK], BF16, name=f"w1_bf{a}", tag=f"w1_bf{a}", align_bytes=64)
             codes = sb.tile([P, H], U32, name=f"w1_codes{a}", align_bytes=64)
-            wsc = sb.tile([P, H], U8, name=f"w1_sc{a}", tag=("tab_sc", "tab2_sc", "w1_sc2")[a], align_bytes=64)
+            wsc = sb.tile([P, H], U8, name=f"w1_sc{a}", tag=("w4_raw", "tab2_sc", "w1_sc2")[a], align_bytes=64)
             nc.scalar.activation(
                 grouped[:].rearrange("p (i m j) -> p m j i", i=PACK, j=PACK),
                 w1_raw[a][:].rearrange("p j (m i) -> p m j i", i=PACK),
@@ -127,14 +136,7 @@ def tile_list_plot_track_scores_kernel(
             w1_codes.append(codes)
             w1_sc.append(wsc)
 
-        pick_words(0, 0, S, "v_words0")
-        v_sc = sb.tile([P, S], U8, name="v_sc", align_bytes=64)
-        nc.vector.tensor_copy(v_sc[:], tab_sc[:].indirect(idx[:]))
-        for a in range(1, PASSES):
-            nc.gpsimd.dma_start(moved[a - 1][:].bitcast(I32)[0:112, :], v_sc[:].bitcast(I32)[4 * a : 4 * a + 112, :])
-        v_sc_base = [v_sc] + moved
-
-        w4_codes = sb.tile([P, PASSES, 2 * H], U8, name="w4_codes", align_bytes=64)
+        w4_codes = sb.tile([P, PASSES, 2 * H], U8, name="w4_codes", tag="tab_sc", align_bytes=64)
         for a in range(PASSES):
             nc.vector.tensor_copy(
                 w4_codes[:, a, :].bitcast(U16).rearrange("p (i m) -> p i m", i=PACK),
@@ -164,44 +166,51 @@ def tile_list_plot_track_scores_kernel(
             turned.append(bank)
         factor = {}
 
-        def deal_factor(pos, tag, first_bank):
+        spreads = {}
+
+        def spread_factor(pos, tag):
             i = ORDER[pos]
             spread = sb.tile([P, 2, PACK, 4, 32], F32, name=f"spread{i}", tag=tag, align_bytes=64)
-            factor[i] = sb.tile([P, S], F32, name=f"factor{i}", tag=f"factor{i}_0", align_bytes=64)
             for b in range(2):
                 rows = turned[b][:].rearrange("p u (q i) -> p u q i", i=PACK)[:, :, :, i]
                 nc.scalar.copy(spread[:, b], rows.unsqueeze(2).to_broadcast([P, PACK, 4, 32]))
+            spreads[i] = spread
+
+        def turn_back(pos, first_bank):
+            i = ORDER[pos]
+            spread = spreads[i]
+            factor[i] = sb.tile([P, S], F32, name=f"factor{i}", tag=f"factor{i}_0", align_bytes=64)
             for b in range(2):
                 bank = psum.tile([P, PACK, P], F32, name=f"back{i}{b}", tag=f"bank{first_bank + b}")
                 for u in range(PACK):
                     nc.tensor.transpose(bank[:, u, :], spread[:, b, u].rearrange("p g q -> p (g q)"), ident[:])
                 nc.scalar.copy(factor[i][:, b * BANK : (b + 1) * BANK], bank[:].rearrange("p u j -> p (u j)"))
 
-        deal_factor(0, "spread0", 6)
-        deal_factor(1, "spread1", 6)
+        for pos in range(2):
+            spread_factor(pos, f"spread{pos}")
+            turn_back(pos, 6)
+        spread_factor(2, "raw2")
 
         chunks = T // BANK
         acc, h = {}, {}
 
-        def views(pos):
+        def views(pos, halves=(0, 1)):
             i = ORDER[pos]
             cols = slice(P * i, P * (i + 1))
-            for c in range(2):
-                acc[i, c] = psum.tile([P, BANK], F32, name=f"acc{i}{c}", tag=f"bank{(0, 2, 6, 2)[pos] + c}")
+            for c in halves:
+                acc[i, c] = psum.tile([P, BANK], F32, name=f"acc{i}{c}", tag=f"bank{((0, 0), (1, 2), (1, 2), (0, 1))[pos][c]}")
                 picked = slice(c * BANK, (c + 1) * BANK)
-                passes = [("w1", 0), ("w4", 0)] + [(which, a) for a in range(1, PASSES) for which in ("w4", "w1")]
+                passes = [(which, a) for a in range(PASSES) for which in ("w4", "w1")]
                 for k, (which, a) in enumerate(passes):
                     if which == "w4":
                         lhsT = w4_codes[:, a, 2 * P * i : 2 * P * (i + 1)].bitcast(FP4X4)
                         lhsT_sc = w4_sc[:, a, cols]
-                        rhs_sc = v_sc_base[a][:, picked]
                     else:
                         lhsT = w1_codes[a][:, cols].bitcast(FP8X4)
                         lhsT_sc = w1_sc[a][:, cols]
-                        rhs_sc = v_sc[4 * a : P, picked]
                     nc.tensor.matmul_mx(
                         out=acc[i, c][:], lhsT=lhsT, lhsT_scale=lhsT_sc,
-                        rhs=v_words[a, c].bitcast(FP8X4), rhs_scale=rhs_sc,
+                        rhs=v_words[a, c].bitcast(FP8X4), rhs_scale=moved[a][:, picked],
                         start=(k == 0), stop=(k == len(passes) - 1),
                     )
 
@@ -211,11 +220,16 @@ def tile_list_plot_track_scores_kernel(
             for c in range(2):
                 nc.scalar.activation(h[i][:, c * BANK : (c + 1) * BANK], acc[i, c][:], ACT.Abs)
 
+        def magnitude_half(pos, c, tag):
+            i = ORDER[pos]
+            h[i, c] = sb.tile([P, BANK], F32, name=f"h{i}_{c}", tag=tag, align_bytes=64)
+            nc.scalar.activation(h[i, c][:], acc[i, c][:], ACT.Abs)
+
         def replace(pos):
             i = ORDER[pos]
             if pos == 0:
                 for c in range(2):
-                    nc.vector.tensor_tensor(page[i][:].indirect(half(idx3, c)), h[i][:, c * BANK : (c + 1) * BANK],
+                    nc.vector.tensor_tensor(page[i][:].indirect(half(idx3, c)), h[i, c][:],
                                             factor[i][:, c * BANK : (c + 1) * BANK], ALU.mult)
             else:
                 nc.vector.tensor_tensor(page[i][:].indirect(idx3[:]), h[i][:], factor[i][:], ALU.mult)
@@ -240,16 +254,21 @@ def tile_list_plot_track_scores_kernel(
             for n in range(lo // P, hi // P):
                 plots[n] = (words[:, P * n - lo : P * (n + 1) - lo], v2_sc[:, P * n : P * (n + 1)])
 
-        for pos in range(PACK - 1):
-            views(pos)
-            magnitude(pos, f"h{pos}")
-            if pos == 1:
-                deal_factor(2, "spread0", 0)
+        views(0, (0,))
+        magnitude_half(0, 0, "h_first")
+        views(1)
+        magnitude(1, "h1")
+        views(0, (1,))
+        magnitude_half(0, 1, "h0")
+        turn_back(2, 1)
+        views(2)
+        magnitude(2, "h2")
         views(PACK - 1)
         pairs = [sb.tile([P, 2, BANK, 2], BF16, name=f"pairs{c}", align_bytes=64) for c in range(chunks)]
         replace(0)
         weave(0)
-        deal_factor(PACK - 1, "h0", 0)
+        spread_factor(PACK - 1, "h0")
+        turn_back(PACK - 1, 6)
         magnitude(PACK - 1, f"page{ORDER[0]}")
         for pos in range(1, PACK):
             if pos == PACK - 1:

@@ -24,7 +24,8 @@ BANK = 512
 QUADS = (0, 2, 1, 3)
 ORDER = (2, 0, 1, 3)
 SCALAR_SQUARES = (5, 6)
-HEAD = 32 - 4 * PASSES
+MOVED = 100
+PLOT_ROW = 12
 LAST = ((0, 512), (512, 768), (768, 1024))
 
 
@@ -43,12 +44,12 @@ def tile_list_plot_track_scores_kernel(
             nc.sync.dma_start(t[:], src)
             return t
 
-        def load_scale_rows(queue, plane, src):
+        def load_scale_rows(queue, plane, src, first_row):
             passes = src.shape[0]
             rows = plane[:].bitcast(I32).rearrange("p (a c) -> p a c", a=passes)
             for r in range(4):
                 queue.dma_start(
-                    rows[r : P : 32, :, :],
+                    rows[first_row + r : P : 32, :, :],
                     src.bitcast(I32)[:, r : 16 : 4, :].rearrange("a q c -> q a c"),
                 )
 
@@ -58,16 +59,15 @@ def tile_list_plot_track_scores_kernel(
         tab_sc = sb.tile([P, T], U8, name="tab_sc", tag="tab_sc", align_bytes=64)
         w4_sc_raw = sb.tile([P, PASSES * H], U8, name="w4_sc_raw", tag="w4_sc_raw", align_bytes=64)
         tab2_sc = sb.tile([P, T], U8, name="tab2_sc", tag="tab2_sc", align_bytes=64)
-        moved = [sb.tile([P, S], U8, name=f"moved{a}", align_bytes=64) for a in range(PASSES)]
+        moved = {a: sb.tile([P, S], U8, name=f"moved{a}", align_bytes=64) for a in range(1, PASSES)}
         ident = sb.tile([P, P], F32, name="ident", align_bytes=64)
         make_identity(nc, ident[:])
         nc.gpsimd.memset(tab2_sc[:].bitcast(I32), 0)
-        load_scale_rows(nc.gpsimd, tab2_sc, tab2_scales)
+        load_scale_rows(nc.gpsimd, tab2_sc, tab2_scales, PLOT_ROW)
+        nc.vector.memset(tab_sc[:].bitcast(I32), 0)
         nc.vector.memset(w4_sc_raw[:].bitcast(I32), 0)
-        for q in range(4):
-            nc.vector.memset(tab_sc[:].bitcast(I32)[32 * q : 32 * q + HEAD, :], 0)
-        for plane in moved:
-            nc.vector.memset(plane[:].bitcast(I32), 0)
+        for plane in moved.values():
+            nc.vector.memset(plane[:].bitcast(I32)[96:P], 0)
 
         def load_words(a):
             win = sb.tile([P, T], I32, name=f"tab_win{a}", tag=f"win{a}", align_bytes=64)
@@ -79,21 +79,25 @@ def tile_list_plot_track_scores_kernel(
             nc.sync.dma_start(raw[:], w1[512 * a : 512 * (a + 1), :].rearrange("(p j) c -> p j c", j=PACK))
             return raw
 
+        def load_wgs(b):
+            part = sb.tile([P, BANK], F32, name=f"wgs{b}", align_bytes=64)
+            nc.sync.dma_start(part[:], wgs[:, b * BANK : (b + 1) * BANK])
+            return part
+
         tab_win = [load_words(0)]
         idx = load_list(offs, "idx")
-        wgs_sb = sb.tile([P, S], F32, name="wgs_sb", align_bytes=64)
-        nc.sync.dma_start(wgs_sb[:], wgs)
-        for q in QUADS:
-            nc.sync.dma_start(tab_sc[:].bitcast(I32)[32 * q + HEAD : 32 * q + 32, :],
-                              tab_scales.bitcast(I32)[:, 4 * q : 4 * q + 4, :])
         w1_raw = [load_w1(0)]
+        for q in QUADS:
+            nc.sync.dma_start(tab_sc[:].bitcast(I32)[32 * q : 32 * q + 4 * PASSES, :],
+                              tab_scales.bitcast(I32)[:, 4 * q : 4 * q + 4, :])
+        wgs_sb = [load_wgs(0)]
         w4_raw = sb.tile([P, PASSES, 2 * H], U8, name="w4_raw", tag="w4_raw", align_bytes=64)
         nc.sync.dma_start(w4_raw[:].bitcast(I32), w4_words.bitcast(I32).rearrange("a p c -> p a c"))
         tab_win.append(load_words(1))
+        load_scale_rows(nc.sync, w4_sc_raw, w4_scales, 0)
         idx2 = load_list(offs2, "idx2")
-        load_scale_rows(nc.sync, w4_sc_raw, w4_scales)
         w1_raw.append(load_w1(1))
-        w1_raw.append(load_w1(2))
+        tab_win.append(load_words(2))
 
         v_words = {}
 
@@ -106,10 +110,9 @@ def tile_list_plot_track_scores_kernel(
         pick_words(0, 0, S, "v_words0")
         v_sc = sb.tile([P, S], U8, name="v_sc", align_bytes=64)
         nc.vector.tensor_copy(v_sc[:], tab_sc[:].indirect(idx[:]))
-        for a in range(PASSES):
-            nc.sync.dma_start(moved[a][:].bitcast(I32)[0:100, :],
-                              v_sc[:].bitcast(I32)[HEAD + 4 * a : HEAD + 4 * a + 100, :])
-        tab_win.append(load_words(2))
+        for a in moved:
+            nc.sync.dma_start(moved[a][0:MOVED, :].bitcast(I32), v_sc[4 * a : 4 * a + MOVED, :].bitcast(I32))
+        w1_raw.append(load_w1(2))
         idx3 = load_list(offs3, "idx3")
 
         page_rows = page0.rearrange("(p i) t -> p i t", i=PACK)
@@ -119,77 +122,82 @@ def tile_list_plot_track_scores_kernel(
             if i == ORDER[-1]:
                 nc.sync.dma_start(tab2_win[:], tab2_words[0].rearrange("p t i -> p (t i)").bitcast(I32))
             nc.sync.dma_start(page[i][:], page_rows[:, i, :])
+            if i == ORDER[0]:
+                wgs_sb.append(load_wgs(1))
         idx4 = load_list(offs4, "idx4")
 
-        w1_codes, w1_sc = [], []
+        w1_codes, w1_sc = {}, {}
 
-        def quantise_w1(a):
-            grouped = sb.tile([P, H * PACK], BF16, name=f"w1_bf{a}", tag=f"w1_bf{a}", align_bytes=64)
-            codes = sb.tile([P, H], U32, name=f"w1_codes{a}", align_bytes=64)
-            wsc = sb.tile([P, H], U8, name=f"w1_sc{a}", tag=("w4_raw", "tab2_sc", "w1_sc2")[a], align_bytes=64)
+        def quantise_w1(a, lo, hi):
+            n = hi - lo
+            grouped = sb.tile([P, n * P * PACK], BF16, name=f"w1_bf{a}_{lo}", align_bytes=64)
+            codes = sb.tile([P, n * P], U32, name=f"w1_codes{a}_{lo}", align_bytes=64)
+            wsc = sb.tile([P, n * P], U8, name=f"w1_sc{a}_{lo}", align_bytes=64)
             nc.scalar.activation(
-                grouped[:].rearrange("p (i m j) -> p m j i", i=PACK, j=PACK),
-                w1_raw[a][:].rearrange("p j (m i) -> p m j i", i=PACK),
+                grouped[:].rearrange("p (i m j) -> p m j i", i=n, j=PACK),
+                w1_raw[a][:].rearrange("p j (m i) -> p m j i", i=PACK)[:, :, :, lo:hi],
                 ACT.Copy, scale=-1.0,
             )
             nc.vector.quantize_mx(out=codes[:].bitcast(FP8X4), scales=wsc[:], in_=grouped[:])
-            w1_codes.append(codes)
-            w1_sc.append(wsc)
+            for i in range(lo, hi):
+                w1_codes[a, i] = codes[:, P * (i - lo) : P * (i - lo + 1)]
+                w1_sc[a, i] = wsc[:, P * (i - lo) : P * (i - lo + 1)]
 
-        w4_codes = sb.tile([P, PASSES, 2 * H], U8, name="w4_codes", tag="tab_sc", align_bytes=64)
-        for a in range(PASSES):
-            nc.vector.tensor_copy(
-                w4_codes[:, a, :].bitcast(U16).rearrange("p (i m) -> p i m", i=PACK),
-                w4_raw[:, a, :].bitcast(U16).rearrange("p (m i) -> p i m", i=PACK),
-            )
-        quantise_w1(0)
-        pick_words(1, 0, S, "w1_bf0")
-        w4_sc = sb.tile([P, PASSES, H], U8, name="w4_sc", tag="win1", align_bytes=64)
-        for a in range(PASSES):
-            nc.vector.tensor_copy(
-                w4_sc[:, a, :].rearrange("p (i m) -> p i m", i=PACK),
-                w4_sc_raw[:, a * H : (a + 1) * H].rearrange("p (m i) -> p i m", i=PACK),
-            )
-        v2_sc = sb.tile([P, S], U8, name="v2_sc", tag="w4_sc_raw", align_bytes=64)
-        nc.vector.tensor_copy(v2_sc[:], tab2_sc[:].indirect(idx2[:]))
-        quantise_w1(1)
-        pick_words(2, 0, BANK, "w1_bf1")
-        quantise_w1(2)
-        pick_words(2, BANK, S, "w1_bf2")
+        w4_codes = sb.tile([P, PASSES, 2 * H], U8, name="w4_codes", align_bytes=64)
+        nc.vector.tensor_copy(
+            w4_codes[:].bitcast(U16).rearrange("p a (i m) -> p i a m", i=PACK),
+            w4_raw[:].bitcast(U16).rearrange("p a (m i) -> p i a m", i=PACK),
+        )
+        quantise_w1(0, 0, PACK)
+        pick_words(1, 0, S, "v_words1")
+        w4_sc = sb.tile([P, PASSES, H], U8, name="w4_sc", align_bytes=64)
+        nc.vector.tensor_copy(
+            w4_sc[:].rearrange("p a (i m) -> p i a m", i=PACK),
+            w4_sc_raw[:].rearrange("p (a m i) -> p i a m", a=PASSES, i=PACK),
+        )
+        v2_sc = []
 
-        turned = []
-        for b in range(2):
-            bank = psum.tile([P, PACK, P], F32, name=f"turned{b}", tag=f"bank{4 + b}")
+        def pick_plot_scales(c, tag):
+            plane = sb.tile([P, BANK], U8, name=f"v2_sc{c}", tag=tag, align_bytes=64)
+            nc.vector.tensor_copy(plane[:], tab2_sc[:].indirect(half(idx2, c)))
+            v2_sc.append(plane)
+
+        pick_plot_scales(0, "v2_sc0")
+        quantise_w1(1, 0, PACK)
+        pick_words(2, 0, BANK, "v_words2a")
+        pick_words(2, BANK, S, "v_words2b")
+        quantise_w1(2, 2, PACK)
+        pick_plot_scales(1, "w1_bf2_2")
+        quantise_w1(2, 0, 2)
+
+
+        turned, factor = {}, {}
+        spread_tags = ("spread_c", "spread_d")
+
+        def turn(b):
+            turned[b] = psum.tile([P, PACK, P], F32, name=f"turned{b}", tag=f"bank{4 + b}")
             for u in range(PACK):
-                col = P * (PACK * b + u)
-                nc.tensor.transpose(bank[:, u, :], wgs_sb[:, col : col + P], ident[:])
-            turned.append(bank)
-        factor = {}
+                nc.tensor.transpose(turned[b][:, u, :], wgs_sb[b][:, P * u : P * (u + 1)], ident[:])
 
-        spreads = {}
-
-        def spread_factor(pos, tag):
+        def deal(pos, b, dst, spread_tag, back_bank):
             i = ORDER[pos]
-            spread = sb.tile([P, 2, PACK, 4, 32], F32, name=f"spread{i}", tag=tag, align_bytes=64)
-            for b in range(2):
-                rows = turned[b][:].rearrange("p u (q i) -> p u q i", i=PACK)[:, :, :, i]
-                nc.scalar.copy(spread[:, b], rows.unsqueeze(2).to_broadcast([P, PACK, 4, 32]))
-            spreads[i] = spread
+            spread = sb.tile([P, PACK, 4, 32], F32, name=f"spread{i}{b}", tag=spread_tag, align_bytes=64)
+            rows = turned[b][:].rearrange("p u (q i) -> p u q i", i=PACK)[:, :, :, i]
+            nc.scalar.copy(spread[:], rows.unsqueeze(2).to_broadcast([P, PACK, 4, 32]))
+            bank = psum.tile([P, PACK, P], F32, name=f"back{i}{b}", tag=f"bank{back_bank}")
+            for u in range(PACK):
+                nc.tensor.transpose(bank[:, u, :], spread[:, u].rearrange("p g q -> p (g q)"), ident[:])
+            nc.scalar.copy(dst, bank[:].rearrange("p u j -> p (u j)"))
 
-        def turn_back(pos, first_bank):
-            i = ORDER[pos]
-            spread = spreads[i]
-            factor[i] = sb.tile([P, S], F32, name=f"factor{i}", tag=f"factor{i}_0", align_bytes=64)
-            for b in range(2):
-                bank = psum.tile([P, PACK, P], F32, name=f"back{i}{b}", tag=f"bank{first_bank + b}")
-                for u in range(PACK):
-                    nc.tensor.transpose(bank[:, u, :], spread[:, b, u].rearrange("p g q -> p (g q)"), ident[:])
-                nc.scalar.copy(factor[i][:, b * BANK : (b + 1) * BANK], bank[:].rearrange("p u j -> p (u j)"))
+        for pos in range(PACK):
+            factor[ORDER[pos]] = sb.tile([P, S], F32, name=f"factor{pos}", align_bytes=64)
 
-        for pos in range(2):
-            spread_factor(pos, f"spread{pos}")
-            turn_back(pos, 6)
-        spread_factor(2, "raw2")
+        def deal_half(pos, b, spread_tag):
+            deal(pos, b, factor[ORDER[pos]][:, b * BANK : (b + 1) * BANK], spread_tag, ((6, 6), (7, 7), (6, 7), (2, 3))[pos][b])
+
+        turn(0)
+        deal_half(0, 0, "spread_a")
+        deal_half(1, 0, "spread_b")
 
         chunks = T // BANK
         acc, h = {}, {}
@@ -198,19 +206,21 @@ def tile_list_plot_track_scores_kernel(
             i = ORDER[pos]
             cols = slice(P * i, P * (i + 1))
             for c in halves:
-                acc[i, c] = psum.tile([P, BANK], F32, name=f"acc{i}{c}", tag=f"bank{((0, 0), (1, 2), (1, 2), (0, 1))[pos][c]}")
+                acc[i, c] = psum.tile([P, BANK], F32, name=f"acc{i}{c}", tag=f"bank{((0, 0), (1, 1), (0, 1), (6, 7))[pos][c]}")
                 picked = slice(c * BANK, (c + 1) * BANK)
-                passes = [(which, a) for a in range(PASSES) for which in ("w4", "w1")]
+                passes = [("w1", 0), ("w4", 0), ("w1", 1), ("w4", 1), ("w4", 2), ("w1", 2)]
                 for k, (which, a) in enumerate(passes):
                     if which == "w4":
                         lhsT = w4_codes[:, a, 2 * P * i : 2 * P * (i + 1)].bitcast(FP4X4)
                         lhsT_sc = w4_sc[:, a, cols]
+                        rhs_sc = moved[a][:, picked] if a else v_sc[:, picked]
                     else:
-                        lhsT = w1_codes[a][:, cols].bitcast(FP8X4)
-                        lhsT_sc = w1_sc[a][:, cols]
+                        lhsT = w1_codes[a, i].bitcast(FP8X4)
+                        lhsT_sc = w1_sc[a, i]
+                        rhs_sc = v_sc[4 * a : P, picked]
                     nc.tensor.matmul_mx(
                         out=acc[i, c][:], lhsT=lhsT, lhsT_scale=lhsT_sc,
-                        rhs=v_words[a, c].bitcast(FP8X4), rhs_scale=moved[a][:, picked],
+                        rhs=v_words[a, c].bitcast(FP8X4), rhs_scale=rhs_sc,
                         start=(k == 0), stop=(k == len(passes) - 1),
                     )
 
@@ -225,22 +235,22 @@ def tile_list_plot_track_scores_kernel(
             h[i, c] = sb.tile([P, BANK], F32, name=f"h{i}_{c}", tag=tag, align_bytes=64)
             nc.scalar.activation(h[i, c][:], acc[i, c][:], ACT.Abs)
 
+        def replace_half(pos, c):
+            i = ORDER[pos]
+            nc.vector.tensor_tensor(page[i][:].indirect(half(idx3, c)), h[i, c][:],
+                                    factor[i][:, c * BANK : (c + 1) * BANK], ALU.mult)
+
         def replace(pos):
             i = ORDER[pos]
-            if pos == 0:
-                for c in range(2):
-                    nc.vector.tensor_tensor(page[i][:].indirect(half(idx3, c)), h[i, c][:],
-                                            factor[i][:, c * BANK : (c + 1) * BANK], ALU.mult)
+            if pos == 1:
+                replace_half(pos, 1)
             else:
                 nc.vector.tensor_tensor(page[i][:].indirect(idx3[:]), h[i][:], factor[i][:], ALU.mult)
 
         def weave_chunk(pos, c):
             i = ORDER[pos]
             src = page[i][:, c * BANK : (c + 1) * BANK]
-            if pos == PACK - 1 and c == 0:
-                nc.vector.tensor_copy(pairs[c][:, i // 2, :, i % 2], src)
-            else:
-                nc.scalar.copy(pairs[c][:, i // 2, :, i % 2], src)
+            nc.scalar.copy(pairs[c][:, i // 2, :, i % 2], src)
 
         def weave(pos):
             for c in range(chunks):
@@ -252,44 +262,54 @@ def tile_list_plot_track_scores_kernel(
             words = sb.tile([P, hi - lo], U32, name=f"v2_words{lo}", tag=tag, align_bytes=64)
             nc.vector.tensor_copy(words[:], tab2_win[:].bitcast(U32).indirect(idx2[:, lo // 16 : hi // 16]))
             for n in range(lo // P, hi // P):
-                plots[n] = (words[:, P * n - lo : P * (n + 1) - lo], v2_sc[:, P * n : P * (n + 1)])
+                plots[n] = (words[:, P * n - lo : P * (n + 1) - lo], v2_sc[lo // BANK][PLOT_ROW:P, P * n - lo : P * (n + 1) - lo])
 
-        views(0, (0,))
-        magnitude_half(0, 0, "h_first")
-        views(1)
-        magnitude(1, "h1")
-        views(0, (1,))
-        magnitude_half(0, 1, "h0")
-        turn_back(2, 1)
-        views(2)
-        magnitude(2, "h2")
-        views(PACK - 1)
-        pairs = [sb.tile([P, 2, BANK, 2], BF16, name=f"pairs{c}", align_bytes=64) for c in range(chunks)]
-        replace(0)
+        for pos in range(2):
+            views(pos, (0,))
+            magnitude_half(pos, 0, f"h_first{pos}")
+        turn(1)
+        for pos in range(2):
+            replace_half(pos, 0)
+            views(pos, (1,))
+            deal_half(pos, 1, spread_tags[pos])
+            magnitude_half(pos, 1, f"h{pos}")
+        replace_half(0, 1)
+        for pos in range(2, PACK):
+            for b in range(2):
+                deal_half(pos, b, spread_tags[b])
+            views(pos)
+            magnitude(pos, f"h{pos}")
+        pair_tags = ("v_words2b", "v_words2a", "v_words1", "v_words0")
+        pairs = [sb.tile([P, 2, BANK, 2], BF16, name=f"pairs{c}", tag=pair_tags[c], align_bytes=64) for c in range(chunks)]
         weave(0)
-        spread_factor(PACK - 1, "h0")
-        turn_back(PACK - 1, 6)
-        magnitude(PACK - 1, f"page{ORDER[0]}")
         for pos in range(1, PACK):
-            if pos == PACK - 1:
-                pick_plots(0, BANK, f"factor{ORDER[2]}_0")
             replace(pos)
             weave(pos)
+        pick_plots(0, BANK, "factor3")
 
-        page_codes, page_sc = [], []
-        woven_tags = ("h0", "h1", f"factor{ORDER[0]}_0", f"factor{ORDER[1]}_0")
-        for c in range(chunks):
-            woven = sb.tile([P, BANK * PACK], BF16, name=f"woven{c}", tag=woven_tags[c], align_bytes=64)
+        woven, page_codes, page_sc = [], [], []
+        woven_tags = ("h0", "h1", "factor0", "factor1")
+
+        def interleave(c):
+            tile = sb.tile([P, BANK * PACK], BF16, name=f"woven{c}", tag=woven_tags[c], align_bytes=64)
             nc.vector.tensor_copy(
-                woven[:].bitcast(I32).rearrange("p (t u) -> p t u", u=2),
+                tile[:].bitcast(I32).rearrange("p (t u) -> p t u", u=2),
                 pairs[c][:].rearrange("p u t e -> p (u t e)").bitcast(I32).rearrange("p (u t) -> p t u", u=2),
             )
+            woven.append(tile)
+
+        def quantise_page(c):
             codes = sb.tile([P, BANK], U32, name=f"page_codes{c}", align_bytes=64)
             sc = sb.tile([P, BANK], U8, name=f"page_sc{c}", align_bytes=64)
-            nc.vector.quantize_mx(out=codes[:].bitcast(FP8X4), scales=sc[:],
-                                  in_=woven[:])
+            nc.vector.quantize_mx(out=codes[:].bitcast(FP8X4), scales=sc[:], in_=woven[c][:])
             page_codes.append(codes)
             page_sc.append(sc)
+
+        for step in range(chunks + 1):
+            if step < chunks:
+                interleave(step)
+            if step >= 1:
+                quantise_page(step - 1)
         pick_plots(BANK, S, woven_tags[-1])
 
         gates = []

@@ -21,12 +21,17 @@ P = 128
 PACK = 4
 PASSES = K // (P * PACK)
 BANK = 512
+CHUNKS = T // BANK
+TILES = S // P
 QUADS = (0, 2, 1, 3)
 ORDER = (2, 0, 1, 3)
-SCALAR_SQUARES = (5, 6)
 MOVED = 100
 PLOT_ROW = 12
-LAST = ((0, 512), (512, 768), (768, 1024))
+H_BANKS = ((0, 0), (1, 1), (0, 1), (6, 7))
+FACTOR_BANKS = ((6, 6), (7, 7), (6, 7), (2, 3))
+SCALAR_SQUARES = (5, 6)
+LAST_PIECES = (slice(0, 512), slice(512, 768), slice(768, 1024))
+GATHER_LAG, SQUARE_LAG, EXP_LAG = 1, 2, 4
 
 
 def tile_list_plot_track_scores_kernel(
@@ -39,35 +44,37 @@ def tile_list_plot_track_scores_kernel(
         sb = ctx.enter_context(tc.tile_pool(name="sb", bufs=1))
         psum = ctx.enter_context(tc.psum_pool(name="psum", bufs=1))
 
+        def columns(c):
+            return slice(c * BANK, (c + 1) * BANK)
+
+        def entries(lst, cols):
+            return lst[:, cols.start // 16 : cols.stop // 16]
+
         def load_list(src, name):
             t = lists.tile([P, S // 16], U16, name=name)
             nc.sync.dma_start(t[:], src)
             return t
 
-        def load_scale_rows(queue, plane, src, first_row):
-            passes = src.shape[0]
-            rows = plane[:].bitcast(I32).rearrange("p (a c) -> p a c", a=passes)
+        def load_scale_rows(queue, dst, src, first_row):
+            rows = dst[:].bitcast(I32).rearrange("p (a c) -> p a c", a=src.shape[0])
             for r in range(4):
                 queue.dma_start(
                     rows[first_row + r : P : 32, :, :],
                     src.bitcast(I32)[:, r : 16 : 4, :].rearrange("a q c -> q a c"),
                 )
 
-        def half(lst, c):
-            return lst[:, c * 32 : (c + 1) * 32]
-
-        tab_sc = sb.tile([P, T], U8, name="tab_sc", tag="tab_sc", align_bytes=64)
-        w4_sc_raw = sb.tile([P, PASSES * H], U8, name="w4_sc_raw", tag="w4_sc_raw", align_bytes=64)
-        tab2_sc = sb.tile([P, T], U8, name="tab2_sc", tag="tab2_sc", align_bytes=64)
+        tab_sc = sb.tile([P, T], U8, name="tab_sc", align_bytes=64)
+        w4_sc_raw = sb.tile([P, PASSES * H], U8, name="w4_sc_raw", align_bytes=64)
+        tab2_sc = sb.tile([P, T], U8, name="tab2_sc", align_bytes=64)
         moved = {a: sb.tile([P, S], U8, name=f"moved{a}", align_bytes=64) for a in range(1, PASSES)}
         ident = sb.tile([P, P], F32, name="ident", align_bytes=64)
-        make_identity(nc, ident[:])
         nc.gpsimd.memset(tab2_sc[:].bitcast(I32), 0)
         load_scale_rows(nc.gpsimd, tab2_sc, tab2_scales, PLOT_ROW)
+        make_identity(nc, ident[:])
         nc.vector.memset(tab_sc[:].bitcast(I32), 0)
         nc.vector.memset(w4_sc_raw[:].bitcast(I32), 0)
-        for plane in moved.values():
-            nc.vector.memset(plane[:].bitcast(I32)[96:P], 0)
+        for dst in moved.values():
+            nc.vector.memset(dst[:].bitcast(I32)[96:P], 0)
 
         def load_words(a):
             win = sb.tile([P, T], I32, name=f"tab_win{a}", tag=f"win{a}", align_bytes=64)
@@ -81,33 +88,34 @@ def tile_list_plot_track_scores_kernel(
 
         def load_wgs(b):
             part = sb.tile([P, BANK], F32, name=f"wgs{b}", align_bytes=64)
-            nc.sync.dma_start(part[:], wgs[:, b * BANK : (b + 1) * BANK])
+            nc.sync.dma_start(part[:], wgs[:, columns(b)])
             return part
 
         tab_win = [load_words(0)]
         idx = load_list(offs, "idx")
-        w1_raw = [load_w1(0)]
+        tab_win.append(load_words(1))
         for q in QUADS:
             nc.sync.dma_start(tab_sc[:].bitcast(I32)[32 * q : 32 * q + 4 * PASSES, :],
                               tab_scales.bitcast(I32)[:, 4 * q : 4 * q + 4, :])
+        w1_raw = [load_w1(0)]
         wgs_sb = [load_wgs(0)]
-        w4_raw = sb.tile([P, PASSES, 2 * H], U8, name="w4_raw", tag="w4_raw", align_bytes=64)
+        w4_raw = sb.tile([P, PASSES, 2 * H], U8, name="w4_raw", align_bytes=64)
         nc.sync.dma_start(w4_raw[:].bitcast(I32), w4_words.bitcast(I32).rearrange("a p c -> p a c"))
-        tab_win.append(load_words(1))
+        w1_raw.append(load_w1(1))
         load_scale_rows(nc.sync, w4_sc_raw, w4_scales, 0)
         idx2 = load_list(offs2, "idx2")
-        w1_raw.append(load_w1(1))
         tab_win.append(load_words(2))
 
         v_words = {}
 
         def pick_words(a, lo, hi, tag):
             words = sb.tile([P, hi - lo], U32, name=f"v_words{a}_{lo}", tag=tag, align_bytes=64)
-            nc.vector.tensor_copy(words[:], tab_win[a][:].bitcast(U32).indirect(idx[:, lo // 16 : hi // 16]))
+            nc.vector.tensor_copy(words[:], tab_win[a][:].bitcast(U32).indirect(entries(idx, slice(lo, hi))))
             for c in range(lo // BANK, hi // BANK):
                 v_words[a, c] = words[:, c * BANK - lo : (c + 1) * BANK - lo]
 
         pick_words(0, 0, S, "v_words0")
+        pick_words(1, 0, S, "v_words1")
         v_sc = sb.tile([P, S], U8, name="v_sc", align_bytes=64)
         nc.vector.tensor_copy(v_sc[:], tab_sc[:].indirect(idx[:]))
         for a in moved:
@@ -116,7 +124,7 @@ def tile_list_plot_track_scores_kernel(
         idx3 = load_list(offs3, "idx3")
 
         page_rows = page0.rearrange("(p i) t -> p i t", i=PACK)
-        page = [sb.tile([P, T], F32, name=f"page{i}", tag=f"page{i}", align_bytes=64) for i in range(PACK)]
+        page = [sb.tile([P, T], F32, name=f"page{i}", align_bytes=64) for i in range(PACK)]
         tab2_win = sb.tile([P, T], I32, name="tab2_win", align_bytes=64)
         for i in ORDER:
             if i == ORDER[-1]:
@@ -128,246 +136,247 @@ def tile_list_plot_track_scores_kernel(
 
         w1_codes, w1_sc = {}, {}
 
-        def quantise_w1(a, lo, hi):
+        def round_on_scalar(dst, src):
+            nc.scalar.activation(dst, src, ACT.Copy, scale=-1.0)
+
+        def round_on_vector(dst, src):
+            nc.vector.tensor_scalar_mul(dst, src, -1.0)
+
+        def quantise_w1(a, lo, hi, negate_and_round):
             n = hi - lo
             grouped = sb.tile([P, n * P * PACK], BF16, name=f"w1_bf{a}_{lo}", align_bytes=64)
             codes = sb.tile([P, n * P], U32, name=f"w1_codes{a}_{lo}", align_bytes=64)
-            wsc = sb.tile([P, n * P], U8, name=f"w1_sc{a}_{lo}", align_bytes=64)
-            nc.scalar.activation(
+            scales = sb.tile([P, n * P], U8, name=f"w1_sc{a}_{lo}", align_bytes=64)
+            negate_and_round(
                 grouped[:].rearrange("p (i m j) -> p m j i", i=n, j=PACK),
                 w1_raw[a][:].rearrange("p j (m i) -> p m j i", i=PACK)[:, :, :, lo:hi],
-                ACT.Copy, scale=-1.0,
             )
-            nc.vector.quantize_mx(out=codes[:].bitcast(FP8X4), scales=wsc[:], in_=grouped[:])
+            nc.vector.quantize_mx(out=codes[:].bitcast(FP8X4), scales=scales[:], in_=grouped[:])
             for i in range(lo, hi):
                 w1_codes[a, i] = codes[:, P * (i - lo) : P * (i - lo + 1)]
-                w1_sc[a, i] = wsc[:, P * (i - lo) : P * (i - lo + 1)]
+                w1_sc[a, i] = scales[:, P * (i - lo) : P * (i - lo + 1)]
 
         w4_codes = sb.tile([P, PASSES, 2 * H], U8, name="w4_codes", align_bytes=64)
         nc.vector.tensor_copy(
             w4_codes[:].bitcast(U16).rearrange("p a (i m) -> p i a m", i=PACK),
             w4_raw[:].bitcast(U16).rearrange("p a (m i) -> p i a m", i=PACK),
         )
-        quantise_w1(0, 0, PACK)
-        pick_words(1, 0, S, "v_words1")
+        quantise_w1(0, 0, PACK, round_on_scalar)
         w4_sc = sb.tile([P, PASSES, H], U8, name="w4_sc", align_bytes=64)
         nc.vector.tensor_copy(
             w4_sc[:].rearrange("p a (i m) -> p i a m", i=PACK),
             w4_sc_raw[:].rearrange("p (a m i) -> p i a m", a=PASSES, i=PACK),
         )
-        v2_sc = []
+        plot_sc = []
 
         def pick_plot_scales(c, tag):
-            plane = sb.tile([P, BANK], U8, name=f"v2_sc{c}", tag=tag, align_bytes=64)
-            nc.vector.tensor_copy(plane[:], tab2_sc[:].indirect(half(idx2, c)))
-            v2_sc.append(plane)
+            scales = sb.tile([P, BANK], U8, name=f"v2_sc{c}", tag=tag, align_bytes=64)
+            nc.vector.tensor_copy(scales[:], tab2_sc[:].indirect(entries(idx2, columns(c))))
+            plot_sc.append(scales)
 
         pick_plot_scales(0, "v2_sc0")
-        quantise_w1(1, 0, PACK)
+        quantise_w1(1, 0, PACK, round_on_scalar)
         pick_words(2, 0, BANK, "v_words2a")
         pick_words(2, BANK, S, "v_words2b")
-        quantise_w1(2, 2, PACK)
+        quantise_w1(2, 2, PACK, round_on_vector)
         pick_plot_scales(1, "w1_bf2_2")
-        quantise_w1(2, 0, 2)
+        quantise_w1(2, 0, 2, round_on_scalar)
 
-
-        turned, factor = {}, {}
-        spread_tags = ("spread_c", "spread_d")
+        turned = {}
+        factor = {ORDER[pos]: sb.tile([P, S], F32, name=f"factor{pos}", align_bytes=64) for pos in range(PACK)}
 
         def turn(b):
             turned[b] = psum.tile([P, PACK, P], F32, name=f"turned{b}", tag=f"bank{4 + b}")
             for u in range(PACK):
                 nc.tensor.transpose(turned[b][:, u, :], wgs_sb[b][:, P * u : P * (u + 1)], ident[:])
 
-        def deal(pos, b, dst, spread_tag, back_bank):
+        def deal_factor(pos, b, spread_tag):
             i = ORDER[pos]
             spread = sb.tile([P, PACK, 4, 32], F32, name=f"spread{i}{b}", tag=spread_tag, align_bytes=64)
             rows = turned[b][:].rearrange("p u (q i) -> p u q i", i=PACK)[:, :, :, i]
             nc.scalar.copy(spread[:], rows.unsqueeze(2).to_broadcast([P, PACK, 4, 32]))
-            bank = psum.tile([P, PACK, P], F32, name=f"back{i}{b}", tag=f"bank{back_bank}")
+            bank = psum.tile([P, PACK, P], F32, name=f"back{i}{b}", tag=f"bank{FACTOR_BANKS[pos][b]}")
             for u in range(PACK):
                 nc.tensor.transpose(bank[:, u, :], spread[:, u].rearrange("p g q -> p (g q)"), ident[:])
-            nc.scalar.copy(dst, bank[:].rearrange("p u j -> p (u j)"))
-
-        for pos in range(PACK):
-            factor[ORDER[pos]] = sb.tile([P, S], F32, name=f"factor{pos}", align_bytes=64)
-
-        def deal_half(pos, b, spread_tag):
-            deal(pos, b, factor[ORDER[pos]][:, b * BANK : (b + 1) * BANK], spread_tag, ((6, 6), (7, 7), (6, 7), (2, 3))[pos][b])
+            nc.scalar.copy(factor[i][:, columns(b)], bank[:].rearrange("p u j -> p (u j)"))
 
         turn(0)
-        deal_half(0, 0, "spread_a")
-        deal_half(1, 0, "spread_b")
+        deal_factor(0, 0, "spread_a")
+        deal_factor(1, 0, "spread_b")
 
-        chunks = T // BANK
         acc, h = {}, {}
+        passes = (("w1", 0), ("w4", 0), ("w1", 1), ("w4", 1), ("w4", 2), ("w1", 2))
 
-        def views(pos, halves=(0, 1)):
+        def difference(pos, c):
             i = ORDER[pos]
-            cols = slice(P * i, P * (i + 1))
-            for c in halves:
-                acc[i, c] = psum.tile([P, BANK], F32, name=f"acc{i}{c}", tag=f"bank{((0, 0), (1, 1), (0, 1), (6, 7))[pos][c]}")
-                picked = slice(c * BANK, (c + 1) * BANK)
-                passes = [("w1", 0), ("w4", 0), ("w1", 1), ("w4", 1), ("w4", 2), ("w1", 2)]
-                for k, (which, a) in enumerate(passes):
-                    if which == "w4":
-                        lhsT = w4_codes[:, a, 2 * P * i : 2 * P * (i + 1)].bitcast(FP4X4)
-                        lhsT_sc = w4_sc[:, a, cols]
-                        rhs_sc = moved[a][:, picked] if a else v_sc[:, picked]
-                    else:
-                        lhsT = w1_codes[a, i].bitcast(FP8X4)
-                        lhsT_sc = w1_sc[a, i]
-                        rhs_sc = v_sc[4 * a : P, picked]
-                    nc.tensor.matmul_mx(
-                        out=acc[i, c][:], lhsT=lhsT, lhsT_scale=lhsT_sc,
-                        rhs=v_words[a, c].bitcast(FP8X4), rhs_scale=rhs_sc,
-                        start=(k == 0), stop=(k == len(passes) - 1),
-                    )
-
-        def magnitude(pos, tag):
-            i = ORDER[pos]
-            h[i] = sb.tile([P, S], F32, name=f"h{i}", tag=tag, align_bytes=64)
-            for c in range(2):
-                nc.scalar.activation(h[i][:, c * BANK : (c + 1) * BANK], acc[i, c][:], ACT.Abs)
+            acc[i, c] = psum.tile([P, BANK], F32, name=f"acc{i}{c}", tag=f"bank{H_BANKS[pos][c]}")
+            for k, (weight, a) in enumerate(passes):
+                if weight == "w4":
+                    lhsT = w4_codes[:, a, 2 * P * i : 2 * P * (i + 1)].bitcast(FP4X4)
+                    lhsT_sc = w4_sc[:, a, P * i : P * (i + 1)]
+                    rhs_sc = moved[a][:, columns(c)] if a else v_sc[:, columns(c)]
+                else:
+                    lhsT = w1_codes[a, i].bitcast(FP8X4)
+                    lhsT_sc = w1_sc[a, i]
+                    rhs_sc = v_sc[4 * a : P, columns(c)]
+                nc.tensor.matmul_mx(
+                    out=acc[i, c][:], lhsT=lhsT, lhsT_scale=lhsT_sc,
+                    rhs=v_words[a, c].bitcast(FP8X4), rhs_scale=rhs_sc,
+                    start=(k == 0), stop=(k == len(passes) - 1),
+                )
 
         def magnitude_half(pos, c, tag):
             i = ORDER[pos]
             h[i, c] = sb.tile([P, BANK], F32, name=f"h{i}_{c}", tag=tag, align_bytes=64)
             nc.scalar.activation(h[i, c][:], acc[i, c][:], ACT.Abs)
 
+        def magnitude(pos):
+            i = ORDER[pos]
+            h[i] = sb.tile([P, S], F32, name=f"h{i}_all", tag=f"h{pos}", align_bytes=64)
+            for c in range(2):
+                nc.scalar.activation(h[i][:, columns(c)], acc[i, c][:], ACT.Abs)
+
         def replace_half(pos, c):
             i = ORDER[pos]
-            nc.vector.tensor_tensor(page[i][:].indirect(half(idx3, c)), h[i, c][:],
-                                    factor[i][:, c * BANK : (c + 1) * BANK], ALU.mult)
+            nc.vector.tensor_tensor(page[i][:].indirect(entries(idx3, columns(c))), h[i, c][:],
+                                    factor[i][:, columns(c)], ALU.mult)
 
         def replace(pos):
             i = ORDER[pos]
-            if pos == 1:
-                replace_half(pos, 1)
-            else:
-                nc.vector.tensor_tensor(page[i][:].indirect(idx3[:]), h[i][:], factor[i][:], ALU.mult)
-
-        def weave_chunk(pos, c):
-            i = ORDER[pos]
-            src = page[i][:, c * BANK : (c + 1) * BANK]
-            nc.scalar.copy(pairs[c][:, i // 2, :, i % 2], src)
-
-        def weave(pos):
-            for c in range(chunks):
-                weave_chunk(pos, c)
-
-        plots = {}
-
-        def pick_plots(lo, hi, tag):
-            words = sb.tile([P, hi - lo], U32, name=f"v2_words{lo}", tag=tag, align_bytes=64)
-            nc.vector.tensor_copy(words[:], tab2_win[:].bitcast(U32).indirect(idx2[:, lo // 16 : hi // 16]))
-            for n in range(lo // P, hi // P):
-                plots[n] = (words[:, P * n - lo : P * (n + 1) - lo], v2_sc[lo // BANK][PLOT_ROW:P, P * n - lo : P * (n + 1) - lo])
+            nc.vector.tensor_tensor(page[i][:].indirect(idx3[:]), h[i][:], factor[i][:], ALU.mult)
 
         for pos in range(2):
-            views(pos, (0,))
+            difference(pos, 0)
             magnitude_half(pos, 0, f"h_first{pos}")
         turn(1)
+        spread_tags = ("spread_c", "spread_d")
         for pos in range(2):
             replace_half(pos, 0)
-            views(pos, (1,))
-            deal_half(pos, 1, spread_tags[pos])
+            difference(pos, 1)
+            deal_factor(pos, 1, spread_tags[pos])
             magnitude_half(pos, 1, f"h{pos}")
         replace_half(0, 1)
         for pos in range(2, PACK):
             for b in range(2):
-                deal_half(pos, b, spread_tags[b])
-            views(pos)
-            magnitude(pos, f"h{pos}")
+                deal_factor(pos, b, spread_tags[b])
+            for c in range(2):
+                difference(pos, c)
+            magnitude(pos)
+
         pair_tags = ("v_words2b", "v_words2a", "v_words1", "v_words0")
-        pairs = [sb.tile([P, 2, BANK, 2], BF16, name=f"pairs{c}", tag=pair_tags[c], align_bytes=64) for c in range(chunks)]
-        weave(0)
-        for pos in range(1, PACK):
+        pairs = [sb.tile([P, 2, BANK, 2], BF16, name=f"pairs{c}", tag=pair_tags[c], align_bytes=64) for c in range(CHUNKS)]
+
+        def round_slice(pos):
+            i = ORDER[pos]
+            for c in range(CHUNKS):
+                nc.scalar.copy(pairs[c][:, i // 2, :, i % 2], page[i][:, columns(c)])
+
+        round_slice(0)
+        replace_half(1, 1)
+        round_slice(1)
+        for pos in range(2, PACK):
             replace(pos)
-            weave(pos)
-        pick_plots(0, BANK, "factor3")
+            round_slice(pos)
+
+        plots = {}
+
+        def pick_plots(c, tag):
+            words = sb.tile([P, BANK], U32, name=f"v2_words{c * BANK}", tag=tag, align_bytes=64)
+            nc.vector.tensor_copy(words[:], tab2_win[:].bitcast(U32).indirect(entries(idx2, columns(c))))
+            for u in range(BANK // P):
+                cols = slice(P * u, P * (u + 1))
+                plots[c * BANK // P + u] = (words[:, cols], plot_sc[c][PLOT_ROW:P, cols])
+
+        pick_plots(0, "factor3")
 
         woven, page_codes, page_sc = [], [], []
         woven_tags = ("h0", "h1", "factor0", "factor1")
 
         def interleave(c):
-            tile = sb.tile([P, BANK * PACK], BF16, name=f"woven{c}", tag=woven_tags[c], align_bytes=64)
+            both = sb.tile([P, BANK * PACK], BF16, name=f"woven{c}", tag=woven_tags[c], align_bytes=64)
             nc.vector.tensor_copy(
-                tile[:].bitcast(I32).rearrange("p (t u) -> p t u", u=2),
+                both[:].bitcast(I32).rearrange("p (t u) -> p t u", u=2),
                 pairs[c][:].rearrange("p u t e -> p (u t e)").bitcast(I32).rearrange("p (u t) -> p t u", u=2),
             )
-            woven.append(tile)
+            woven.append(both)
 
         def quantise_page(c):
             codes = sb.tile([P, BANK], U32, name=f"page_codes{c}", align_bytes=64)
-            sc = sb.tile([P, BANK], U8, name=f"page_sc{c}", align_bytes=64)
-            nc.vector.quantize_mx(out=codes[:].bitcast(FP8X4), scales=sc[:], in_=woven[c][:])
+            scales = sb.tile([P, BANK], U8, name=f"page_sc{c}", align_bytes=64)
+            nc.vector.quantize_mx(out=codes[:].bitcast(FP8X4), scales=scales[:], in_=woven[c][:])
             page_codes.append(codes)
-            page_sc.append(sc)
+            page_sc.append(scales)
 
-        for step in range(chunks + 1):
-            if step < chunks:
+        for step in range(CHUNKS + 1):
+            if step < CHUNKS:
                 interleave(step)
             if step >= 1:
                 quantise_page(step - 1)
-        pick_plots(BANK, S, woven_tags[-1])
+        pick_plots(1, woven_tags[-1])
 
         gates = []
         for n in range(2):
-            single = sb.tile([P, S], F32, name=f"gate{n}", tag=f"gate{n}", align_bytes=64)
+            single = sb.tile([P, S], F32, name=f"gate{n}", align_bytes=64)
             nc.sync.dma_start(single[:], gate[P * n : P * (n + 1), :])
             gates.append(single[:])
         for g in range(PASSES):
-            pair = sb.tile([P, 2, S], F32, name=f"gates{g}", tag=f"raw{g}", align_bytes=64)
-            nc.sync.dma_start(pair[:], gate[2 * P * (g + 1) : 2 * P * (g + 2), :].rearrange("(u p) m -> p u m", u=2))
-            gates.extend([pair[:, 0, :], pair[:, 1, :]])
+            both = sb.tile([P, 2, S], F32, name=f"gates{g}", tag=f"raw{g}", align_bytes=64)
+            nc.sync.dma_start(both[:], gate[2 * P * (g + 1) : 2 * P * (g + 2), :].rearrange("(u p) m -> p u m", u=2))
+            gates.extend([both[:, 0, :], both[:, 1, :]])
 
-        tiles = S // P
         e, d = {}, {}
+        e_tags = ("win0", "win1", "win2", "tab2_win")
+        score_tags = ("h0", "h1", "h2")
+        whole = slice(0, S)
+        last = TILES - 1
 
         def product(n):
-            e[n] = sb.tile([P, T], F32, name=f"e{n}", tag=f"win{n % PASSES}", align_bytes=64)
-            for c in range(chunks):
-                bank = psum.tile([P, BANK], F32, name=f"e{n}{c}", tag=f"bank{chunks * (n % 2) + c}")
+            e[n] = sb.tile([P, T], F32, name=f"e{n}", tag=e_tags[n % len(e_tags)], align_bytes=64)
+            for c in range(CHUNKS):
+                bank = psum.tile([P, BANK], F32, name=f"e{n}{c}", tag=f"bank{CHUNKS * (n % 2) + c}")
                 nc.tensor.matmul_mx(
                     out=bank[:], lhsT=plots[n][0].bitcast(FP8X4), lhsT_scale=plots[n][1],
                     rhs=page_codes[c][:].bitcast(FP8X4), rhs_scale=page_sc[c][:], start=True, stop=True,
                 )
-                nc.scalar.copy(e[n][:, c * BANK : (c + 1) * BANK], bank[:])
+                if n == 0 and c == CHUNKS - 1:
+                    nc.vector.tensor_copy(e[n][:, columns(c)], bank[:])
+                else:
+                    nc.scalar.copy(e[n][:, columns(c)], bank[:])
 
-        def pick(n):
+        def pick(n, cols):
+            nc.vector.tensor_tensor(d[n][:, cols], e[n][:].indirect(entries(idx4, cols)), gates[n][:, cols], ALU.subtract)
+
+        def square_on_vector(n, cols):
+            nc.vector.tensor_tensor(d[n][:, cols], d[n][:, cols], d[n][:, cols], ALU.mult)
+
+        def gather(n):
             d[n] = sb.tile([P, S], F32, name=f"d{n}", tag=f"page{n % PACK}", align_bytes=64)
-            if n < tiles - 1:
-                nc.vector.tensor_tensor(d[n][:], e[n][:].indirect(idx4[:]), gates[n], ALU.subtract)
+            if n < last:
+                pick(n, whole)
             else:
-                for lo, hi in LAST:
-                    nc.vector.tensor_tensor(d[n][:, lo:hi], e[n][:].indirect(idx4[:, lo // 16 : hi // 16]),
-                                            gates[n][:, lo:hi], ALU.subtract)
-
-
-        def parts(n):
-            return [slice(lo, hi) for lo, hi in (LAST if n == tiles - 1 else ((0, S),))]
-
-        def square(n):
-            if n not in SCALAR_SQUARES:
-                for cols in parts(n):
-                    nc.vector.tensor_tensor(d[n][:, cols], d[n][:, cols], d[n][:, cols], ALU.mult)
+                first, second, third = LAST_PIECES
+                pick(n, first)
+                pick(n, second)
+                square_on_vector(n, first)
+                pick(n, third)
+                square_on_vector(n, second)
+                square_on_vector(n, third)
 
         def finish(n):
-            rows = slice(P * n, P * (n + 1))
-            score = sb.tile([P, S], F32, name=f"score{n}", tag=f"h{n % 3}", align_bytes=64)
-            for cols in parts(n):
+            score = sb.tile([P, S], F32, name=f"score{n}", tag=score_tags[n % len(score_tags)], align_bytes=64)
+            pieces = {last - 1: (columns(0), columns(1)), last: LAST_PIECES}.get(n, (whole,))
+            for cols in pieces:
                 if n in SCALAR_SQUARES:
                     nc.scalar.activation(d[n][:, cols], d[n][:, cols], ACT.Square)
                 nc.scalar.activation(score[:, cols], d[n][:, cols], ACT.Exp, scale=-0.25)
-                nc.sync.dma_start(out[rows, cols], score[:, cols])
+                nc.sync.dma_start(out[P * n : P * (n + 1), cols], score[:, cols])
 
-        for step in range(tiles + 3):
-            if step < tiles:
+        for step in range(TILES + EXP_LAG):
+            if step < TILES:
                 product(step)
-            if 1 <= step <= tiles:
-                pick(step - 1)
-            if 2 <= step <= tiles + 1:
-                square(step - 2)
-            if step >= 3:
-                finish(step - 3)
+            if 0 <= step - GATHER_LAG < TILES:
+                gather(step - GATHER_LAG)
+            if 0 <= step - SQUARE_LAG < last and step - SQUARE_LAG not in SCALAR_SQUARES:
+                square_on_vector(step - SQUARE_LAG, whole)
+            if step >= EXP_LAG:
+                finish(step - EXP_LAG)

@@ -29,7 +29,7 @@ MOVED = 100
 PLOT_ROW = 12
 H_BANKS = ((0, 0), (1, 1), (0, 1), (6, 7))
 FACTOR_BANKS = ((6, 6), (7, 7), (6, 7), (2, 3))
-SCALAR_SQUARES = (5, 6)
+SCALAR_SQUARES = (4, 5, 6)
 LAST_PIECES = (slice(0, 512), slice(512, 768), slice(768, 1024))
 GATHER_LAG, SQUARE_LAG, EXP_LAG = 1, 2, 4
 
@@ -338,7 +338,7 @@ def tile_list_plot_track_scores_kernel(
                     out=bank[:], lhsT=plots[n][0].bitcast(FP8X4), lhsT_scale=plots[n][1],
                     rhs=page_codes[c][:].bitcast(FP8X4), rhs_scale=page_sc[c][:], start=True, stop=True,
                 )
-                if n == 0 and c == CHUNKS - 1:
+                if n < 2 and c == CHUNKS - 1:
                     nc.vector.tensor_copy(e[n][:, columns(c)], bank[:])
                 else:
                     nc.scalar.copy(e[n][:, columns(c)], bank[:])

@@ -29,9 +29,8 @@ MOVED = 100
 PLOT_ROW = 12
 H_BANKS = ((0, 0), (1, 1), (0, 1), (6, 7))
 FACTOR_BANKS = ((6, 6), (7, 7), (6, 7), (2, 3))
-SCALAR_SQUARES = (4, 5, 6)
-LAST_PIECES = (slice(0, 512), slice(512, 768), slice(768, 1024))
-GATHER_LAG, SQUARE_LAG, EXP_LAG = 1, 2, 4
+GPSIMD_SQUARES, VECTOR_EMPTIES = 0, 2
+LAST_PIECES = (slice(0, 640), slice(640, 896), slice(896, 1024))
 
 
 def tile_list_plot_track_scores_kernel(
@@ -325,58 +324,62 @@ def tile_list_plot_track_scores_kernel(
             gates.extend([both[:, 0, :], both[:, 1, :]])
 
         e, d = {}, {}
-        e_tags = ("win0", "win1", "win2", "tab2_win")
-        score_tags = ("h0", "h1", "h2")
         whole = slice(0, S)
         last = TILES - 1
+        e_tags = ("win0", "win1", "win0", "win2", "page0", "page1", "page2", "page3")
+        bank_sets = (0, 1, 0, 1, 1, 1, 1, 1)
+        for n, tag in enumerate(("h2", "h3", "factor2", "v_words0", "v_words1", "h0", "h1", "factor0")):
+            d[n] = sb.tile([P, S], F32, name=f"d{n}", tag=tag, align_bytes=64)[:]
 
         def product(n):
-            e[n] = sb.tile([P, T], F32, name=f"e{n}", tag=e_tags[n % len(e_tags)], align_bytes=64)
+            e[n] = sb.tile([P, T], F32, name=f"e{n}", tag=e_tags[n], align_bytes=64)
             for c in range(CHUNKS):
-                bank = psum.tile([P, BANK], F32, name=f"e{n}{c}", tag=f"bank{CHUNKS * (n % 2) + c}")
+                bank = psum.tile([P, BANK], F32, name=f"e{n}{c}", tag=f"bank{CHUNKS * bank_sets[n] + c}")
                 nc.tensor.matmul_mx(
                     out=bank[:], lhsT=plots[n][0].bitcast(FP8X4), lhsT_scale=plots[n][1],
                     rhs=page_codes[c][:].bitcast(FP8X4), rhs_scale=page_sc[c][:], start=True, stop=True,
                 )
-                if n < 2 and c == CHUNKS - 1:
+                if n == VECTOR_EMPTIES or (n, c) == (0, CHUNKS - 1):
                     nc.vector.tensor_copy(e[n][:, columns(c)], bank[:])
                 else:
                     nc.scalar.copy(e[n][:, columns(c)], bank[:])
 
-        def pick(n, cols):
+        def pick(n, cols=whole):
             nc.vector.tensor_tensor(d[n][:, cols], e[n][:].indirect(entries(idx4, cols)), gates[n][:, cols], ALU.subtract)
 
-        def square_on_vector(n, cols):
-            nc.vector.tensor_tensor(d[n][:, cols], d[n][:, cols], d[n][:, cols], ALU.mult)
+        def multiply(engine, n, cols=whole):
+            engine.tensor_tensor(d[n][:, cols], d[n][:, cols], d[n][:, cols], ALU.mult)
 
-        def gather(n):
-            d[n] = sb.tile([P, S], F32, name=f"d{n}", tag=f"page{n % PACK}", align_bytes=64)
-            if n < last:
-                pick(n, whole)
-            else:
-                first, second, third = LAST_PIECES
-                pick(n, first)
-                pick(n, second)
-                square_on_vector(n, first)
-                pick(n, third)
-                square_on_vector(n, second)
-                square_on_vector(n, third)
+        def square(n, cols=whole):
+            nc.scalar.activation(d[n][:, cols], d[n][:, cols], ACT.Square)
 
-        def finish(n):
-            score = sb.tile([P, S], F32, name=f"score{n}", tag=score_tags[n % len(score_tags)], align_bytes=64)
-            pieces = {last - 1: (columns(0), columns(1)), last: LAST_PIECES}.get(n, (whole,))
-            for cols in pieces:
-                if n in SCALAR_SQUARES:
-                    nc.scalar.activation(d[n][:, cols], d[n][:, cols], ACT.Square)
-                nc.scalar.activation(score[:, cols], d[n][:, cols], ACT.Exp, scale=-0.25)
-                nc.sync.dma_start(out[P * n : P * (n + 1), cols], score[:, cols])
+        def finish(n, cols=whole):
+            nc.scalar.activation(d[n][:, cols], d[n][:, cols], ACT.Exp, scale=-0.25)
+            nc.sync.dma_start(out[P * n : P * (n + 1), cols], d[n][:, cols])
 
-        for step in range(TILES + EXP_LAG):
-            if step < TILES:
-                product(step)
-            if 0 <= step - GATHER_LAG < TILES:
-                gather(step - GATHER_LAG)
-            if 0 <= step - SQUARE_LAG < last and step - SQUARE_LAG not in SCALAR_SQUARES:
-                square_on_vector(step - SQUARE_LAG, whole)
-            if step >= EXP_LAG:
-                finish(step - EXP_LAG)
+        for n in range(TILES):
+            product(n)
+            if n == 1:
+                pick(GPSIMD_SQUARES)
+                multiply(nc.gpsimd, GPSIMD_SQUARES)
+        for n in range(1, last):
+            pick(n)
+            if n == 2:
+                multiply(nc.vector, 1)
+        finish(0)
+        for n in range(2, last - 1):
+            square(n)
+            finish(n - 1)
+        finish(last - 2)
+        first, second, third = LAST_PIECES
+        pick(last, first)
+        multiply(nc.vector, last - 1)
+        multiply(nc.vector, last, first)
+        pick(last, second)
+        pick(last, third)
+        multiply(nc.vector, last, second)
+        multiply(nc.vector, last, third)
+        for c in range(2):
+            finish(last - 1, columns(c))
+        for cols in LAST_PIECES:
+            finish(last, cols)

@@ -25,7 +25,6 @@ CHUNKS = T // BANK
 TILES = S // P
 QUADS = (0, 2, 1, 3)
 ORDER = (2, 0, 1, 3)
-MOVED = 100
 PLOT_ROW = 12
 H_BANKS = ((0, 0), (1, 1), (0, 1), (6, 7))
 FACTOR_BANKS = ((6, 6), (7, 7), (6, 7), (2, 3))
@@ -67,13 +66,13 @@ def tile_list_plot_track_scores_kernel(
         tab2_sc = sb.tile([P, T], U8, name="tab2_sc", align_bytes=64)
         moved = {a: sb.tile([P, S], U8, name=f"moved{a}", align_bytes=64) for a in range(1, PASSES)}
         ident = sb.tile([P, P], F32, name="ident", align_bytes=64)
-        nc.gpsimd.memset(tab2_sc[:].bitcast(I32), 0)
-        load_scale_rows(nc.gpsimd, tab2_sc, tab2_scales, PLOT_ROW)
+        nc.gpsimd.memset(w4_sc_raw[:].bitcast(I32), 0)
+        load_scale_rows(nc.gpsimd, w4_sc_raw, w4_scales, 0)
         make_identity(nc, ident[:])
         nc.vector.memset(tab_sc[:].bitcast(I32), 0)
-        nc.vector.memset(w4_sc_raw[:].bitcast(I32), 0)
+        nc.vector.memset(tab2_sc[:].bitcast(I32), 0)
         for dst in moved.values():
-            nc.vector.memset(dst[:].bitcast(I32)[96:P], 0)
+            nc.vector.memset(dst[:].bitcast(I32), 0)
 
         def load_words(a):
             win = sb.tile([P, T], I32, name=f"tab_win{a}", tag=f"win{a}", align_bytes=64)
@@ -101,7 +100,7 @@ def tile_list_plot_track_scores_kernel(
         w4_raw = sb.tile([P, PASSES, 2 * H], U8, name="w4_raw", align_bytes=64)
         nc.sync.dma_start(w4_raw[:].bitcast(I32), w4_words.bitcast(I32).rearrange("a p c -> p a c"))
         w1_raw.append(load_w1(1))
-        load_scale_rows(nc.sync, w4_sc_raw, w4_scales, 0)
+        load_scale_rows(nc.sync, tab2_sc, tab2_scales, PLOT_ROW)
         idx2 = load_list(offs2, "idx2")
         tab_win.append(load_words(2))
 
@@ -118,8 +117,11 @@ def tile_list_plot_track_scores_kernel(
         v_sc = sb.tile([P, S], U8, name="v_sc", align_bytes=64)
         nc.vector.tensor_copy(v_sc[:], tab_sc[:].indirect(idx[:]))
         for a in moved:
-            nc.sync.dma_start(moved[a][0:MOVED, :].bitcast(I32), v_sc[4 * a : 4 * a + MOVED, :].bitcast(I32))
-        w1_raw.append(load_w1(2))
+            for q in QUADS:
+                nc.sync.dma_start(moved[a][32 * q : 32 * q + 4, :].bitcast(I32),
+                                  v_sc[32 * q + 4 * a : 32 * q + 4 * a + 4, :].bitcast(I32))
+            if a == 1:
+                w1_raw.append(load_w1(2))
         idx3 = load_list(offs3, "idx3")
 
         page_rows = page0.rearrange("(p i) t -> p i t", i=PACK)
@@ -156,13 +158,13 @@ def tile_list_plot_track_scores_kernel(
                 w1_sc[a, i] = scales[:, P * (i - lo) : P * (i - lo + 1)]
 
         w4_codes = sb.tile([P, PASSES, 2 * H], U8, name="w4_codes", align_bytes=64)
-        nc.vector.tensor_copy(
+        nc.scalar.copy(
             w4_codes[:].bitcast(U16).rearrange("p a (i m) -> p i a m", i=PACK),
             w4_raw[:].bitcast(U16).rearrange("p a (m i) -> p i a m", i=PACK),
         )
         quantise_w1(0, 0, PACK, round_on_scalar)
         w4_sc = sb.tile([P, PASSES, H], U8, name="w4_sc", align_bytes=64)
-        nc.vector.tensor_copy(
+        nc.gpsimd.tensor_copy(
             w4_sc[:].rearrange("p a (i m) -> p i a m", i=PACK),
             w4_sc_raw[:].rearrange("p (a m i) -> p i a m", a=PASSES, i=PACK),
         )

@@ -26,6 +26,7 @@ TILES = S // P
 QUADS = (0, 2, 1, 3)
 ORDER = (2, 0, 1, 3)
 PLOT_ROW = 12
+SC_ROW = (0, 16, 64)
 H_BANKS = ((0, 0), (1, 1), (0, 1), (6, 7))
 FACTOR_BANKS = ((6, 6), (7, 7), (6, 7), (2, 3))
 GPSIMD_SQUARES, VECTOR_EMPTIES = 0, 2
@@ -64,14 +65,15 @@ def tile_list_plot_track_scores_kernel(
         tab_sc = sb.tile([P, T], U8, name="tab_sc", align_bytes=64)
         w4_sc_raw = sb.tile([P, PASSES * H], U8, name="w4_sc_raw", align_bytes=64)
         tab2_sc = sb.tile([P, T], U8, name="tab2_sc", align_bytes=64)
-        moved = {a: sb.tile([P, S], U8, name=f"moved{a}", align_bytes=64) for a in range(1, PASSES)}
+        moved = {a: sb.tile([P, S], U8, name=f"moved{a}", align_bytes=64) for a in range(PASSES)}
+        plot_planes = sb.tile([P, S], U8, name="plot_planes", align_bytes=64)
         ident = sb.tile([P, P], F32, name="ident", align_bytes=64)
         nc.gpsimd.memset(w4_sc_raw[:].bitcast(I32), 0)
         load_scale_rows(nc.gpsimd, w4_sc_raw, w4_scales, 0)
         make_identity(nc, ident[:])
         nc.vector.memset(tab_sc[:].bitcast(I32), 0)
         nc.vector.memset(tab2_sc[:].bitcast(I32), 0)
-        for dst in moved.values():
+        for dst in (*moved.values(), plot_planes):
             nc.vector.memset(dst[:].bitcast(I32), 0)
 
         def load_words(a):
@@ -91,18 +93,17 @@ def tile_list_plot_track_scores_kernel(
 
         tab_win = [load_words(0)]
         idx = load_list(offs, "idx")
+        sc_rows = tab_scales.bitcast(I32).rearrange("a q c -> (a q) c")
+        nc.sync.dma_start(tab_sc[:].bitcast(I32)[0:32, :], sc_rows[0:32, :])
+        nc.sync.dma_start(tab_sc[:].bitcast(I32)[SC_ROW[2] : SC_ROW[2] + 16, :], sc_rows[32:48, :])
         tab_win.append(load_words(1))
-        for q in QUADS:
-            nc.sync.dma_start(tab_sc[:].bitcast(I32)[32 * q : 32 * q + 4 * PASSES, :],
-                              tab_scales.bitcast(I32)[:, 4 * q : 4 * q + 4, :])
         w1_raw = [load_w1(0)]
         wgs_sb = [load_wgs(0)]
         w4_raw = sb.tile([P, PASSES, 2 * H], U8, name="w4_raw", align_bytes=64)
         nc.sync.dma_start(w4_raw[:].bitcast(I32), w4_words.bitcast(I32).rearrange("a p c -> p a c"))
         w1_raw.append(load_w1(1))
-        load_scale_rows(nc.sync, tab2_sc, tab2_scales, PLOT_ROW)
+        nc.sync.dma_start(tab2_sc[:].bitcast(I32)[0:16, :], tab2_scales.bitcast(I32)[0])
         idx2 = load_list(offs2, "idx2")
-        tab_win.append(load_words(2))
 
         v_words = {}
 
@@ -113,15 +114,20 @@ def tile_list_plot_track_scores_kernel(
                 v_words[a, c] = words[:, c * BANK - lo : (c + 1) * BANK - lo]
 
         pick_words(0, 0, S, "v_words0")
-        pick_words(1, 0, S, "v_words1")
         v_sc = sb.tile([P, S], U8, name="v_sc", align_bytes=64)
         nc.vector.tensor_copy(v_sc[:], tab_sc[:].indirect(idx[:]))
-        for a in moved:
+        pick_words(1, 0, S, "v_words1")
+
+        def move_rows(dst, dst_row, src, src_row):
             for q in QUADS:
-                nc.sync.dma_start(moved[a][32 * q : 32 * q + 4, :].bitcast(I32),
-                                  v_sc[32 * q + 4 * a : 32 * q + 4 * a + 4, :].bitcast(I32))
-            if a == 1:
-                w1_raw.append(load_w1(2))
+                nc.sync.dma_start(dst[32 * q + dst_row : 32 * q + dst_row + 4, :].bitcast(I32),
+                                  src[src_row + 4 * q : src_row + 4 * q + 4, :].bitcast(I32))
+
+        move_rows(moved[0], 0, v_sc, SC_ROW[0])
+        tab_win.append(load_words(2))
+        move_rows(moved[1], 0, v_sc, SC_ROW[1])
+        w1_raw.append(load_w1(2))
+        move_rows(moved[2], 0, v_sc, SC_ROW[2])
         idx3 = load_list(offs3, "idx3")
 
         page_rows = page0.rearrange("(p i) t -> p i t", i=PACK)
@@ -168,19 +174,12 @@ def tile_list_plot_track_scores_kernel(
             w4_sc[:].rearrange("p a (i m) -> p i a m", i=PACK),
             w4_sc_raw[:].rearrange("p (a m i) -> p i a m", a=PASSES, i=PACK),
         )
-        plot_sc = []
-
-        def pick_plot_scales(c, tag):
-            scales = sb.tile([P, BANK], U8, name=f"v2_sc{c}", tag=tag, align_bytes=64)
-            nc.vector.tensor_copy(scales[:], tab2_sc[:].indirect(entries(idx2, columns(c))))
-            plot_sc.append(scales)
-
-        pick_plot_scales(0, "v2_sc0")
+        v2_sc = sb.tile([P, S], U8, name="v2_sc", align_bytes=64)
+        nc.vector.tensor_copy(v2_sc[:], tab2_sc[:].indirect(idx2[:]))
         quantise_w1(1, 0, PACK, round_on_scalar)
         pick_words(2, 0, BANK, "v_words2a")
         pick_words(2, BANK, S, "v_words2b")
         quantise_w1(2, 2, PACK, round_on_vector)
-        pick_plot_scales(1, "w1_bf2_2")
         quantise_w1(2, 0, 2, round_on_scalar)
 
         turned = {}
@@ -215,14 +214,12 @@ def tile_list_plot_track_scores_kernel(
                 if weight == "w4":
                     lhsT = w4_codes[:, a, 2 * P * i : 2 * P * (i + 1)].bitcast(FP4X4)
                     lhsT_sc = w4_sc[:, a, P * i : P * (i + 1)]
-                    rhs_sc = moved[a][:, columns(c)] if a else v_sc[:, columns(c)]
                 else:
                     lhsT = w1_codes[a, i].bitcast(FP8X4)
                     lhsT_sc = w1_sc[a, i]
-                    rhs_sc = v_sc[4 * a : P, columns(c)]
                 nc.tensor.matmul_mx(
                     out=acc[i, c][:], lhsT=lhsT, lhsT_scale=lhsT_sc,
-                    rhs=v_words[a, c].bitcast(FP8X4), rhs_scale=rhs_sc,
+                    rhs=v_words[a, c].bitcast(FP8X4), rhs_scale=moved[a][:, columns(c)],
                     start=(k == 0), stop=(k == len(passes) - 1),
                 )
 
@@ -279,6 +276,7 @@ def tile_list_plot_track_scores_kernel(
             replace(pos)
             round_slice(pos)
 
+        move_rows(plot_planes, PLOT_ROW, v2_sc, 0)
         plots = {}
 
         def pick_plots(c, tag):
@@ -286,7 +284,7 @@ def tile_list_plot_track_scores_kernel(
             nc.vector.tensor_copy(words[:], tab2_win[:].bitcast(U32).indirect(entries(idx2, columns(c))))
             for u in range(BANK // P):
                 cols = slice(P * u, P * (u + 1))
-                plots[c * BANK // P + u] = (words[:, cols], plot_sc[c][PLOT_ROW:P, cols])
+                plots[c * BANK // P + u] = (words[:, cols], plot_planes[PLOT_ROW:P, BANK * c + P * u : BANK * c + P * (u + 1)])
 
         pick_plots(0, "factor3")
 

@@ -27,8 +27,8 @@ QUADS = (0, 2, 1, 3)
 ORDER = (2, 0, 1, 3)
 PLOT_ROW = 12
 SC_ROW = (0, 16, 64)
-H_BANKS = ((0, 0), (1, 1), (0, 1), (6, 7))
-FACTOR_BANKS = ((6, 6), (7, 7), (6, 7), (2, 3))
+H_BANKS = ((0, 0), (1, 1), (6, 5), (0, 1))
+FACTOR_BANKS = ((6, 6), (7, 7))
 GPSIMD_SQUARES, VECTOR_EMPTIES = 0, 2
 LAST_PIECES = (slice(0, 640), slice(640, 896), slice(896, 1024))
 
@@ -86,6 +86,11 @@ def tile_list_plot_track_scores_kernel(
             nc.sync.dma_start(raw[:], w1[512 * a : 512 * (a + 1), :].rearrange("(p j) c -> p j c", j=PACK))
             return raw
 
+        def load_w4(lo, hi):
+            raw = sb.tile([P, hi - lo, 2 * H], U8, name=f"w4_raw{lo}", align_bytes=64)
+            nc.sync.dma_start(raw[:].bitcast(I32), w4_words.bitcast(I32)[lo:hi].rearrange("a p c -> p a c"))
+            return raw
+
         def load_wgs(b):
             part = sb.tile([P, BANK], F32, name=f"wgs{b}", align_bytes=64)
             nc.sync.dma_start(part[:], wgs[:, columns(b)])
@@ -99,8 +104,7 @@ def tile_list_plot_track_scores_kernel(
         tab_win.append(load_words(1))
         w1_raw = [load_w1(0)]
         wgs_sb = [load_wgs(0)]
-        w4_raw = sb.tile([P, PASSES, 2 * H], U8, name="w4_raw", align_bytes=64)
-        nc.sync.dma_start(w4_raw[:].bitcast(I32), w4_words.bitcast(I32).rearrange("a p c -> p a c"))
+        w4_raw = [load_w4(0, PASSES - 1)]
         w1_raw.append(load_w1(1))
         nc.sync.dma_start(tab2_sc[:].bitcast(I32)[0:16, :], tab2_scales.bitcast(I32)[0])
         idx2 = load_list(offs2, "idx2")
@@ -127,13 +131,18 @@ def tile_list_plot_track_scores_kernel(
         tab_win.append(load_words(2))
         move_rows(moved[1], 0, v_sc, SC_ROW[1])
         w1_raw.append(load_w1(2))
+        w4_raw.append(load_w4(PASSES - 1, PASSES))
         move_rows(moved[2], 0, v_sc, SC_ROW[2])
         idx3 = load_list(offs3, "idx3")
 
         page_rows = page0.rearrange("(p i) t -> p i t", i=PACK)
         page = [sb.tile([P, T], F32, name=f"page{i}", align_bytes=64) for i in range(PACK)]
         tab2_win = sb.tile([P, T], I32, name="tab2_win", align_bytes=64)
+        factor = {ORDER[pos]: sb.tile([P, S], F32, name=f"factor{pos}", align_bytes=64) for pos in range(PACK)}
         for i in ORDER:
+            if i in ORDER[2:]:
+                for q in QUADS:
+                    nc.sync.dma_start(factor[i][32 * q : 32 * (q + 1), :], wgs[i:P:PACK, :])
             if i == ORDER[-1]:
                 nc.sync.dma_start(tab2_win[:], tab2_words[0].rearrange("p t i -> p (t i)").bitcast(I32))
             nc.sync.dma_start(page[i][:], page_rows[:, i, :])
@@ -149,7 +158,7 @@ def tile_list_plot_track_scores_kernel(
         def round_on_vector(dst, src):
             nc.vector.tensor_scalar_mul(dst, src, -1.0)
 
-        def quantise_w1(a, lo, hi, negate_and_round):
+        def quantise_w1(a, lo, hi, negate_and_round, between=None):
             n = hi - lo
             grouped = sb.tile([P, n * P * PACK], BF16, name=f"w1_bf{a}_{lo}", align_bytes=64)
             codes = sb.tile([P, n * P], U32, name=f"w1_codes{a}_{lo}", align_bytes=64)
@@ -158,16 +167,26 @@ def tile_list_plot_track_scores_kernel(
                 grouped[:].rearrange("p (i m j) -> p m j i", i=n, j=PACK),
                 w1_raw[a][:].rearrange("p j (m i) -> p m j i", i=PACK)[:, :, :, lo:hi],
             )
+            if between:
+                between()
             nc.vector.quantize_mx(out=codes[:].bitcast(FP8X4), scales=scales[:], in_=grouped[:])
             for i in range(lo, hi):
                 w1_codes[a, i] = codes[:, P * (i - lo) : P * (i - lo + 1)]
                 w1_sc[a, i] = scales[:, P * (i - lo) : P * (i - lo + 1)]
 
-        w4_codes = sb.tile([P, PASSES, 2 * H], U8, name="w4_codes", align_bytes=64)
-        nc.scalar.copy(
-            w4_codes[:].bitcast(U16).rearrange("p a (i m) -> p i a m", i=PACK),
-            w4_raw[:].bitcast(U16).rearrange("p a (m i) -> p i a m", i=PACK),
-        )
+        w4_codes = {}
+
+        def deal_w4(copy, raw, first):
+            n = raw.shape[1]
+            dealt = sb.tile([P, n, 2 * H], U8, name=f"w4_codes{first}", align_bytes=64)
+            copy(
+                dealt[:].bitcast(U16).rearrange("p a (i m) -> p i a m", i=PACK),
+                raw[:].bitcast(U16).rearrange("p a (m i) -> p i a m", i=PACK),
+            )
+            for a in range(n):
+                w4_codes[first + a] = dealt[:, a, :]
+
+        deal_w4(nc.scalar.copy, w4_raw[0], 0)
         quantise_w1(0, 0, PACK, round_on_scalar)
         w4_sc = sb.tile([P, PASSES, H], U8, name="w4_sc", align_bytes=64)
         nc.gpsimd.tensor_copy(
@@ -178,12 +197,11 @@ def tile_list_plot_track_scores_kernel(
         nc.vector.tensor_copy(v2_sc[:], tab2_sc[:].indirect(idx2[:]))
         quantise_w1(1, 0, PACK, round_on_scalar)
         pick_words(2, 0, BANK, "v_words2a")
-        pick_words(2, BANK, S, "v_words2b")
-        quantise_w1(2, 2, PACK, round_on_vector)
+        quantise_w1(2, 2, PACK, round_on_vector, lambda: deal_w4(nc.vector.tensor_copy, w4_raw[1], PASSES - 1))
         quantise_w1(2, 0, 2, round_on_scalar)
+        pick_words(2, BANK, S, "w1_bf2_2")
 
         turned = {}
-        factor = {ORDER[pos]: sb.tile([P, S], F32, name=f"factor{pos}", align_bytes=64) for pos in range(PACK)}
 
         def turn(b):
             turned[b] = psum.tile([P, PACK, P], F32, name=f"turned{b}", tag=f"bank{4 + b}")
@@ -212,7 +230,7 @@ def tile_list_plot_track_scores_kernel(
             acc[i, c] = psum.tile([P, BANK], F32, name=f"acc{i}{c}", tag=f"bank{H_BANKS[pos][c]}")
             for k, (weight, a) in enumerate(passes):
                 if weight == "w4":
-                    lhsT = w4_codes[:, a, 2 * P * i : 2 * P * (i + 1)].bitcast(FP4X4)
+                    lhsT = w4_codes[a][:, 2 * P * i : 2 * P * (i + 1)].bitcast(FP4X4)
                     lhsT_sc = w4_sc[:, a, P * i : P * (i + 1)]
                 else:
                     lhsT = w1_codes[a, i].bitcast(FP8X4)
@@ -228,9 +246,9 @@ def tile_list_plot_track_scores_kernel(
             h[i, c] = sb.tile([P, BANK], F32, name=f"h{i}_{c}", tag=tag, align_bytes=64)
             nc.scalar.activation(h[i, c][:], acc[i, c][:], ACT.Abs)
 
-        def magnitude(pos):
+        def magnitude(pos, tag):
             i = ORDER[pos]
-            h[i] = sb.tile([P, S], F32, name=f"h{i}_all", tag=f"h{pos}", align_bytes=64)
+            h[i] = sb.tile([P, S], F32, name=f"h{i}_all", tag=tag, align_bytes=64)
             for c in range(2):
                 nc.scalar.activation(h[i][:, columns(c)], acc[i, c][:], ACT.Abs)
 
@@ -255,63 +273,73 @@ def tile_list_plot_track_scores_kernel(
             magnitude_half(pos, 1, f"h{pos}")
         replace_half(0, 1)
         for pos in range(2, PACK):
-            for b in range(2):
-                deal_factor(pos, b, spread_tags[b])
             for c in range(2):
                 difference(pos, c)
-            magnitude(pos)
+            if pos < PACK - 1:
+                magnitude(pos, f"h{pos}")
 
-        pair_tags = ("v_words2b", "v_words2a", "v_words1", "v_words0")
-        pairs = [sb.tile([P, 2, BANK, 2], BF16, name=f"pairs{c}", tag=pair_tags[c], align_bytes=64) for c in range(CHUNKS)]
+        woven = {0: sb.tile([P, BANK, PACK], BF16, name="woven0", tag="w1_bf2_2", align_bytes=64)}
+        pairs = {
+            c: sb.tile([P, 2, BANK, 2], BF16, name=f"pairs{c}", tag=tag, align_bytes=64)
+            for c, tag in ((1, "v_words2a"), (2, "v_words1"), (3, "v_words0"))
+        }
 
-        def round_slice(pos):
+        def round_first_chunk(copy, pos):
             i = ORDER[pos]
-            for c in range(CHUNKS):
+            copy(woven[0][:, :, i], page[i][:, columns(0)])
+
+        def round_into_pairs(pos):
+            i = ORDER[pos]
+            for c in pairs:
                 nc.scalar.copy(pairs[c][:, i // 2, :, i % 2], page[i][:, columns(c)])
 
-        round_slice(0)
-        replace_half(1, 1)
-        round_slice(1)
-        for pos in range(2, PACK):
-            replace(pos)
-            round_slice(pos)
+        for pos in range(PACK):
+            if pos == 1:
+                replace_half(1, 1)
+            elif pos > 1:
+                replace(pos)
+            round_first_chunk(nc.scalar.copy if pos < PACK - 1 else nc.vector.tensor_copy, pos)
+            round_into_pairs(pos)
+            if pos == 0:
+                magnitude(PACK - 1, "h3")
 
         move_rows(plot_planes, PLOT_ROW, v2_sc, 0)
         plots = {}
 
-        def pick_plots(c, tag):
-            words = sb.tile([P, BANK], U32, name=f"v2_words{c * BANK}", tag=tag, align_bytes=64)
-            nc.vector.tensor_copy(words[:], tab2_win[:].bitcast(U32).indirect(entries(idx2, columns(c))))
-            for u in range(BANK // P):
-                cols = slice(P * u, P * (u + 1))
-                plots[c * BANK // P + u] = (words[:, cols], plot_planes[PLOT_ROW:P, BANK * c + P * u : BANK * c + P * (u + 1)])
+        def pick_plots(lo, hi, tag):
+            words = sb.tile([P, P * (hi - lo)], U32, name=f"v2_words{lo}", tag=tag, align_bytes=64)
+            nc.vector.tensor_copy(words[:], tab2_win[:].bitcast(U32).indirect(entries(idx2, slice(P * lo, P * hi))))
+            for n in range(lo, hi):
+                plots[n] = (words[:, P * (n - lo) : P * (n - lo + 1)], plot_planes[PLOT_ROW:P, P * n : P * (n + 1)])
 
-        pick_plots(0, "factor3")
+        pick_plots(0, 2, "factor3")
 
-        woven, page_codes, page_sc = [], [], []
-        woven_tags = ("h0", "h1", "factor0", "factor1")
+        page_codes, page_sc = [], []
+        woven_tags = {1: "h1", 2: "factor0", 3: "factor1"}
 
         def interleave(c):
-            both = sb.tile([P, BANK * PACK], BF16, name=f"woven{c}", tag=woven_tags[c], align_bytes=64)
+            woven[c] = sb.tile([P, BANK, PACK], BF16, name=f"woven{c}", tag=woven_tags[c], align_bytes=64)
             nc.vector.tensor_copy(
-                both[:].bitcast(I32).rearrange("p (t u) -> p t u", u=2),
+                woven[c][:].rearrange("p t i -> p (t i)").bitcast(I32).rearrange("p (t u) -> p t u", u=2),
                 pairs[c][:].rearrange("p u t e -> p (u t e)").bitcast(I32).rearrange("p (u t) -> p t u", u=2),
             )
-            woven.append(both)
 
         def quantise_page(c):
             codes = sb.tile([P, BANK], U32, name=f"page_codes{c}", align_bytes=64)
             scales = sb.tile([P, BANK], U8, name=f"page_sc{c}", align_bytes=64)
-            nc.vector.quantize_mx(out=codes[:].bitcast(FP8X4), scales=scales[:], in_=woven[c][:])
+            nc.vector.quantize_mx(out=codes[:].bitcast(FP8X4), scales=scales[:],
+                                  in_=woven[c][:].rearrange("p t i -> p (t i)"))
             page_codes.append(codes)
             page_sc.append(scales)
 
-        for step in range(CHUNKS + 1):
-            if step < CHUNKS:
-                interleave(step)
-            if step >= 1:
-                quantise_page(step - 1)
-        pick_plots(1, woven_tags[-1])
+        interleave(1)
+        quantise_page(0)
+        quantise_page(1)
+        interleave(2)
+        interleave(3)
+        quantise_page(2)
+        quantise_page(3)
+        pick_plots(2, TILES, woven_tags[3])
 
         gates = []
         for n in range(2):
@@ -339,7 +367,7 @@ def tile_list_plot_track_scores_kernel(
                     out=bank[:], lhsT=plots[n][0].bitcast(FP8X4), lhsT_scale=plots[n][1],
                     rhs=page_codes[c][:].bitcast(FP8X4), rhs_scale=page_sc[c][:], start=True, stop=True,
                 )
-                if n == VECTOR_EMPTIES or (n, c) == (0, CHUNKS - 1):
+                if n == VECTOR_EMPTIES:
                     nc.vector.tensor_copy(e[n][:, columns(c)], bank[:])
                 else:
                     nc.scalar.copy(e[n][:, columns(c)], bank[:])
@@ -367,10 +395,14 @@ def tile_list_plot_track_scores_kernel(
             if n == 2:
                 multiply(nc.vector, 1)
         finish(0)
-        for n in range(2, last - 1):
+        for n in range(2, last - 2):
             square(n)
             finish(n - 1)
-        finish(last - 2)
+        finish(last - 3)
+        for c in range(2):
+            square(last - 2, columns(c))
+        for c in range(2):
+            finish(last - 2, columns(c))
         first, second, third = LAST_PIECES
         pick(last, first)
         multiply(nc.vector, last - 1)

@@ -86,11 +86,6 @@ def tile_list_plot_track_scores_kernel(
             nc.sync.dma_start(raw[:], w1[512 * a : 512 * (a + 1), :].rearrange("(p j) c -> p j c", j=PACK))
             return raw
 
-        def load_w4(lo, hi):
-            raw = sb.tile([P, hi - lo, 2 * H], U8, name=f"w4_raw{lo}", align_bytes=64)
-            nc.sync.dma_start(raw[:].bitcast(I32), w4_words.bitcast(I32)[lo:hi].rearrange("a p c -> p a c"))
-            return raw
-
         def load_wgs(b):
             part = sb.tile([P, BANK], F32, name=f"wgs{b}", align_bytes=64)
             nc.sync.dma_start(part[:], wgs[:, columns(b)])
@@ -104,7 +99,8 @@ def tile_list_plot_track_scores_kernel(
         tab_win.append(load_words(1))
         w1_raw = [load_w1(0)]
         wgs_sb = [load_wgs(0)]
-        w4_raw = [load_w4(0, PASSES - 1)]
+        w4_raw = sb.tile([P, PASSES, 2 * H], U8, name="w4_raw", align_bytes=64)
+        nc.sync.dma_start(w4_raw[:].bitcast(I32), w4_words.bitcast(I32).rearrange("a p c -> p a c"))
         w1_raw.append(load_w1(1))
         nc.sync.dma_start(tab2_sc[:].bitcast(I32)[0:16, :], tab2_scales.bitcast(I32)[0])
         idx2 = load_list(offs2, "idx2")
@@ -131,7 +127,6 @@ def tile_list_plot_track_scores_kernel(
         tab_win.append(load_words(2))
         move_rows(moved[1], 0, v_sc, SC_ROW[1])
         w1_raw.append(load_w1(2))
-        w4_raw.append(load_w4(PASSES - 1, PASSES))
         move_rows(moved[2], 0, v_sc, SC_ROW[2])
         idx3 = load_list(offs3, "idx3")
 
@@ -158,7 +153,7 @@ def tile_list_plot_track_scores_kernel(
         def round_on_vector(dst, src):
             nc.vector.tensor_scalar_mul(dst, src, -1.0)
 
-        def quantise_w1(a, lo, hi, negate_and_round, between=None):
+        def quantise_w1(a, lo, hi, negate_and_round):
             n = hi - lo
             grouped = sb.tile([P, n * P * PACK], BF16, name=f"w1_bf{a}_{lo}", align_bytes=64)
             codes = sb.tile([P, n * P], U32, name=f"w1_codes{a}_{lo}", align_bytes=64)
@@ -167,26 +162,16 @@ def tile_list_plot_track_scores_kernel(
                 grouped[:].rearrange("p (i m j) -> p m j i", i=n, j=PACK),
                 w1_raw[a][:].rearrange("p j (m i) -> p m j i", i=PACK)[:, :, :, lo:hi],
             )
-            if between:
-                between()
             nc.vector.quantize_mx(out=codes[:].bitcast(FP8X4), scales=scales[:], in_=grouped[:])
             for i in range(lo, hi):
                 w1_codes[a, i] = codes[:, P * (i - lo) : P * (i - lo + 1)]
                 w1_sc[a, i] = scales[:, P * (i - lo) : P * (i - lo + 1)]
 
-        w4_codes = {}
-
-        def deal_w4(copy, raw, first):
-            n = raw.shape[1]
-            dealt = sb.tile([P, n, 2 * H], U8, name=f"w4_codes{first}", align_bytes=64)
-            copy(
-                dealt[:].bitcast(U16).rearrange("p a (i m) -> p i a m", i=PACK),
-                raw[:].bitcast(U16).rearrange("p a (m i) -> p i a m", i=PACK),
-            )
-            for a in range(n):
-                w4_codes[first + a] = dealt[:, a, :]
-
-        deal_w4(nc.scalar.copy, w4_raw[0], 0)
+        w4_codes = sb.tile([P, PASSES, 2 * H], U8, name="w4_codes", align_bytes=64)
+        nc.scalar.copy(
+            w4_codes[:].bitcast(U16).rearrange("p a (i m) -> p i a m", i=PACK),
+            w4_raw[:].bitcast(U16).rearrange("p a (m i) -> p i a m", i=PACK),
+        )
         quantise_w1(0, 0, PACK, round_on_scalar)
         w4_sc = sb.tile([P, PASSES, H], U8, name="w4_sc", align_bytes=64)
         nc.gpsimd.tensor_copy(
@@ -197,9 +182,9 @@ def tile_list_plot_track_scores_kernel(
         nc.vector.tensor_copy(v2_sc[:], tab2_sc[:].indirect(idx2[:]))
         quantise_w1(1, 0, PACK, round_on_scalar)
         pick_words(2, 0, BANK, "v_words2a")
-        quantise_w1(2, 2, PACK, round_on_vector, lambda: deal_w4(nc.vector.tensor_copy, w4_raw[1], PASSES - 1))
+        pick_words(2, BANK, S, "v_words2b")
+        quantise_w1(2, 2, PACK, round_on_vector)
         quantise_w1(2, 0, 2, round_on_scalar)
-        pick_words(2, BANK, S, "w1_bf2_2")
 
         turned = {}
 
@@ -230,7 +215,7 @@ def tile_list_plot_track_scores_kernel(
             acc[i, c] = psum.tile([P, BANK], F32, name=f"acc{i}{c}", tag=f"bank{H_BANKS[pos][c]}")
             for k, (weight, a) in enumerate(passes):
                 if weight == "w4":
-                    lhsT = w4_codes[a][:, 2 * P * i : 2 * P * (i + 1)].bitcast(FP4X4)
+                    lhsT = w4_codes[:, a, 2 * P * i : 2 * P * (i + 1)].bitcast(FP4X4)
                     lhsT_sc = w4_sc[:, a, P * i : P * (i + 1)]
                 else:
                     lhsT = w1_codes[a, i].bitcast(FP8X4)
@@ -278,10 +263,10 @@ def tile_list_plot_track_scores_kernel(
             if pos < PACK - 1:
                 magnitude(pos, f"h{pos}")
 
-        woven = {0: sb.tile([P, BANK, PACK], BF16, name="woven0", tag="w1_bf2_2", align_bytes=64)}
+        woven = {0: sb.tile([P, BANK, PACK], BF16, name="woven0", tag="w1_codes2_0", align_bytes=64)}
         pairs = {
             c: sb.tile([P, 2, BANK, 2], BF16, name=f"pairs{c}", tag=tag, align_bytes=64)
-            for c, tag in ((1, "v_words2a"), (2, "v_words1"), (3, "v_words0"))
+            for c, tag in ((1, "w1_sc2_0"), (2, "v_words1"), (3, "v_words0"))
         }
 
         def round_first_chunk(copy, pos):

@@ -27,8 +27,8 @@ QUADS = (0, 2, 1, 3)
 ORDER = (2, 0, 1, 3)
 PLOT_ROW = 12
 SC_ROW = (0, 16, 64)
-H_BANKS = ((0, 0), (1, 1), (6, 5), (0, 1))
-FACTOR_BANKS = ((6, 6), (7, 7))
+H_BANKS = ((0, 0), (1, 1), (0, 1), (6, 7))
+FACTOR_BANKS = ((6, 6), (7, 7), (6, 7))
 GPSIMD_SQUARES, VECTOR_EMPTIES = 0, 2
 LAST_PIECES = (slice(0, 640), slice(640, 896), slice(896, 1024))
 
@@ -86,6 +86,11 @@ def tile_list_plot_track_scores_kernel(
             nc.sync.dma_start(raw[:], w1[512 * a : 512 * (a + 1), :].rearrange("(p j) c -> p j c", j=PACK))
             return raw
 
+        def load_w4(lo, hi):
+            raw = sb.tile([P, hi - lo, 2 * H], U8, name=f"w4_raw{lo}", align_bytes=64)
+            nc.sync.dma_start(raw[:].bitcast(I32), w4_words.bitcast(I32)[lo:hi].rearrange("a p c -> p a c"))
+            return raw
+
         def load_wgs(b):
             part = sb.tile([P, BANK], F32, name=f"wgs{b}", align_bytes=64)
             nc.sync.dma_start(part[:], wgs[:, columns(b)])
@@ -99,8 +104,7 @@ def tile_list_plot_track_scores_kernel(
         tab_win.append(load_words(1))
         w1_raw = [load_w1(0)]
         wgs_sb = [load_wgs(0)]
-        w4_raw = sb.tile([P, PASSES, 2 * H], U8, name="w4_raw", align_bytes=64)
-        nc.sync.dma_start(w4_raw[:].bitcast(I32), w4_words.bitcast(I32).rearrange("a p c -> p a c"))
+        w4_raw = [load_w4(0, PASSES - 1)]
         w1_raw.append(load_w1(1))
         nc.sync.dma_start(tab2_sc[:].bitcast(I32)[0:16, :], tab2_scales.bitcast(I32)[0])
         idx2 = load_list(offs2, "idx2")
@@ -127,6 +131,7 @@ def tile_list_plot_track_scores_kernel(
         tab_win.append(load_words(2))
         move_rows(moved[1], 0, v_sc, SC_ROW[1])
         w1_raw.append(load_w1(2))
+        w4_raw.append(load_w4(PASSES - 1, PASSES))
         move_rows(moved[2], 0, v_sc, SC_ROW[2])
         idx3 = load_list(offs3, "idx3")
 
@@ -135,7 +140,7 @@ def tile_list_plot_track_scores_kernel(
         tab2_win = sb.tile([P, T], I32, name="tab2_win", align_bytes=64)
         factor = {ORDER[pos]: sb.tile([P, S], F32, name=f"factor{pos}", align_bytes=64) for pos in range(PACK)}
         for i in ORDER:
-            if i in ORDER[2:]:
+            if i == ORDER[-1]:
                 for q in QUADS:
                     nc.sync.dma_start(factor[i][32 * q : 32 * (q + 1), :], wgs[i:P:PACK, :])
             if i == ORDER[-1]:
@@ -153,7 +158,7 @@ def tile_list_plot_track_scores_kernel(
         def round_on_vector(dst, src):
             nc.vector.tensor_scalar_mul(dst, src, -1.0)
 
-        def quantise_w1(a, lo, hi, negate_and_round):
+        def quantise_w1(a, lo, hi, negate_and_round, between=None):
             n = hi - lo
             grouped = sb.tile([P, n * P * PACK], BF16, name=f"w1_bf{a}_{lo}", align_bytes=64)
             codes = sb.tile([P, n * P], U32, name=f"w1_codes{a}_{lo}", align_bytes=64)
@@ -162,16 +167,26 @@ def tile_list_plot_track_scores_kernel(
                 grouped[:].rearrange("p (i m j) -> p m j i", i=n, j=PACK),
                 w1_raw[a][:].rearrange("p j (m i) -> p m j i", i=PACK)[:, :, :, lo:hi],
             )
+            if between:
+                between()
             nc.vector.quantize_mx(out=codes[:].bitcast(FP8X4), scales=scales[:], in_=grouped[:])
             for i in range(lo, hi):
                 w1_codes[a, i] = codes[:, P * (i - lo) : P * (i - lo + 1)]
                 w1_sc[a, i] = scales[:, P * (i - lo) : P * (i - lo + 1)]
 
-        w4_codes = sb.tile([P, PASSES, 2 * H], U8, name="w4_codes", align_bytes=64)
-        nc.scalar.copy(
-            w4_codes[:].bitcast(U16).rearrange("p a (i m) -> p i a m", i=PACK),
-            w4_raw[:].bitcast(U16).rearrange("p a (m i) -> p i a m", i=PACK),
-        )
+        w4_codes = {}
+
+        def deal_w4(copy, raw, first):
+            n = raw.shape[1]
+            dealt = sb.tile([P, n, 2 * H], U8, name=f"w4_codes{first}", align_bytes=64)
+            copy(
+                dealt[:].bitcast(U16).rearrange("p a (i m) -> p i a m", i=PACK),
+                raw[:].bitcast(U16).rearrange("p a (m i) -> p i a m", i=PACK),
+            )
+            for a in range(n):
+                w4_codes[first + a] = dealt[:, a, :]
+
+        deal_w4(nc.scalar.copy, w4_raw[0], 0)
         quantise_w1(0, 0, PACK, round_on_scalar)
         w4_sc = sb.tile([P, PASSES, H], U8, name="w4_sc", align_bytes=64)
         nc.gpsimd.tensor_copy(
@@ -182,9 +197,9 @@ def tile_list_plot_track_scores_kernel(
         nc.vector.tensor_copy(v2_sc[:], tab2_sc[:].indirect(idx2[:]))
         quantise_w1(1, 0, PACK, round_on_scalar)
         pick_words(2, 0, BANK, "v_words2a")
-        pick_words(2, BANK, S, "v_words2b")
-        quantise_w1(2, 2, PACK, round_on_vector)
+        quantise_w1(2, 2, PACK, round_on_vector, lambda: deal_w4(nc.vector.tensor_copy, w4_raw[1], PASSES - 1))
         quantise_w1(2, 0, 2, round_on_scalar)
+        pick_words(2, BANK, S, "w1_bf2_2")
 
         turned = {}
 
@@ -215,7 +230,7 @@ def tile_list_plot_track_scores_kernel(
             acc[i, c] = psum.tile([P, BANK], F32, name=f"acc{i}{c}", tag=f"bank{H_BANKS[pos][c]}")
             for k, (weight, a) in enumerate(passes):
                 if weight == "w4":
-                    lhsT = w4_codes[:, a, 2 * P * i : 2 * P * (i + 1)].bitcast(FP4X4)
+                    lhsT = w4_codes[a][:, 2 * P * i : 2 * P * (i + 1)].bitcast(FP4X4)
                     lhsT_sc = w4_sc[:, a, P * i : P * (i + 1)]
                 else:
                     lhsT = w1_codes[a, i].bitcast(FP8X4)
@@ -257,6 +272,8 @@ def tile_list_plot_track_scores_kernel(
             deal_factor(pos, 1, spread_tags[pos])
             magnitude_half(pos, 1, f"h{pos}")
         replace_half(0, 1)
+        for b in range(2):
+            deal_factor(2, b, spread_tags[b])
         for pos in range(2, PACK):
             for c in range(2):
                 difference(pos, c)
@@ -384,9 +401,9 @@ def tile_list_plot_track_scores_kernel(
             square(n)
             finish(n - 1)
         finish(last - 3)
-        for c in range(2):
-            square(last - 2, columns(c))
-        for c in range(2):
+        square(last - 2, columns(0))
+        multiply(nc.vector, last - 2, columns(1))
+        for c in (1, 0):
             finish(last - 2, columns(c))
         first, second, third = LAST_PIECES
         pick(last, first)

@@ -223,10 +223,11 @@ def tile_list_plot_track_scores_kernel(
         deal_factor(1, 0, "spread_b")
 
         acc, h = {}, {}
-        passes = (("w1", 0), ("w4", 0), ("w1", 1), ("w4", 1), ("w4", 2), ("w1", 2))
+        early = (("w1", 0), ("w4", 0), ("w1", 1), ("w4", 1))
 
         def difference(pos, c):
             i = ORDER[pos]
+            passes = early + ((("w4", 2), ("w1", 2)) if (pos, c) == (0, 0) else (("w1", 2), ("w4", 2)))
             acc[i, c] = psum.tile([P, BANK], F32, name=f"acc{i}{c}", tag=f"bank{H_BANKS[pos][c]}")
             for k, (weight, a) in enumerate(passes):
                 if weight == "w4":

@@ -26,7 +26,6 @@ TILES = S // P
 QUADS = (0, 2, 1, 3)
 ORDER = (2, 0, 1, 3)
 PLOT_ROW = 12
-SC_ROW = (0, 16, 64)
 H_BANKS = ((0, 0), (1, 1), (0, 1), (6, 7))
 FACTOR_BANKS = ((6, 6), (7, 7), (6, 7))
 GPSIMD_SQUARES, VECTOR_EMPTIES = 0, 2
@@ -65,15 +64,18 @@ def tile_list_plot_track_scores_kernel(
         tab_sc = sb.tile([P, T], U8, name="tab_sc", align_bytes=64)
         w4_sc_raw = sb.tile([P, PASSES * H], U8, name="w4_sc_raw", align_bytes=64)
         tab2_sc = sb.tile([P, T], U8, name="tab2_sc", align_bytes=64)
-        moved = {a: sb.tile([P, S], U8, name=f"moved{a}", align_bytes=64) for a in range(PASSES)}
+        moved_first = sb.tile([P, 2, S], U8, name="moved_first", align_bytes=64)
+        moved_last = sb.tile([P, S], U8, name="moved_last", align_bytes=64)
+        moved = (moved_first[:, 0, :], moved_first[:, 1, :], moved_last[:])
         plot_planes = sb.tile([P, S], U8, name="plot_planes", align_bytes=64)
         ident = sb.tile([P, P], F32, name="ident", align_bytes=64)
         nc.gpsimd.memset(w4_sc_raw[:].bitcast(I32), 0)
         load_scale_rows(nc.gpsimd, w4_sc_raw, w4_scales, 0)
         make_identity(nc, ident[:])
-        nc.vector.memset(tab_sc[:].bitcast(I32), 0)
+        for q in (1, 3):
+            nc.vector.memset(tab_sc[:].bitcast(I32)[32 * q : 32 * (q + 1), :], 0)
         nc.vector.memset(tab2_sc[:].bitcast(I32), 0)
-        for dst in (*moved.values(), plot_planes):
+        for dst in (moved_first, moved_last, plot_planes):
             nc.vector.memset(dst[:].bitcast(I32), 0)
 
         def load_words(a):
@@ -91,23 +93,23 @@ def tile_list_plot_track_scores_kernel(
             nc.sync.dma_start(raw[:].bitcast(I32), w4_words.bitcast(I32)[lo:hi].rearrange("a p c -> p a c"))
             return raw
 
-        def load_wgs(b):
-            part = sb.tile([P, BANK], F32, name=f"wgs{b}", align_bytes=64)
-            nc.sync.dma_start(part[:], wgs[:, columns(b)])
+        def load_wgs(name, rows):
+            part = sb.tile([P, 2 * P], F32, name=name, align_bytes=64)
+            nc.sync.dma_start(part[:], rows.rearrange("x (k j) -> x k j", j=2 * P))
             return part
 
-        tab_win = [load_words(0)]
         idx = load_list(offs, "idx")
-        sc_rows = tab_scales.bitcast(I32).rearrange("a q c -> (a q) c")
-        nc.sync.dma_start(tab_sc[:].bitcast(I32)[0:32, :], sc_rows[0:32, :])
-        nc.sync.dma_start(tab_sc[:].bitcast(I32)[SC_ROW[2] : SC_ROW[2] + 16, :], sc_rows[32:48, :])
+        for a in range(2):
+            nc.sync.dma_start(tab_sc[:].bitcast(I32)[64 * a : 64 * a + 32, :],
+                              tab_scales.bitcast(I32)[a : a + 2].rearrange("a x c -> x a c"))
+        tab_win = [load_words(0)]
         tab_win.append(load_words(1))
-        w1_raw = [load_w1(0)]
-        wgs_sb = [load_wgs(0)]
-        w4_raw = [load_w4(0, PASSES - 1)]
-        w1_raw.append(load_w1(1))
         nc.sync.dma_start(tab2_sc[:].bitcast(I32)[0:16, :], tab2_scales.bitcast(I32)[0])
         idx2 = load_list(offs2, "idx2")
+        w1_raw = [load_w1(0)]
+        wgs_even = [load_wgs("wgs_even0", wgs[0:P:2, columns(0)])]
+        w4_raw = [load_w4(0, PASSES - 1)]
+        w1_raw.append(load_w1(1))
 
         v_words = {}
 
@@ -117,22 +119,22 @@ def tile_list_plot_track_scores_kernel(
             for c in range(lo // BANK, hi // BANK):
                 v_words[a, c] = words[:, c * BANK - lo : (c + 1) * BANK - lo]
 
-        pick_words(0, 0, S, "v_words0")
         v_sc = sb.tile([P, S], U8, name="v_sc", align_bytes=64)
         nc.vector.tensor_copy(v_sc[:], tab_sc[:].indirect(idx[:]))
+        pick_words(0, 0, S, "v_words0")
         pick_words(1, 0, S, "v_words1")
 
-        def move_rows(dst, dst_row, src, src_row):
+        def move_rows(dst, dst_row, src, src_row, step=1):
             for q in QUADS:
                 nc.sync.dma_start(dst[32 * q + dst_row : 32 * q + dst_row + 4, :].bitcast(I32),
-                                  src[src_row + 4 * q : src_row + 4 * q + 4, :].bitcast(I32))
+                                  src[src_row + 4 * step * q : src_row + 4 * step * (q + 1) - step + 1 : step, :].bitcast(I32))
 
-        move_rows(moved[0], 0, v_sc, SC_ROW[0])
+        for q in QUADS:
+            nc.sync.dma_start(moved_first[32 * q : 32 * q + 4].bitcast(I32), v_sc[8 * q : 8 * q + 8, :].bitcast(I32))
         tab_win.append(load_words(2))
-        move_rows(moved[1], 0, v_sc, SC_ROW[1])
+        move_rows(moved_last, 0, v_sc, 65, 2)
         w1_raw.append(load_w1(2))
         w4_raw.append(load_w4(PASSES - 1, PASSES))
-        move_rows(moved[2], 0, v_sc, SC_ROW[2])
         idx3 = load_list(offs3, "idx3")
 
         page_rows = page0.rearrange("(p i) t -> p i t", i=PACK)
@@ -147,7 +149,9 @@ def tile_list_plot_track_scores_kernel(
                 nc.sync.dma_start(tab2_win[:], tab2_words[0].rearrange("p t i -> p (t i)").bitcast(I32))
             nc.sync.dma_start(page[i][:], page_rows[:, i, :])
             if i == ORDER[0]:
-                wgs_sb.append(load_wgs(1))
+                wgs_even.append(load_wgs("wgs_even1", wgs[0:P:2, columns(1)]))
+            if i == ORDER[1]:
+                wgs_third = load_wgs("wgs_third", wgs[ORDER[2] : P : PACK, :])
         idx4 = load_list(offs4, "idx4")
 
         w1_codes, w1_sc = {}, {}
@@ -201,26 +205,27 @@ def tile_list_plot_track_scores_kernel(
         quantise_w1(2, 0, 2, round_on_scalar)
         pick_words(2, BANK, S, "w1_bf2_2")
 
-        turned = {}
+        def turn(part, name, bank):
+            turned = psum.tile([P, 2, P], F32, name=name, tag=f"bank{bank}")
+            for u in range(2):
+                nc.tensor.transpose(turned[:, u, :], part[:, P * u : P * (u + 1)], ident[:])
+            return turned
 
-        def turn(b):
-            turned[b] = psum.tile([P, PACK, P], F32, name=f"turned{b}", tag=f"bank{4 + b}")
-            for u in range(PACK):
-                nc.tensor.transpose(turned[b][:, u, :], wgs_sb[b][:, P * u : P * (u + 1)], ident[:])
-
-        def deal_factor(pos, b, spread_tag):
+        def deal_factor(pos, b, turned, spread_tag):
             i = ORDER[pos]
+            first = i if pos < 2 else 2 * b
             spread = sb.tile([P, PACK, 4, 32], F32, name=f"spread{i}{b}", tag=spread_tag, align_bytes=64)
-            rows = turned[b][:].rearrange("p u (q i) -> p u q i", i=PACK)[:, :, :, i]
-            nc.scalar.copy(spread[:], rows.unsqueeze(2).to_broadcast([P, PACK, 4, 32]))
+            rows = turned[:].rearrange("p u (q k) -> p k u q", k=PACK)[:, first : first + 2]
+            nc.scalar.copy(spread[:].rearrange("p (k u) g q -> p k u g q", u=2),
+                           rows.unsqueeze(3).to_broadcast([P, 2, 2, 4, 32]))
             bank = psum.tile([P, PACK, P], F32, name=f"back{i}{b}", tag=f"bank{FACTOR_BANKS[pos][b]}")
             for u in range(PACK):
                 nc.tensor.transpose(bank[:, u, :], spread[:, u].rearrange("p g q -> p (g q)"), ident[:])
             nc.scalar.copy(factor[i][:, columns(b)], bank[:].rearrange("p u j -> p (u j)"))
 
-        turn(0)
-        deal_factor(0, 0, "spread_a")
-        deal_factor(1, 0, "spread_b")
+        turned = turn(wgs_even[0], "turned0", 4)
+        deal_factor(0, 0, turned, "spread_a")
+        deal_factor(1, 0, turned, "spread_b")
 
         acc, h = {}, {}
         early = (("w1", 0), ("w4", 0), ("w1", 1), ("w4", 1))
@@ -265,16 +270,17 @@ def tile_list_plot_track_scores_kernel(
         for pos in range(2):
             difference(pos, 0)
             magnitude_half(pos, 0, f"h_first{pos}")
-        turn(1)
+        turned = turn(wgs_even[1], "turned1", 5)
         spread_tags = ("spread_c", "spread_d")
         for pos in range(2):
             replace_half(pos, 0)
             difference(pos, 1)
-            deal_factor(pos, 1, spread_tags[pos])
+            deal_factor(pos, 1, turned, spread_tags[pos])
             magnitude_half(pos, 1, f"h{pos}")
         replace_half(0, 1)
+        turned = turn(wgs_third, "turned2", 4)
         for b in range(2):
-            deal_factor(2, b, spread_tags[b])
+            deal_factor(2, b, turned, spread_tags[b])
         for pos in range(2, PACK):
             for c in range(2):
                 difference(pos, c)

@@ -88,11 +88,6 @@ def tile_list_plot_track_scores_kernel(
             nc.sync.dma_start(raw[:], w1[512 * a : 512 * (a + 1), :].rearrange("(p j) c -> p j c", j=PACK))
             return raw
 
-        def load_w4(lo, hi):
-            raw = sb.tile([P, hi - lo, 2 * H], U8, name=f"w4_raw{lo}", align_bytes=64)
-            nc.sync.dma_start(raw[:].bitcast(I32), w4_words.bitcast(I32)[lo:hi].rearrange("a p c -> p a c"))
-            return raw
-
         def load_wgs(name, rows):
             part = sb.tile([P, 2 * P], F32, name=name, align_bytes=64)
             nc.sync.dma_start(part[:], rows.rearrange("x (k j) -> x k j", j=2 * P))
@@ -106,10 +101,11 @@ def tile_list_plot_track_scores_kernel(
         tab_win.append(load_words(1))
         nc.sync.dma_start(tab2_sc[:].bitcast(I32)[0:16, :], tab2_scales.bitcast(I32)[0])
         idx2 = load_list(offs2, "idx2")
-        w1_raw = [load_w1(0)]
         wgs_even = [load_wgs("wgs_even0", wgs[0:P:2, columns(0)])]
-        w4_raw = [load_w4(0, PASSES - 1)]
-        w1_raw.append(load_w1(1))
+        w4_raw = sb.tile([P, PASSES, 2 * H], U8, name="w4_raw", align_bytes=64)
+        nc.sync.dma_start(w4_raw[:].bitcast(I32), w4_words.bitcast(I32).rearrange("a p c -> p a c"))
+        w1_raw = [load_w1(0)]
+        tab_win.append(load_words(2))
 
         v_words = {}
 
@@ -131,10 +127,9 @@ def tile_list_plot_track_scores_kernel(
 
         for q in QUADS:
             nc.sync.dma_start(moved_first[32 * q : 32 * q + 4].bitcast(I32), v_sc[8 * q : 8 * q + 8, :].bitcast(I32))
-        tab_win.append(load_words(2))
+        w1_raw.append(load_w1(1))
         move_rows(moved_last, 0, v_sc, 65, 2)
         w1_raw.append(load_w1(2))
-        w4_raw.append(load_w4(PASSES - 1, PASSES))
         idx3 = load_list(offs3, "idx3")
 
         page_rows = page0.rearrange("(p i) t -> p i t", i=PACK)
@@ -162,48 +157,47 @@ def tile_list_plot_track_scores_kernel(
         def round_on_vector(dst, src):
             nc.vector.tensor_scalar_mul(dst, src, -1.0)
 
-        def quantise_w1(a, lo, hi, negate_and_round, between=None):
+        def round_w1(a, lo, hi, negate_and_round, codes_tag=None):
             n = hi - lo
             grouped = sb.tile([P, n * P * PACK], BF16, name=f"w1_bf{a}_{lo}", align_bytes=64)
-            codes = sb.tile([P, n * P], U32, name=f"w1_codes{a}_{lo}", align_bytes=64)
-            scales = sb.tile([P, n * P], U8, name=f"w1_sc{a}_{lo}", align_bytes=64)
             negate_and_round(
                 grouped[:].rearrange("p (i m j) -> p m j i", i=n, j=PACK),
                 w1_raw[a][:].rearrange("p j (m i) -> p m j i", i=PACK)[:, :, :, lo:hi],
             )
-            if between:
-                between()
-            nc.vector.quantize_mx(out=codes[:].bitcast(FP8X4), scales=scales[:], in_=grouped[:])
-            for i in range(lo, hi):
-                w1_codes[a, i] = codes[:, P * (i - lo) : P * (i - lo + 1)]
-                w1_sc[a, i] = scales[:, P * (i - lo) : P * (i - lo + 1)]
 
-        w4_codes = {}
+            def quantise():
+                name = f"w1_codes{a}_{lo}"
+                codes = sb.tile([P, n * P], U32, name=name, tag=codes_tag or name, align_bytes=64)
+                scales = sb.tile([P, n * P], U8, name=f"w1_sc{a}_{lo}", align_bytes=64)
+                nc.vector.quantize_mx(out=codes[:].bitcast(FP8X4), scales=scales[:], in_=grouped[:])
+                for i in range(lo, hi):
+                    w1_codes[a, i] = codes[:, P * (i - lo) : P * (i - lo + 1)]
+                    w1_sc[a, i] = scales[:, P * (i - lo) : P * (i - lo + 1)]
 
-        def deal_w4(copy, raw, first):
-            n = raw.shape[1]
-            dealt = sb.tile([P, n, 2 * H], U8, name=f"w4_codes{first}", align_bytes=64)
-            copy(
-                dealt[:].bitcast(U16).rearrange("p a (i m) -> p i a m", i=PACK),
-                raw[:].bitcast(U16).rearrange("p a (m i) -> p i a m", i=PACK),
-            )
-            for a in range(n):
-                w4_codes[first + a] = dealt[:, a, :]
+            return quantise
 
-        deal_w4(nc.scalar.copy, w4_raw[0], 0)
-        quantise_w1(0, 0, PACK, round_on_scalar)
-        w4_sc = sb.tile([P, PASSES, H], U8, name="w4_sc", align_bytes=64)
-        nc.gpsimd.tensor_copy(
-            w4_sc[:].rearrange("p a (i m) -> p i a m", i=PACK),
-            w4_sc_raw[:].rearrange("p (a m i) -> p i a m", a=PASSES, i=PACK),
+        w4_codes = sb.tile([P, PASSES, 2 * H], U8, name="w4_codes", align_bytes=64)
+        nc.scalar.copy(
+            w4_codes[:].bitcast(U16).rearrange("p a (i m) -> p i a m", i=PACK),
+            w4_raw[:].bitcast(U16).rearrange("p a (m i) -> p i a m", i=PACK),
         )
+        w4_sc = []
+        for odd in range(2):
+            dealt = sb.tile([P, PASSES, 2, P], U8, name=f"w4_sc{odd}", align_bytes=64)
+            nc.gpsimd.tensor_copy(
+                dealt[:].rearrange("p a i m -> p i a m"),
+                w4_sc_raw[:].rearrange("p (a m i) -> p i a m", a=PASSES, i=PACK)[:, odd:PACK:2],
+            )
+            w4_sc.append(dealt)
         v2_sc = sb.tile([P, S], U8, name="v2_sc", align_bytes=64)
         nc.vector.tensor_copy(v2_sc[:], tab2_sc[:].indirect(idx2[:]))
-        quantise_w1(1, 0, PACK, round_on_scalar)
-        pick_words(2, 0, BANK, "v_words2a")
-        quantise_w1(2, 2, PACK, round_on_vector, lambda: deal_w4(nc.vector.tensor_copy, w4_raw[1], PASSES - 1))
-        quantise_w1(2, 0, 2, round_on_scalar)
-        pick_words(2, BANK, S, "w1_bf2_2")
+        round_w1(0, 0, PACK, round_on_scalar)()
+        pick_words(2, 0, S, "w1_bf0_0")
+        round_w1(1, 2, PACK, round_on_scalar)()
+        quantise_second = round_w1(1, 0, 2, round_on_scalar, "w1_bf2_2")
+        round_w1(2, 2, PACK, round_on_vector)()
+        quantise_second()
+        round_w1(2, 0, 2, round_on_scalar)()
 
         def turn(part, name, bank):
             turned = psum.tile([P, 2, P], F32, name=name, tag=f"bank{bank}")
@@ -228,16 +222,15 @@ def tile_list_plot_track_scores_kernel(
         deal_factor(1, 0, turned, "spread_b")
 
         acc, h = {}, {}
-        early = (("w1", 0), ("w4", 0), ("w1", 1), ("w4", 1))
+        passes = (("w4", 0), ("w4", 1), ("w1", 0), ("w4", 2), ("w1", 1), ("w1", 2))
 
         def difference(pos, c):
             i = ORDER[pos]
-            passes = early + ((("w4", 2), ("w1", 2)) if (pos, c) == (0, 0) else (("w1", 2), ("w4", 2)))
             acc[i, c] = psum.tile([P, BANK], F32, name=f"acc{i}{c}", tag=f"bank{H_BANKS[pos][c]}")
             for k, (weight, a) in enumerate(passes):
                 if weight == "w4":
-                    lhsT = w4_codes[a][:, 2 * P * i : 2 * P * (i + 1)].bitcast(FP4X4)
-                    lhsT_sc = w4_sc[:, a, P * i : P * (i + 1)]
+                    lhsT = w4_codes[:, a, 2 * P * i : 2 * P * (i + 1)].bitcast(FP4X4)
+                    lhsT_sc = w4_sc[i % 2][:, a, i // 2, :]
                 else:
                     lhsT = w1_codes[a, i].bitcast(FP8X4)
                     lhsT_sc = w1_sc[a, i]

@@ -88,6 +88,11 @@ def tile_list_plot_track_scores_kernel(
             nc.sync.dma_start(raw[:], w1[512 * a : 512 * (a + 1), :].rearrange("(p j) c -> p j c", j=PACK))
             return raw
 
+        def load_w4(lo, hi):
+            raw = sb.tile([P, hi - lo, 2 * H], U8, name=f"w4_raw{lo}", align_bytes=64)
+            nc.sync.dma_start(raw[:].bitcast(I32), w4_words.bitcast(I32)[lo:hi].rearrange("a p c -> p a c"))
+            return raw
+
         def load_wgs(name, rows):
             part = sb.tile([P, 2 * P], F32, name=name, align_bytes=64)
             nc.sync.dma_start(part[:], rows.rearrange("x (k j) -> x k j", j=2 * P))
@@ -102,8 +107,7 @@ def tile_list_plot_track_scores_kernel(
         nc.sync.dma_start(tab2_sc[:].bitcast(I32)[0:16, :], tab2_scales.bitcast(I32)[0])
         idx2 = load_list(offs2, "idx2")
         wgs_even = [load_wgs("wgs_even0", wgs[0:P:2, columns(0)])]
-        w4_raw = sb.tile([P, PASSES, 2 * H], U8, name="w4_raw", align_bytes=64)
-        nc.sync.dma_start(w4_raw[:].bitcast(I32), w4_words.bitcast(I32).rearrange("a p c -> p a c"))
+        w4_raw = [load_w4(0, PASSES - 1)]
         w1_raw = [load_w1(0)]
         tab_win.append(load_words(2))
 
@@ -130,6 +134,7 @@ def tile_list_plot_track_scores_kernel(
         w1_raw.append(load_w1(1))
         move_rows(moved_last, 0, v_sc, 65, 2)
         w1_raw.append(load_w1(2))
+        w4_raw.append(load_w4(PASSES - 1, PASSES))
         idx3 = load_list(offs3, "idx3")
 
         page_rows = page0.rearrange("(p i) t -> p i t", i=PACK)
@@ -176,11 +181,19 @@ def tile_list_plot_track_scores_kernel(
 
             return quantise
 
-        w4_codes = sb.tile([P, PASSES, 2 * H], U8, name="w4_codes", align_bytes=64)
-        nc.scalar.copy(
-            w4_codes[:].bitcast(U16).rearrange("p a (i m) -> p i a m", i=PACK),
-            w4_raw[:].bitcast(U16).rearrange("p a (m i) -> p i a m", i=PACK),
-        )
+        w4_codes = {}
+
+        def deal_w4(copy, raw, first):
+            n = raw.shape[1]
+            dealt = sb.tile([P, n, 2 * H], U8, name=f"w4_codes{first}", align_bytes=64)
+            copy(
+                dealt[:].bitcast(U16).rearrange("p a (i m) -> p i a m", i=PACK),
+                raw[:].bitcast(U16).rearrange("p a (m i) -> p i a m", i=PACK),
+            )
+            for a in range(n):
+                w4_codes[first + a] = dealt[:, a, :]
+
+        deal_w4(nc.scalar.copy, w4_raw[0], 0)
         w4_sc = []
         for odd in range(2):
             dealt = sb.tile([P, PASSES, 2, P], U8, name=f"w4_sc{odd}", align_bytes=64)
@@ -195,7 +208,9 @@ def tile_list_plot_track_scores_kernel(
         pick_words(2, 0, S, "w1_bf0_0")
         round_w1(1, 2, PACK, round_on_scalar)()
         quantise_second = round_w1(1, 0, 2, round_on_scalar, "w1_bf2_2")
-        round_w1(2, 2, PACK, round_on_vector)()
+        quantise_last = round_w1(2, 2, PACK, round_on_vector)
+        deal_w4(nc.vector.tensor_copy, w4_raw[1], PASSES - 1)
+        quantise_last()
         quantise_second()
         round_w1(2, 0, 2, round_on_scalar)()
 
@@ -222,21 +237,22 @@ def tile_list_plot_track_scores_kernel(
         deal_factor(1, 0, turned, "spread_b")
 
         acc, h = {}, {}
-        passes = (("w4", 0), ("w4", 1), ("w1", 0), ("w4", 2), ("w1", 1), ("w1", 2))
+        passes = (("w4", 0), ("w4", 1), ("w1", 0), ("w1", 1), ("w4", 2), ("w1", 2))
 
-        def difference(pos, c):
+        def difference(pos, c, cols=slice(0, BANK), bank=None):
             i = ORDER[pos]
-            acc[i, c] = psum.tile([P, BANK], F32, name=f"acc{i}{c}", tag=f"bank{H_BANKS[pos][c]}")
+            bank = H_BANKS[pos][c] if bank is None else bank
+            acc[i, c] = psum.tile([P, cols.stop - cols.start], F32, name=f"acc{i}{c}_{cols.start}", tag=f"bank{bank}")
             for k, (weight, a) in enumerate(passes):
                 if weight == "w4":
-                    lhsT = w4_codes[:, a, 2 * P * i : 2 * P * (i + 1)].bitcast(FP4X4)
+                    lhsT = w4_codes[a][:, 2 * P * i : 2 * P * (i + 1)].bitcast(FP4X4)
                     lhsT_sc = w4_sc[i % 2][:, a, i // 2, :]
                 else:
                     lhsT = w1_codes[a, i].bitcast(FP8X4)
                     lhsT_sc = w1_sc[a, i]
                 nc.tensor.matmul_mx(
                     out=acc[i, c][:], lhsT=lhsT, lhsT_scale=lhsT_sc,
-                    rhs=v_words[a, c].bitcast(FP8X4), rhs_scale=moved[a][:, columns(c)],
+                    rhs=v_words[a, c][:, cols].bitcast(FP8X4), rhs_scale=moved[a][:, columns(c)][:, cols],
                     start=(k == 0), stop=(k == len(passes) - 1),
                 )
 
@@ -260,13 +276,22 @@ def tile_list_plot_track_scores_kernel(
             i = ORDER[pos]
             nc.vector.tensor_tensor(page[i][:].indirect(idx3[:]), h[i][:], factor[i][:], ALU.mult)
 
-        for pos in range(2):
-            difference(pos, 0)
-            magnitude_half(pos, 0, f"h_first{pos}")
+        quarters = (slice(0, BANK // 2), slice(BANK // 2, BANK))
+        for k, cols in enumerate(quarters):
+            difference(0, 0, cols, 2 * k)
+            h[cols.start] = sb.tile([P, BANK // 2], F32, name=f"h_quarter{k}", align_bytes=64)
+            nc.scalar.activation(h[cols.start][:], acc[ORDER[0], 0][:], ACT.Abs)
+        difference(1, 0)
+        magnitude_half(1, 0, "h_first1")
         turned = turn(wgs_even[1], "turned1", 5)
         spread_tags = ("spread_c", "spread_d")
         for pos in range(2):
-            replace_half(pos, 0)
+            if pos == 0:
+                for cols in quarters:
+                    nc.vector.tensor_tensor(page[ORDER[0]][:].indirect(entries(idx3, cols)), h[cols.start][:],
+                                            factor[ORDER[0]][:, cols], ALU.mult)
+            else:
+                replace_half(pos, 0)
             difference(pos, 1)
             deal_factor(pos, 1, turned, spread_tags[pos])
             magnitude_half(pos, 1, f"h{pos}")

from contextlib import ExitStack

import concourse.mybir as mybir
from concourse.masks import make_identity

K, H, T, S = 1536, 512, 2048, 1024
FLOPS = 2 * 2 * K * H * S + 2 * H * S * T

F32 = mybir.dt.float32
BF16 = mybir.dt.bfloat16
I32 = mybir.dt.int32
U32 = mybir.dt.uint32
U16 = mybir.dt.uint16
U8 = mybir.dt.uint8
FP8X4 = mybir.dt.float8_e4m3fn_x4
FP4X4 = mybir.dt.float4_e2m1fn_x4
ACT = mybir.ActivationFunctionType
ALU = mybir.AluOpType

P = 128
PACK = 4
PASSES = K // (P * PACK)
BANK = 512
CHUNKS = T // BANK
TILES = S // P
QUADS = (0, 2, 1, 3)
ORDER = (2, 0, 1, 3)
PLOT_ROW = 12
H_BANKS = ((0, 0), (1, 1), (0, 1), (6, 7))
FACTOR_BANKS = ((6, 6), (7, 7), (6, 7))
GPSIMD_SQUARES, VECTOR_EMPTIES = 0, 2
LAST_PIECES = (slice(0, 640), slice(640, 896), slice(896, 1024))


def tile_list_plot_track_scores_kernel(
    tc, tab_words, tab_scales, offs, tab2_words, tab2_scales, offs2, w1, w4_words, w4_scales,
    page0, wgs, offs3, offs4, gate, out,
):
    nc = tc.nc
    with ExitStack() as ctx:
        lists = ctx.enter_context(tc.tile_pool(name="lists", bufs=1))
        sb = ctx.enter_context(tc.tile_pool(name="sb", bufs=1))
        psum = ctx.enter_context(tc.psum_pool(name="psum", bufs=1))

        def columns(c):
            return slice(c * BANK, (c + 1) * BANK)

        def entries(lst, cols):
            return lst[:, cols.start // 16 : cols.stop // 16]

        def load_list(src, name):
            t = lists.tile([P, S // 16], U16, name=name)
            nc.sync.dma_start(t[:], src)
            return t

        def load_scale_rows(queue, dst, src, first_row):
            rows = dst[:].bitcast(I32).rearrange("p (a c) -> p a c", a=src.shape[0])
            for r in range(4):
                queue.dma_start(
                    rows[first_row + r : P : 32, :, :],
                    src.bitcast(I32)[:, r : 16 : 4, :].rearrange("a q c -> q a c"),
                )

        tab_sc = sb.tile([P, T], U8, name="tab_sc", align_bytes=64)
        w4_sc_raw = sb.tile([P, PASSES * H], U8, name="w4_sc_raw", align_bytes=64)
        tab2_sc = sb.tile([P, T], U8, name="tab2_sc", align_bytes=64)
        moved_first = sb.tile([P, 2, S], U8, name="moved_first", align_bytes=64)
        moved_last = sb.tile([P, S], U8, name="moved_last", align_bytes=64)
        moved = (moved_first[:, 0, :], moved_first[:, 1, :], moved_last[:])
        plot_planes = sb.tile([P, S], U8, name="plot_planes", align_bytes=64)
        ident = sb.tile([P, P], F32, name="ident", align_bytes=64)
        nc.gpsimd.memset(w4_sc_raw[:].bitcast(I32), 0)
        load_scale_rows(nc.gpsimd, w4_sc_raw, w4_scales, 0)
        make_identity(nc, ident[:])
        for q in (1, 3):
            nc.vector.memset(tab_sc[:].bitcast(I32)[32 * q : 32 * (q + 1), :], 0)
        nc.vector.memset(tab2_sc[:].bitcast(I32), 0)
        for dst in (moved_first, moved_last, plot_planes):
            nc.vector.memset(dst[:].bitcast(I32), 0)

        def load_words(a):
            win = sb.tile([P, T], I32, name=f"tab_win{a}", tag=f"win{a}", align_bytes=64)
            nc.sync.dma_start(win[:], tab_words[a].rearrange("p t i -> p (t i)").bitcast(I32))
            return win

        def load_w1(a):
            raw = sb.tile([P, PACK, H], F32, name=f"w1_raw{a}", tag=f"raw{a}", align_bytes=64)
            nc.sync.dma_start(raw[:], w1[512 * a : 512 * (a + 1), :].rearrange("(p j) c -> p j c", j=PACK))
            return raw

        def load_w4(lo, hi):
            raw = sb.tile([P, hi - lo, 2 * H], U8, name=f"w4_raw{lo}", align_bytes=64)
            nc.sync.dma_start(raw[:].bitcast(I32), w4_words.bitcast(I32)[lo:hi].rearrange("a p c -> p a c"))
            return raw

        def load_wgs(name, rows):
            part = sb.tile([P, 2 * P], F32, name=name, align_bytes=64)
            nc.sync.dma_start(part[:], rows.rearrange("x (k j) -> x k j", j=2 * P))
            return part

        idx = load_list(offs, "idx")
        for a in range(2):
            nc.sync.dma_start(tab_sc[:].bitcast(I32)[64 * a : 64 * a + 32, :],
                              tab_scales.bitcast(I32)[a : a + 2].rearrange("a x c -> x a c"))
        tab_win = [load_words(0)]
        tab_win.append(load_words(1))
        nc.sync.dma_start(tab2_sc[:].bitcast(I32)[0:16, :], tab2_scales.bitcast(I32)[0])
        idx2 = load_list(offs2, "idx2")
        wgs_even = [load_wgs("wgs_even0", wgs[0:P:2, columns(0)])]
        w4_raw = [load_w4(0, PASSES - 1)]
        w1_raw = [load_w1(0)]
        tab_win.append(load_words(2))

        v_words = {}

        def pick_words(a, lo, hi, tag):
            words = sb.tile([P, hi - lo], U32, name=f"v_words{a}_{lo}", tag=tag, align_bytes=64)
            nc.vector.tensor_copy(words[:], tab_win[a][:].bitcast(U32).indirect(entries(idx, slice(lo, hi))))
            for c in range(lo // BANK, hi // BANK):
                v_words[a, c] = words[:, c * BANK - lo : (c + 1) * BANK - lo]

        v_sc = sb.tile([P, S], U8, name="v_sc", align_bytes=64)
        nc.vector.tensor_copy(v_sc[:], tab_sc[:].indirect(idx[:]))
        pick_words(0, 0, S, "v_words0")
        pick_words(1, 0, S, "v_words1")

        def move_rows(dst, dst_row, src, src_row, step=1):
            for q in QUADS:
                nc.sync.dma_start(dst[32 * q + dst_row : 32 * q + dst_row + 4, :].bitcast(I32),
                                  src[src_row + 4 * step * q : src_row + 4 * step * (q + 1) - step + 1 : step, :].bitcast(I32))

        for q in QUADS:
            nc.sync.dma_start(moved_first[32 * q : 32 * q + 4].bitcast(I32), v_sc[8 * q : 8 * q + 8, :].bitcast(I32))
        w1_raw.append(load_w1(1))
        move_rows(moved_last, 0, v_sc, 65, 2)
        w1_raw.append(load_w1(2))
        w4_raw.append(load_w4(PASSES - 1, PASSES))
        idx3 = load_list(offs3, "idx3")

        page_rows = page0.rearrange("(p i) t -> p i t", i=PACK)
        page = [sb.tile([P, T], F32, name=f"page{i}", align_bytes=64) for i in range(PACK)]
        tab2_win = sb.tile([P, T], I32, name="tab2_win", align_bytes=64)
        factor = {ORDER[pos]: sb.tile([P, S], F32, name=f"factor{pos}", align_bytes=64) for pos in range(PACK)}
        for i in ORDER:
            if i == ORDER[-1]:
                for q in QUADS:
                    nc.sync.dma_start(factor[i][32 * q : 32 * (q + 1), :], wgs[i:P:PACK, :])
            if i == ORDER[-1]:
                nc.sync.dma_start(tab2_win[:], tab2_words[0].rearrange("p t i -> p (t i)").bitcast(I32))
            nc.sync.dma_start(page[i][:], page_rows[:, i, :])
            if i == ORDER[0]:
                wgs_even.append(load_wgs("wgs_even1", wgs[0:P:2, columns(1)]))
            if i == ORDER[1]:
                wgs_third = load_wgs("wgs_third", wgs[ORDER[2] : P : PACK, :])
        idx4 = load_list(offs4, "idx4")

        w1_codes, w1_sc = {}, {}

        def round_on_scalar(dst, src):
            nc.scalar.activation(dst, src, ACT.Copy, scale=-1.0)

        def round_on_vector(dst, src):
            nc.vector.tensor_scalar_mul(dst, src, -1.0)

        def round_w1(a, lo, hi, negate_and_round, codes_tag=None):
            n = hi - lo
            grouped = sb.tile([P, n * P * PACK], BF16, name=f"w1_bf{a}_{lo}", align_bytes=64)
            negate_and_round(
                grouped[:].rearrange("p (i m j) -> p m j i", i=n, j=PACK),
                w1_raw[a][:].rearrange("p j (m i) -> p m j i", i=PACK)[:, :, :, lo:hi],
            )

            def quantise():
                name = f"w1_codes{a}_{lo}"
                codes = sb.tile([P, n * P], U32, name=name, tag=codes_tag or name, align_bytes=64)
                scales = sb.tile([P, n * P], U8, name=f"w1_sc{a}_{lo}", align_bytes=64)
                nc.vector.quantize_mx(out=codes[:].bitcast(FP8X4), scales=scales[:], in_=grouped[:])
                for i in range(lo, hi):
                    w1_codes[a, i] = codes[:, P * (i - lo) : P * (i - lo + 1)]
                    w1_sc[a, i] = scales[:, P * (i - lo) : P * (i - lo + 1)]

            return quantise

        w4_codes = {}

        def deal_w4(copy, raw, first):
            n = raw.shape[1]
            dealt = sb.tile([P, n, 2 * H], U8, name=f"w4_codes{first}", align_bytes=64)
            copy(
                dealt[:].bitcast(U16).rearrange("p a (i m) -> p i a m", i=PACK),
                raw[:].bitcast(U16).rearrange("p a (m i) -> p i a m", i=PACK),
            )
            for a in range(n):
                w4_codes[first + a] = dealt[:, a, :]

        deal_w4(nc.scalar.copy, w4_raw[0], 0)
        w4_sc = []
        for odd in range(2):
            dealt = sb.tile([P, PASSES, 2, P], U8, name=f"w4_sc{odd}", align_bytes=64)
            nc.gpsimd.tensor_copy(
                dealt[:].rearrange("p a i m -> p i a m"),
                w4_sc_raw[:].rearrange("p (a m i) -> p i a m", a=PASSES, i=PACK)[:, odd:PACK:2],
            )
            w4_sc.append(dealt)
        v2_sc = sb.tile([P, S], U8, name="v2_sc", align_bytes=64)
        nc.vector.tensor_copy(v2_sc[:], tab2_sc[:].indirect(idx2[:]))
        round_w1(0, 0, PACK, round_on_scalar)()
        pick_words(2, 0, S, "w1_bf0_0")
        round_w1(1, 2, PACK, round_on_scalar)()
        quantise_second = round_w1(1, 0, 2, round_on_scalar, "w1_bf2_2")
        quantise_last = round_w1(2, 2, PACK, round_on_vector)
        deal_w4(nc.vector.tensor_copy, w4_raw[1], PASSES - 1)
        quantise_last()
        quantise_second()
        round_w1(2, 0, 2, round_on_scalar)()

        def turn(part, name, bank):
            turned = psum.tile([P, 2, P], F32, name=name, tag=f"bank{bank}")
            for u in range(2):
                nc.tensor.transpose(turned[:, u, :], part[:, P * u : P * (u + 1)], ident[:])
            return turned

        def deal_factor(pos, b, turned, spread_tag):
            i = ORDER[pos]
            first = i if pos < 2 else 2 * b
            spread = sb.tile([P, PACK, 4, 32], F32, name=f"spread{i}{b}", tag=spread_tag, align_bytes=64)
            rows = turned[:].rearrange("p u (q k) -> p k u q", k=PACK)[:, first : first + 2]
            nc.scalar.copy(spread[:].rearrange("p (k u) g q -> p k u g q", u=2),
                           rows.unsqueeze(3).to_broadcast([P, 2, 2, 4, 32]))
            bank = psum.tile([P, PACK, P], F32, name=f"back{i}{b}", tag=f"bank{FACTOR_BANKS[pos][b]}")
            for u in range(PACK):
                nc.tensor.transpose(bank[:, u, :], spread[:, u].rearrange("p g q -> p (g q)"), ident[:])
            nc.scalar.copy(factor[i][:, columns(b)], bank[:].rearrange("p u j -> p (u j)"))

        turned = turn(wgs_even[0], "turned0", 4)
        deal_factor(0, 0, turned, "spread_a")
        deal_factor(1, 0, turned, "spread_b")

        acc, h = {}, {}
        passes = (("w4", 0), ("w4", 1), ("w1", 0), ("w1", 1), ("w4", 2), ("w1", 2))

        def difference(pos, c, cols=slice(0, BANK), bank=None):
            i = ORDER[pos]
            bank = H_BANKS[pos][c] if bank is None else bank
            acc[i, c] = psum.tile([P, cols.stop - cols.start], F32, name=f"acc{i}{c}_{cols.start}", tag=f"bank{bank}")
            for k, (weight, a) in enumerate(passes):
                if weight == "w4":
                    lhsT = w4_codes[a][:, 2 * P * i : 2 * P * (i + 1)].bitcast(FP4X4)
                    lhsT_sc = w4_sc[i % 2][:, a, i // 2, :]
                else:
                    lhsT = w1_codes[a, i].bitcast(FP8X4)
                    lhsT_sc = w1_sc[a, i]
                nc.tensor.matmul_mx(
                    out=acc[i, c][:], lhsT=lhsT, lhsT_scale=lhsT_sc,
                    rhs=v_words[a, c][:, cols].bitcast(FP8X4), rhs_scale=moved[a][:, columns(c)][:, cols],
                    start=(k == 0), stop=(k == len(passes) - 1),
                )

        def magnitude_half(pos, c, tag):
            i = ORDER[pos]
            h[i, c] = sb.tile([P, BANK], F32, name=f"h{i}_{c}", tag=tag, align_bytes=64)
            nc.scalar.activation(h[i, c][:], acc[i, c][:], ACT.Abs)

        def magnitude(pos, tag):
            i = ORDER[pos]
            h[i] = sb.tile([P, S], F32, name=f"h{i}_all", tag=tag, align_bytes=64)
            for c in range(2):
                nc.scalar.activation(h[i][:, columns(c)], acc[i, c][:], ACT.Abs)

        def replace_half(pos, c):
            i = ORDER[pos]
            nc.vector.tensor_tensor(page[i][:].indirect(entries(idx3, columns(c))), h[i, c][:],
                                    factor[i][:, columns(c)], ALU.mult)

        def replace(pos):
            i = ORDER[pos]
            nc.vector.tensor_tensor(page[i][:].indirect(idx3[:]), h[i][:], factor[i][:], ALU.mult)

        quarters = (slice(0, BANK // 2), slice(BANK // 2, BANK))
        for k, cols in enumerate(quarters):
            difference(0, 0, cols, 2 * k)
            h[cols.start] = sb.tile([P, BANK // 2], F32, name=f"h_quarter{k}", align_bytes=64)
            nc.scalar.activation(h[cols.start][:], acc[ORDER[0], 0][:], ACT.Abs)
        difference(1, 0)
        magnitude_half(1, 0, "h_first1")
        turned = turn(wgs_even[1], "turned1", 5)
        spread_tags = ("spread_c", "spread_d")
        for pos in range(2):
            if pos == 0:
                for cols in quarters:
                    nc.vector.tensor_tensor(page[ORDER[0]][:].indirect(entries(idx3, cols)), h[cols.start][:],
                                            factor[ORDER[0]][:, cols], ALU.mult)
            else:
                replace_half(pos, 0)
            difference(pos, 1)
            deal_factor(pos, 1, turned, spread_tags[pos])
            magnitude_half(pos, 1, f"h{pos}")
        replace_half(0, 1)
        turned = turn(wgs_third, "turned2", 4)
        for b in range(2):
            deal_factor(2, b, turned, spread_tags[b])
        for pos in range(2, PACK):
            for c in range(2):
                difference(pos, c)
            if pos < PACK - 1:
                magnitude(pos, f"h{pos}")

        woven = {0: sb.tile([P, BANK, PACK], BF16, name="woven0", tag="w1_codes2_0", align_bytes=64)}
        pairs = {
            c: sb.tile([P, 2, BANK, 2], BF16, name=f"pairs{c}", tag=tag, align_bytes=64)
            for c, tag in ((1, "w1_sc2_0"), (2, "v_words1"), (3, "v_words0"))
        }

        def round_first_chunk(copy, pos):
            i = ORDER[pos]
            copy(woven[0][:, :, i], page[i][:, columns(0)])

        def round_into_pairs(pos):
            i = ORDER[pos]
            for c in pairs:
                nc.scalar.copy(pairs[c][:, i // 2, :, i % 2], page[i][:, columns(c)])

        for pos in range(PACK):
            if pos == 1:
                replace_half(1, 1)
            elif pos > 1:
                replace(pos)
            round_first_chunk(nc.scalar.copy if pos < PACK - 1 else nc.vector.tensor_copy, pos)
            round_into_pairs(pos)
            if pos == 0:
                magnitude(PACK - 1, "h3")

        move_rows(plot_planes, PLOT_ROW, v2_sc, 0)
        plots = {}

        def pick_plots(lo, hi, tag):
            words = sb.tile([P, P * (hi - lo)], U32, name=f"v2_words{lo}", tag=tag, align_bytes=64)
            nc.vector.tensor_copy(words[:], tab2_win[:].bitcast(U32).indirect(entries(idx2, slice(P * lo, P * hi))))
            for n in range(lo, hi):
                plots[n] = (words[:, P * (n - lo) : P * (n - lo + 1)], plot_planes[PLOT_ROW:P, P * n : P * (n + 1)])

        pick_plots(0, 2, "factor3")

        page_codes, page_sc = [], []
        woven_tags = {1: "h1", 2: "factor0", 3: "factor1"}

        def interleave(c):
            woven[c] = sb.tile([P, BANK, PACK], BF16, name=f"woven{c}", tag=woven_tags[c], align_bytes=64)
            nc.vector.tensor_copy(
                woven[c][:].rearrange("p t i -> p (t i)").bitcast(I32).rearrange("p (t u) -> p t u", u=2),
                pairs[c][:].rearrange("p u t e -> p (u t e)").bitcast(I32).rearrange("p (u t) -> p t u", u=2),
            )

        def quantise_page(c):
            codes = sb.tile([P, BANK], U32, name=f"page_codes{c}", align_bytes=64)
            scales = sb.tile([P, BANK], U8, name=f"page_sc{c}", align_bytes=64)
            nc.vector.quantize_mx(out=codes[:].bitcast(FP8X4), scales=scales[:],
                                  in_=woven[c][:].rearrange("p t i -> p (t i)"))
            page_codes.append(codes)
            page_sc.append(scales)

        interleave(1)
        quantise_page(0)
        quantise_page(1)
        interleave(2)
        interleave(3)
        quantise_page(2)
        quantise_page(3)
        pick_plots(2, TILES, woven_tags[3])

        gates = []
        for n in range(2):
            single = sb.tile([P, S], F32, name=f"gate{n}", align_bytes=64)
            nc.sync.dma_start(single[:], gate[P * n : P * (n + 1), :])
            gates.append(single[:])
        for g in range(PASSES):
            both = sb.tile([P, 2, S], F32, name=f"gates{g}", tag=f"raw{g}", align_bytes=64)
            nc.sync.dma_start(both[:], gate[2 * P * (g + 1) : 2 * P * (g + 2), :].rearrange("(u p) m -> p u m", u=2))
            gates.extend([both[:, 0, :], both[:, 1, :]])

        e, d = {}, {}
        whole = slice(0, S)
        last = TILES - 1
        e_tags = ("win0", "win1", "win0", "win2", "page0", "page1", "page2", "page3")
        bank_sets = (0, 1, 0, 1, 1, 1, 1, 1)
        for n, tag in enumerate(("h2", "h3", "factor2", "v_words0", "v_words1", "h0", "h1", "factor0")):
            d[n] = sb.tile([P, S], F32, name=f"d{n}", tag=tag, align_bytes=64)[:]

        def product(n):
            e[n] = sb.tile([P, T], F32, name=f"e{n}", tag=e_tags[n], align_bytes=64)
            for c in range(CHUNKS):
                bank = psum.tile([P, BANK], F32, name=f"e{n}{c}", tag=f"bank{CHUNKS * bank_sets[n] + c}")
                nc.tensor.matmul_mx(
                    out=bank[:], lhsT=plots[n][0].bitcast(FP8X4), lhsT_scale=plots[n][1],
                    rhs=page_codes[c][:].bitcast(FP8X4), rhs_scale=page_sc[c][:], start=True, stop=True,
                )
                if n == VECTOR_EMPTIES:
                    nc.vector.tensor_copy(e[n][:, columns(c)], bank[:])
                else:
                    nc.scalar.copy(e[n][:, columns(c)], bank[:])

        def pick(n, cols=whole):
            nc.vector.tensor_tensor(d[n][:, cols], e[n][:].indirect(entries(idx4, cols)), gates[n][:, cols], ALU.subtract)

        def multiply(engine, n, cols=whole):
            engine.tensor_tensor(d[n][:, cols], d[n][:, cols], d[n][:, cols], ALU.mult)

        def square(n, cols=whole):
            nc.scalar.activation(d[n][:, cols], d[n][:, cols], ACT.Square)

        def finish(n, cols=whole):
            nc.scalar.activation(d[n][:, cols], d[n][:, cols], ACT.Exp, scale=-0.25)
            nc.sync.dma_start(out[P * n : P * (n + 1), cols], d[n][:, cols])

        for n in range(TILES):
            product(n)
            if n == 1:
                pick(GPSIMD_SQUARES)
                multiply(nc.gpsimd, GPSIMD_SQUARES)
        for n in range(1, last):
            pick(n)
            if n == 2:
                multiply(nc.vector, 1)
        finish(0)
        for n in range(2, last - 2):
            square(n)
            finish(n - 1)
        finish(last - 3)
        square(last - 2, columns(0))
        multiply(nc.vector, last - 2, columns(1))
        for c in (1, 0):
            finish(last - 2, columns(c))
        first, second, third = LAST_PIECES
        pick(last, first)
        multiply(nc.vector, last - 1)
        multiply(nc.vector, last, first)
        pick(last, second)
        pick(last, third)
        multiply(nc.vector, last, second)
        multiply(nc.vector, last, third)
        for c in range(2):
            finish(last - 1, columns(c))
        for cols in LAST_PIECES:
            finish(last, cols)
